import numpy as np
import ml_dtypes


def mxq(x, axis, fmt="e4m3"):
    dtype, down = {"e4m3": (ml_dtypes.float8_e4m3fn, 7), "e5m2": (ml_dtypes.float8_e5m2, 14)}[fmt]
    v = np.moveaxis(np.asarray(x, np.float32).astype(ml_dtypes.bfloat16).astype(np.float64), axis, -1)
    blocks = v.reshape(v.shape[:-1] + (-1, 32))
    amax = np.abs(blocks).max(-1, keepdims=True)
    byte = np.maximum(np.where(amax > 0, np.frexp(amax)[1] - 1 + 127, 0) - down, 1)
    scale = np.exp2(byte - 127.0)
    codes = (blocks / scale).astype(np.float32).astype(dtype).astype(np.float64)
    return np.moveaxis((codes * scale).reshape(v.shape), -1, axis)


WIDE = False


def mx_kscale(k):
    if not WIDE:
        return np.ones(k)
    levels = np.array([10, -10, 5, -5, 0])
    if k % 512:
        return np.exp2(np.random.permutation(np.resize(levels, k // 32))).repeat(32)
    a = np.empty((k // 512, 16))
    for p in range(k // 512):
        a[p, :8] = np.random.permutation(np.resize(levels, 8))
        for g in range(8):
            far = levels[np.abs(levels - a[p, g]) >= 10]
            a[p, g + 8] = far[np.random.randint(len(far))]
    return np.exp2(a.ravel()).repeat(32)


def f64(x):
    return np.asarray(x).astype(np.float64)


def striped(idx):
    return np.tile(idx.reshape(-1, 16).T, (8, 1)).astype(np.uint16)


def unstriped(offs):
    return offs[:16].T.reshape(-1).astype(np.int64)


E2M1 = np.array([0.0, 0.5, 1.0, 1.5, 2.0, 3.0, 4.0, 6.0, -0.0, -0.5, -1.0, -1.5, -2.0, -3.0, -4.0, -6.0])


def pack_weight(w, fmt):
    k, n = w.shape
    w = f64(np.asarray(w, np.float32).astype(ml_dtypes.bfloat16)).reshape(k // 32, 32, n)
    amax = np.abs(w).max(1)
    if fmt == "e4m3":
        byte = np.frexp(amax)[1] - 1 + 127 - 7
    else:
        mant, ex = np.frexp(amax / 6.0)
        byte = np.where(mant > 0.5, ex, ex - 1) + 127
    byte = np.clip(np.where(amax > 0, byte, 1), 1, 254)
    scaled = (w * np.exp2(127.0 - byte)[:, None, :]).reshape(k, n).astype(np.float32)
    by_word = np.ascontiguousarray(scaled.reshape(k // 512, 128, 4, n).transpose(0, 1, 3, 2))
    if fmt == "e4m3":
        words = by_word.astype(ml_dtypes.float8_e4m3fn).view(np.uint8)
    else:
        c = by_word.astype(ml_dtypes.float4_e2m1fn).view(np.uint8) & 0xF
        words = (c[..., 0::2] | (c[..., 1::2] << 4)).reshape(k // 512, 128, 2 * n)
    return np.ascontiguousarray(words), np.ascontiguousarray(byte.astype(np.uint8).reshape(k // 512, 16, n))


def unpack_weight(words, scales, fmt):
    g, _, n = scales.shape
    words = np.ascontiguousarray(words).reshape(g, 128, n, -1)
    if fmt == "e4m3":
        vals = words.view(ml_dtypes.float8_e4m3fn).astype(np.float64)
    else:
        nib = np.empty((g, 128, n, 4), np.uint8)
        nib[..., 0::2] = words & 0xF
        nib[..., 1::2] = words >> 4
        vals = E2M1[nib]
    vals = vals * np.repeat(np.exp2(scales.astype(np.float64) - 127.0), 8, axis=1)[..., None]
    return vals.transpose(0, 1, 3, 2).reshape(g * 512, n)


def relu(v):
    return np.maximum(v, 0.0)


K, T, E, C, H, N = 1536, 768, 4, 256, 512, 128
PAD = 32


def by_expert(wq, xq):
    return np.concatenate([wq[e].T @ xq[:, e * C:(e + 1) * C] for e in range(E)], axis=1)


def setup_inputs():
    n = np.random.standard_normal
    s = mx_kscale(K)[:, None]
    u = mx_kscale(H)
    first = np.random.permutation(np.repeat(np.arange(E), T // E))
    second = (first + 1 + np.random.permutation(np.repeat(np.arange(E - 1), -(-T // (E - 1)))[:T])) % E
    while np.bincount(second, minlength=E).max() != T // E:
        load = np.bincount(second, minlength=E); hi, lo = int(load.argmax()), int(load.argmin())
        t = np.flatnonzero((second == hi) & (first != lo))[0]; second[t] = lo
    slot_token = np.empty(E * C, np.int64); pos = np.empty((2, T), np.int64); fill = np.zeros(E, np.int64)
    place = np.stack([np.random.permutation(C) for _ in range(E)])
    for r, deal in enumerate((first, second)):
        for t in np.random.permutation(T):
            e = deal[t]
            if fill[e] < C: j = e * C + place[e, fill[e]]; fill[e] += 1; slot_token[j] = t; pos[r, t] = j
            else: pos[r, t] = E * C + t % PAD
    g = np.random.uniform(0.2, 0.8, T)
    w1 = [pack_weight(m, "e2m1") for m in n((E, K, H)) / np.sqrt(K) / s[None]]
    w3 = [pack_weight(m, "e2m1") for m in n((E, K, H)) / np.sqrt(K) / s[None] * u[None, None, :]]
    w2 = [pack_weight(m, "e2m1") for m in n((E, H, N)) / np.sqrt(H) / u[None, :, None]]
    return {
        "xT": (n((K, T)) * s).astype(np.float32),
        "w1_words": np.stack([m[0] for m in w1]),
        "w1_scales": np.stack([m[1] for m in w1]),
        "w3_words": np.stack([m[0] for m in w3]),
        "w3_scales": np.stack([m[1] for m in w3]),
        "w2_words": np.stack([m[0] for m in w2]),
        "w2_scales": np.stack([m[1] for m in w2]),
        "gate": np.stack([np.tile(g, (N, 1)), np.tile(1.0 - g, (N, 1))]).astype(np.float32),
        "offs": striped(slot_token),
        "pos1": striped(pos[0]),
        "pos2": striped(pos[1]),
    }


def reference(xT, w1_words, w1_scales, w3_words, w3_scales, w2_words, w2_scales, gate, offs, pos1, pos2):
    idx = unstriped(offs)
    w1 = np.stack([unpack_weight(w1_words[e], w1_scales[e], "e2m1") for e in range(E)])
    w3 = np.stack([unpack_weight(w3_words[e], w3_scales[e], "e2m1") for e in range(E)])
    w2 = np.stack([unpack_weight(w2_words[e], w2_scales[e], "e2m1") for e in range(E)])
    xq = mxq(f64(xT)[:, idx], 0, "e4m3")
    h = relu(by_expert(w1, xq))
    h = h * by_expert(w3, xq)
    y = by_expert(w2, mxq(h, 0, "e4m3"))
    y = np.concatenate([y, np.zeros((N, PAD))], axis=1)
    return f64(gate[0]) * y[:, unstriped(pos1)] + f64(gate[1]) * y[:, unstriped(pos2)]

@@ -1,0 +1,243 @@
+from contextlib import ExitStack
+
+import concourse.mybir as mybir
+from concourse.masks import make_identity
+
+K, T, E, C, H, N = 1536, 768, 4, 256, 512, 128
+PAD = 32
+FLOPS = 3355443200
+
+F32 = mybir.dt.float32
+BF16 = mybir.dt.bfloat16
+U32 = mybir.dt.uint32
+I32 = mybir.dt.int32
+U16 = mybir.dt.uint16
+U8 = mybir.dt.uint8
+FP8X4 = mybir.dt.float8_e4m3fn_x4
+FP4X4 = mybir.dt.float4_e2m1fn_x4
+COPY = mybir.ActivationFunctionType.Copy
+RELU = mybir.ActivationFunctionType.Relu
+MULT = mybir.AluOpType.mult
+ADD = mybir.AluOpType.add
+
+P = 128
+PASSES = K // 512
+SLOTS = E * C
+CHUNK = 256
+VECTOR_CHUNKS = {(0, 0), (0, 2), (1, 1)}
+BANKS = ((0, 1), (2, 3), (4, 5), (6, 7), (1, 3), (5, 7), (0, 2), (4, 6))
+PIECE = {"A": (0, 256), "B": (256, 512), "F": (0, 512), "C": (512, 1024)}
+
+
+def tile_moe_cap2_glu_relu_kernel(
+    tc, xT, w1_words, w1_scales, w3_words, w3_scales, w2_words, w2_scales, gate, offs, pos1, pos2, out
+):
+    nc = tc.nc
+    with ExitStack() as ctx:
+        keep = ctx.enter_context(tc.tile_pool(name="keep", bufs=1))
+        stage = ctx.enter_context(tc.tile_pool(name="stage", bufs=4))
+        psum = ctx.enter_context(tc.psum_pool(name="psum", bufs=1))
+
+        offs_t = keep.tile([P, SLOTS // 16], U16, name="offs_t")
+        pos1_t = keep.tile([P, T // 16], U16, name="pos1_t")
+        pos2_t = keep.tile([P, T // 16], U16, name="pos2_t")
+        xf = [keep.tile([P, 4, T], F32, name=f"xf{s}") for s in range(PASSES)]
+        xb = [keep.tile([P, 4 * T], BF16, name=f"xb{s}", align_bytes=64) for s in range(PASSES)]
+        xw = [keep.tile([P, T], U32, name=f"xw{s}", align_bytes=64) for s in range(PASSES)]
+        xs01 = keep.tile([P, T], U8, name="xs01", align_bytes=64)
+        xs2 = keep.tile([P, T], U8, name="xs2", align_bytes=64)
+        gw = [keep.tile([P, SLOTS], U32, name=f"gw{s}", align_bytes=64) for s in range(PASSES)]
+        gs = [keep.tile([P, SLOTS], U8, name=f"gs{s}", align_bytes=64) for s in range(PASSES)]
+        w1 = [keep.tile([P, PASSES, 2 * H], U8, name=f"w1_{e}", align_bytes=64) for e in range(E)]
+        w3 = [keep.tile([P, PASSES, 2 * H], U8, name=f"w3_{e}", align_bytes=64) for e in range(E)]
+        w2 = keep.tile([P, E, 2 * N], U8, name="w2", align_bytes=64)
+        w1s = keep.tile([P, E * PASSES, H], U8, name="w1s", align_bytes=64)
+        w3s = keep.tile([P, E * PASSES, H], U8, name="w3s", align_bytes=64)
+        w2s = keep.tile([P, E, N], U8, name="w2s", align_bytes=64)
+        gates = keep.tile([P, 2, T], F32, name="gates")
+        y = keep.tile([P, SLOTS + PAD], F32, name="y")
+        ident = keep.tile([P, P], F32, name="ident")
+
+        def load_x(s):
+            rows = xT[512 * s : 512 * (s + 1), :].rearrange("(p j) t -> p j t", j=4)
+            for cols in (slice(0, 512), slice(512, 768)) if s == 0 else (slice(0, 768),):
+                nc.sync.dma_start(out=xf[s][:, :, cols], in_=rows[:, :, cols])
+
+        def load_w(e):
+            for tile, dram in ((w1[e], w1_words), (w3[e], w3_words)):
+                nc.sync.dma_start(out=tile[:].bitcast(I32), in_=dram[e].rearrange("s p n -> p s n").bitcast(I32))
+
+        def load_scales(tile, dram, e0, e1):
+            passes = dram.shape[1]
+            rows = dram[e0:e1].rearrange("e s q n -> q (e s) n")
+            for quad in range(4):
+                nc.sync.dma_start(
+                    out=tile[32 * quad : 32 * quad + 4, passes * e0 : passes * e1, :].bitcast(I32),
+                    in_=rows[4 * quad : 4 * quad + 4, :, :].bitcast(I32),
+                )
+
+        for tile in (w3s, w1s, w2s):
+            nc.vector.memset(tile[:].bitcast(I32), 0)
+        nc.vector.memset(xs01[:].bitcast(I32), 0)
+        nc.vector.memset(xs2[:].bitcast(I32), 0)
+        nc.vector.memset(gs[0][:].bitcast(I32), 0)
+        nc.gpsimd.memset(y[:, SLOTS:], 0.0)
+        make_identity(nc, ident[:])
+
+        load_x(0)
+        nc.sync.dma_start(offs_t[:], offs)
+        load_x(1)
+        load_x(2)
+        load_w(0)
+        load_scales(w1s, w1_scales, 0, 2)
+        load_scales(w3s, w3_scales, 0, 2)
+        load_w(1)
+
+        def prepare(s):
+            for c in range(3):
+                dst = xb[s][:, 4 * CHUNK * c : 4 * CHUNK * (c + 1)].rearrange("p (c i j) -> p c j i", i=4, j=4)
+                src = xf[s][:, :, CHUNK * c : CHUNK * (c + 1)].rearrange("p j (c i) -> p c j i", i=4)
+                if (s, c) in VECTOR_CHUNKS:
+                    nc.vector.tensor_copy(dst, src)
+                else:
+                    nc.scalar.activation(dst, src, COPY)
+            for start, stop in ((0, 512), (512, 768)):
+                cols = slice(start, stop)
+                nc.vector.quantize_mx(
+                    out=xw[s][:, cols].bitcast(FP8X4),
+                    scales=(xs01[4:128, cols], xs01[:, cols], xs2[:, cols])[s],
+                    in_=xb[s][:, 4 * start : 4 * stop],
+                )
+
+        def g_words(s, piece):
+            start, stop = PIECE[piece]
+            nc.vector.tensor_copy(gw[s][:, start:stop], xw[s][:].indirect(offs_t[:, start // 16 : stop // 16]))
+
+        def g_bytes(s, piece):
+            start, stop = PIECE[piece]
+            nc.vector.tensor_copy(gs[s][:, start:stop], (None, xs01, xs2)[s][:].indirect(offs_t[:, start // 16 : stop // 16]))
+            if s == 1:
+                for q in range(4):
+                    nc.sync.dma_start(
+                        out=gs[0][32 * q : 32 * q + 4, start:stop].bitcast(I32),
+                        in_=gs[1][32 * q + 4 : 32 * q + 8, start:stop].bitcast(I32),
+                    )
+
+        acc, act, hid, hbf, codes = {}, {}, {}, {}, {}
+
+        def open_banks(half):
+            acc[half] = [psum.tile([P, H], F32, name=f"bank{b}") for b in BANKS[half]]
+
+        def mm(half, s, which=(0, 1)):
+            if half not in acc:
+                open_banks(half)
+            e = half // 2
+            slots = slice(128 * half, 128 * (half + 1))
+            for m in which:
+                w, ws = ((w1, w1s), (w3, w3s))[m]
+                nc.tensor.matmul_mx(
+                    out=acc[half][m][:],
+                    lhsT=gw[s][:, slots].bitcast(FP8X4),
+                    lhsT_scale=gs[s][:, slots],
+                    rhs=w[e][:, s, :].bitcast(FP4X4),
+                    rhs_scale=ws[:, PASSES * e + s, :],
+                    start=(s == 1),
+                    stop=(s == 2),
+                )
+
+        def relu(half):
+            act[half] = stage.tile([P, H], F32, name="ra")
+            nc.scalar.activation(
+                act[half][:].rearrange("m (u p d) -> m u p d", u=2, d=2),
+                acc[half][0][:].rearrange("m (p u d) -> m u p d", u=2, d=2),
+                RELU,
+            )
+
+        def mul(half):
+            hid[half] = stage.tile([P, H], BF16, name="h", align_bytes=64)
+            nc.vector.tensor_tensor(
+                hid[half][:].rearrange("m (u p d) -> m u p d", u=2, d=2),
+                acc[half][1][:].rearrange("m (p u d) -> m u p d", u=2, d=2),
+                act[half][:].rearrange("m (u p d) -> m u p d", u=2, d=2),
+                MULT,
+            )
+
+        def tr(half):
+            words = hid[half][:].bitcast(F32)
+            for u in range(2):
+                cols = slice(128 * u, 128 * (u + 1))
+                nc.tensor.transpose(acc[half][0][:, cols], words[:, cols], ident[:])
+
+        def tcp(half):
+            e, side = divmod(half, 2)
+            if side == 0:
+                hbf[e] = stage.tile([P, 4 * 256], BF16, name="hb", align_bytes=64)
+            nc.scalar.copy(
+                hbf[e][:, 512 * side : 512 * (side + 1)].bitcast(F32).rearrange("p (r u) -> p r u", u=2),
+                acc[half][0][:, 0:256].rearrange("p (u r) -> p r u", u=2),
+            )
+
+        def hq(e, c0=0, c1=256):
+            if c0 == 0:
+                hw = stage.tile([P, 256], U32, name="hw", align_bytes=64)
+                hs = stage.tile([P, 256], U8, name="hs", align_bytes=64)
+                codes[e] = (hw, hs)
+            hw, hs = codes[e]
+            nc.vector.quantize_mx(out=hw[:, c0:c1].bitcast(FP8X4), scales=hs[:, c0:c1], in_=hbf[e][:, 4 * c0 : 4 * c1])
+
+        def m2(e, c0=0, c1=256):
+            hw, hs = codes[e]
+            bank = acc[2 * e + 1 if c1 == 256 else 2 * e][0]
+            nc.tensor.matmul_mx(
+                out=bank[:, 256 : 256 + c1 - c0],
+                lhsT=w2[:, e, :].bitcast(FP4X4),
+                lhsT_scale=w2s[:, e, :],
+                rhs=hw[:, c0:c1].bitcast(FP8X4),
+                rhs_scale=hs[:, c0:c1],
+                start=True,
+                stop=True,
+            )
+
+        def ycp(e, c0=0, c1=256):
+            bank = acc[2 * e + 1 if c1 == 256 else 2 * e][0]
+            nc.scalar.copy(y[:, 256 * e + c0 : 256 * e + c1], bank[:, 256 : 256 + c1 - c0])
+
+        A, B = (0,), (1,)
+        prepare(0); g_words(0, "F"); g_words(0, "C")
+        prepare(1); g_bytes(1, "F"); g_words(1, "F"); g_bytes(1, "C")
+        load_scales(w1s, w1_scales, 2, 4)
+        load_scales(w3s, w3_scales, 2, 4)
+        load_w(2)
+        load_scales(w2s, w2_scales, 0, 4)
+        nc.sync.dma_start(out=w2[:].bitcast(I32), in_=w2_words[:, 0].rearrange("e p n -> p e n").bitcast(I32))
+        load_w(3)
+        nc.sync.dma_start(pos1_t[:], pos1)
+        nc.sync.dma_start(pos2_t[:], pos2)
+        nc.sync.dma_start(out=gates[:], in_=gate.rearrange("r p t -> p r t"))
+
+        prepare(2); g_bytes(2, "A"); g_words(2, "A"); g_bytes(2, "B"); g_words(1, "C"); g_words(2, "B")
+        mm(0, 1, A); mm(1, 1, A); mm(0, 1, B); mm(1, 1, B); mm(0, 0); mm(1, 0)
+        for h in (0, 1):
+            mm(h, 2); relu(h)
+        for h in (2, 3):
+            mm(h, 1); mm(h, 0)
+        for h in (2, 3):
+            mm(h, 2); relu(h)
+        mul(0); g_words(2, "C"); mul(1); g_bytes(2, "C"); mul(2); mul(3)
+        mm(4, 1, A); mm(4, 0, A); tr(0); tr(1); tcp(0); mm(4, 1, B); mm(4, 0, B); tcp(1); hq(0)
+        mm(4, 2); relu(4); mm(5, 1, A); mm(5, 0, A); tr(2); tr(3); tcp(2); tcp(3); m2(0); ycp(0); hq(1)
+        mm(5, 1, B); mm(5, 0, B); mm(5, 2); relu(5); mul(4)
+        mm(6, 1); mm(6, 0); m2(1); ycp(1); mul(5); mm(6, 2); relu(6)
+        mm(7, 1, A); mm(7, 0, A); mm(7, 2, A); relu(7); mm(7, 1, B); mm(7, 0, B); mm(7, 2, B); mul(6); mul(7)
+        tr(4); tr(5); tcp(4); tcp(5); tr(6); tcp(6); tr(7); hq(2); hq(3, 0, 128); tcp(7); hq(3, 128, 256)
+        m2(2); m2(3, 0, 128); ycp(2); ycp(3, 0, 128); m2(3, 128, 256); ycp(3, 128, 256)
+
+        t1 = keep.tile([P, T], F32, name="t1")
+        t2 = keep.tile([P, T], F32, name="t2")
+        o = keep.tile([P, T], F32, name="o")
+        nc.vector.tensor_tensor(t1[:], y[:].indirect(pos1_t[:]), gates[:, 0, :], MULT)
+        nc.vector.tensor_tensor(t2[:], y[:].indirect(pos2_t[:]), gates[:, 1, :], MULT)
+        for c in range(2):
+            cols = slice(384 * c, 384 * (c + 1))
+            nc.vector.tensor_tensor(o[:, cols], t1[:, cols], t2[:, cols], ADD)
+            nc.sync.dma_start(out=out[:, cols], in_=o[:, cols])

@@ -23,10 +23,12 @@ ADD = mybir.AluOpType.add
 P = 128
 PASSES = K // 512
 SLOTS = E * C
-CHUNK = 256
-VECTOR_CHUNKS = {(0, 0), (0, 2), (1, 1)}
-BANKS = ((0, 1), (2, 3), (4, 5), (6, 7), (1, 3), (5, 7), (0, 2), (4, 6))
-PIECE = {"A": (0, 256), "B": (256, 512), "F": (0, 512), "C": (512, 1024)}
+X_PIECES = (
+    ((0, 512, 320), (512, 768, 160)),
+    ((0, 768, 512),),
+    ((0, 512, 192), (512, 768, 128)),
+)
+TURN_BANKS = {0: 2, 2: 4, 4: 6, 6: 3, 7: 5}
 
 
 def tile_moe_cap2_glu_relu_kernel(
@@ -35,202 +37,262 @@ def tile_moe_cap2_glu_relu_kernel(
     nc = tc.nc
     with ExitStack() as ctx:
         keep = ctx.enter_context(tc.tile_pool(name="keep", bufs=1))
-        stage = ctx.enter_context(tc.tile_pool(name="stage", bufs=4))
         psum = ctx.enter_context(tc.psum_pool(name="psum", bufs=1))
 
         offs_t = keep.tile([P, SLOTS // 16], U16, name="offs_t")
         pos1_t = keep.tile([P, T // 16], U16, name="pos1_t")
         pos2_t = keep.tile([P, T // 16], U16, name="pos2_t")
-        xf = [keep.tile([P, 4, T], F32, name=f"xf{s}") for s in range(PASSES)]
+        xf = [
+            [keep.tile([P, 4, c1 - c0], F32, name=f"xf{s}_{c0}") for c0, c1, share in X_PIECES[s]] for s in range(PASSES)
+        ]
         xb = [keep.tile([P, 4 * T], BF16, name=f"xb{s}", align_bytes=64) for s in range(PASSES)]
         xw = [keep.tile([P, T], U32, name=f"xw{s}", align_bytes=64) for s in range(PASSES)]
         xs01 = keep.tile([P, T], U8, name="xs01", align_bytes=64)
         xs2 = keep.tile([P, T], U8, name="xs2", align_bytes=64)
         gw = [keep.tile([P, SLOTS], U32, name=f"gw{s}", align_bytes=64) for s in range(PASSES)]
         gs = [keep.tile([P, SLOTS], U8, name=f"gs{s}", align_bytes=64) for s in range(PASSES)]
-        w1 = [keep.tile([P, PASSES, 2 * H], U8, name=f"w1_{e}", align_bytes=64) for e in range(E)]
+        w1 = [[keep.tile([P, 2, 2 * H], U8, name=f"w1_{s}_{i}", align_bytes=64) for i in range(2)] for s in range(PASSES)]
         w3 = [keep.tile([P, PASSES, 2 * H], U8, name=f"w3_{e}", align_bytes=64) for e in range(E)]
-        w2 = keep.tile([P, E, 2 * N], U8, name="w2", align_bytes=64)
         w1s = keep.tile([P, E * PASSES, H], U8, name="w1s", align_bytes=64)
-        w3s = keep.tile([P, E * PASSES, H], U8, name="w3s", align_bytes=64)
+        w3s = [keep.tile([P, 2 * PASSES, H], U8, name=f"w3s_{i}", align_bytes=64) for i in range(2)]
+        w2 = keep.tile([P, E, 2 * N], U8, name="w2", align_bytes=64)
         w2s = keep.tile([P, E, N], U8, name="w2s", align_bytes=64)
         gates = keep.tile([P, 2, T], F32, name="gates")
         y = keep.tile([P, SLOTS + PAD], F32, name="y")
         ident = keep.tile([P, P], F32, name="ident")
 
-        def load_x(s):
+        def load_x(s, k):
+            c0, c1, share = X_PIECES[s][k]
             rows = xT[512 * s : 512 * (s + 1), :].rearrange("(p j) t -> p j t", j=4)
-            for cols in (slice(0, 512), slice(512, 768)) if s == 0 else (slice(0, 768),):
-                nc.sync.dma_start(out=xf[s][:, :, cols], in_=rows[:, :, cols])
+            nc.sync.dma_start(out=xf[s][k][:], in_=rows[:, :, c0:c1])
 
-        def load_w(e):
-            for tile, dram in ((w1[e], w1_words), (w3[e], w3_words)):
-                nc.sync.dma_start(out=tile[:].bitcast(I32), in_=dram[e].rearrange("s p n -> p s n").bitcast(I32))
+        def load_w1(s, i):
+            nc.sync.dma_start(
+                out=w1[s][i][:].bitcast(I32), in_=w1_words[2 * i : 2 * i + 2, s].rearrange("e p n -> p e n").bitcast(I32)
+            )
+
+        def load_w3(e):
+            nc.sync.dma_start(out=w3[e][:].bitcast(I32), in_=w3_words[e].rearrange("s p n -> p s n").bitcast(I32))
 
         def load_scales(tile, dram, e0, e1):
-            passes = dram.shape[1]
-            rows = dram[e0:e1].rearrange("e s q n -> q (e s) n")
-            for quad in range(4):
-                nc.sync.dma_start(
-                    out=tile[32 * quad : 32 * quad + 4, passes * e0 : passes * e1, :].bitcast(I32),
-                    in_=rows[4 * quad : 4 * quad + 4, :, :].bitcast(I32),
-                )
+            rows = dram[e0:e1].rearrange("e s (q r) n -> r q (e s) n", r=4)
+            for r in range(4):
+                nc.sync.dma_start(out=tile[r:128:32, :, :].bitcast(I32), in_=rows[r].bitcast(I32))
 
-        for tile in (w3s, w1s, w2s):
+        for tile in (w1s, xs01, xs2, gs[1], w3s[0], w3s[1], w2s):
             nc.vector.memset(tile[:].bitcast(I32), 0)
-        nc.vector.memset(xs01[:].bitcast(I32), 0)
-        nc.vector.memset(xs2[:].bitcast(I32), 0)
-        nc.vector.memset(gs[0][:].bitcast(I32), 0)
         nc.gpsimd.memset(y[:, SLOTS:], 0.0)
         make_identity(nc, ident[:])
 
-        load_x(0)
+        for k in range(2):
+            load_x(0, k)
         nc.sync.dma_start(offs_t[:], offs)
-        load_x(1)
-        load_x(2)
-        load_w(0)
-        load_scales(w1s, w1_scales, 0, 2)
-        load_scales(w3s, w3_scales, 0, 2)
-        load_w(1)
+        load_x(1, 0)
+        load_scales(w1s, w1_scales, 0, 4)
+        load_w1(0, 0)
+        load_w1(0, 1)
+        for k in range(2):
+            load_x(2, k)
+        load_w1(1, 0)
 
-        def prepare(s):
-            for c in range(3):
-                dst = xb[s][:, 4 * CHUNK * c : 4 * CHUNK * (c + 1)].rearrange("p (c i j) -> p c j i", i=4, j=4)
-                src = xf[s][:, :, CHUNK * c : CHUNK * (c + 1)].rearrange("p j (c i) -> p c j i", i=4)
-                if (s, c) in VECTOR_CHUNKS:
+        def prepare(s, k):
+            c0, c1, share = X_PIECES[s][k]
+            for a, b, engine in ((0, share, "vector"), (share, c1 - c0, "scalar")):
+                if a == b:
+                    continue
+                dst = xb[s][:, 4 * (c0 + a) : 4 * (c0 + b)].rearrange("p (c i j) -> p c j i", i=4, j=4)
+                src = xf[s][k][:, :, a:b].rearrange("p j (c i) -> p c j i", i=4)
+                if engine == "vector":
                     nc.vector.tensor_copy(dst, src)
                 else:
                     nc.scalar.activation(dst, src, COPY)
-            for start, stop in ((0, 512), (512, 768)):
-                cols = slice(start, stop)
-                nc.vector.quantize_mx(
-                    out=xw[s][:, cols].bitcast(FP8X4),
-                    scales=(xs01[4:128, cols], xs01[:, cols], xs2[:, cols])[s],
-                    in_=xb[s][:, 4 * start : 4 * stop],
-                )
 
-        def g_words(s, piece):
-            start, stop = PIECE[piece]
+        def quantise(s, k):
+            c0, c1 = ((0, 512), (512, 768))[k]
+            nc.vector.quantize_mx(
+                out=xw[s][:, c0:c1].bitcast(FP8X4),
+                scales=(xs01[:, c0:c1], xs01[4:128, c0:c1], xs2[:, c0:c1])[s],
+                in_=xb[s][:, 4 * c0 : 4 * c1],
+            )
+
+        def g_words(s, start, stop):
             nc.vector.tensor_copy(gw[s][:, start:stop], xw[s][:].indirect(offs_t[:, start // 16 : stop // 16]))
 
-        def g_bytes(s, piece):
-            start, stop = PIECE[piece]
-            nc.vector.tensor_copy(gs[s][:, start:stop], (None, xs01, xs2)[s][:].indirect(offs_t[:, start // 16 : stop // 16]))
-            if s == 1:
-                for q in range(4):
-                    nc.sync.dma_start(
-                        out=gs[0][32 * q : 32 * q + 4, start:stop].bitcast(I32),
-                        in_=gs[1][32 * q + 4 : 32 * q + 8, start:stop].bitcast(I32),
-                    )
+        def g_bytes(s, start, stop):
+            nc.vector.tensor_copy(gs[s][:, start:stop], (xs01, None, xs2)[s][:].indirect(offs_t[:, start // 16 : stop // 16]))
 
-        acc, act, hid, hbf, codes = {}, {}, {}, {}, {}
+        def move_bytes():
+            for r in range(4):
+                nc.sync.dma_start(out=gs[1][r:128:32, :].bitcast(I32), in_=gs[0][4 + r : 128 : 32, :].bitcast(I32))
 
-        def open_banks(half):
-            acc[half] = [psum.tile([P, H], F32, name=f"bank{b}") for b in BANKS[half]]
+        acc, act, hid, turned = {}, {}, {}, {}
 
-        def mm(half, s, which=(0, 1)):
-            if half not in acc:
-                open_banks(half)
+        def mm(half, m, s):
             e = half // 2
             slots = slice(128 * half, 128 * (half + 1))
-            for m in which:
-                w, ws = ((w1, w1s), (w3, w3s))[m]
-                nc.tensor.matmul_mx(
-                    out=acc[half][m][:],
-                    lhsT=gw[s][:, slots].bitcast(FP8X4),
-                    lhsT_scale=gs[s][:, slots],
-                    rhs=w[e][:, s, :].bitcast(FP4X4),
-                    rhs_scale=ws[:, PASSES * e + s, :],
-                    start=(s == 1),
-                    stop=(s == 2),
-                )
+            if s == 0:
+                acc[half, m] = psum.tile([P, H], F32, name=f"bank{half}")
+            if m == 0:
+                w, ws = w1[s][e // 2][:, e % 2, :], w1s[:, PASSES * e + s, :]
+            else:
+                w, ws = w3[e][:, s, :], w3s[e // 2][:, PASSES * (e % 2) + s, :]
+            nc.tensor.matmul_mx(
+                out=acc[half, m][:],
+                lhsT=gw[s][:, slots].bitcast(FP8X4),
+                lhsT_scale=gs[s][:, slots],
+                rhs=w.bitcast(FP4X4),
+                rhs_scale=ws,
+                start=(s == 0),
+                stop=(s == 2),
+            )
 
         def relu(half):
-            act[half] = stage.tile([P, H], F32, name="ra")
+            act[half] = keep.tile([P, H], F32, name=f"ra{half}", align_bytes=64)
             nc.scalar.activation(
                 act[half][:].rearrange("m (u p d) -> m u p d", u=2, d=2),
-                acc[half][0][:].rearrange("m (p u d) -> m u p d", u=2, d=2),
+                acc[half, 0][:].rearrange("m (p u d) -> m u p d", u=2, d=2),
                 RELU,
             )
 
         def mul(half):
-            hid[half] = stage.tile([P, H], BF16, name="h", align_bytes=64)
+            hid[half] = keep.tile([P, H], BF16, name=f"h{half}", align_bytes=64)
             nc.vector.tensor_tensor(
                 hid[half][:].rearrange("m (u p d) -> m u p d", u=2, d=2),
-                acc[half][1][:].rearrange("m (p u d) -> m u p d", u=2, d=2),
+                acc[half, 1][:].rearrange("m (p u d) -> m u p d", u=2, d=2),
                 act[half][:].rearrange("m (u p d) -> m u p d", u=2, d=2),
                 MULT,
             )
 
+        def turn_bank(half):
+            lead = half if half in TURN_BANKS else half - 1
+            if lead not in turned:
+                turned[lead] = psum.tile([P, H], F32, name=f"bank{TURN_BANKS[lead]}")
+            return turned[lead], 256 * (half - lead)
+
         def tr(half):
+            bank, first = turn_bank(half)
             words = hid[half][:].bitcast(F32)
             for u in range(2):
-                cols = slice(128 * u, 128 * (u + 1))
-                nc.tensor.transpose(acc[half][0][:, cols], words[:, cols], ident[:])
+                nc.tensor.transpose(bank[:, first + 128 * u : first + 128 * (u + 1)], words[:, 128 * u : 128 * (u + 1)], ident[:])
 
-        def tcp(half):
-            e, side = divmod(half, 2)
-            if side == 0:
-                hbf[e] = stage.tile([P, 4 * 256], BF16, name="hb", align_bytes=64)
-            nc.scalar.copy(
-                hbf[e][:, 512 * side : 512 * (side + 1)].bitcast(F32).rearrange("p (r u) -> p r u", u=2),
-                acc[half][0][:, 0:256].rearrange("p (u r) -> p r u", u=2),
-            )
+        def second(half, count):
+            bank, first = turn_bank(half)
+            width = 128 * count
+            hb = keep.tile([P, 4 * 256], BF16, name=f"hb{half}", align_bytes=64)
+            hs = keep.tile([P, 256], U8, name=f"hs{half}", align_bytes=64)
+            codes = []
 
-        def hq(e, c0=0, c1=256):
-            if c0 == 0:
-                hw = stage.tile([P, 256], U32, name="hw", align_bytes=64)
-                hs = stage.tile([P, 256], U8, name="hs", align_bytes=64)
-                codes[e] = (hw, hs)
-            hw, hs = codes[e]
-            nc.vector.quantize_mx(out=hw[:, c0:c1].bitcast(FP8X4), scales=hs[:, c0:c1], in_=hbf[e][:, 4 * c0 : 4 * c1])
+            def tcp():
+                nc.scalar.copy(
+                    hb[:, 0 : 4 * width].bitcast(F32).rearrange("p (g r u) -> p g r u", g=count, u=2),
+                    bank[:, 0 : 2 * width].rearrange("p (g u r) -> p g r u", g=count, u=2),
+                )
 
-        def m2(e, c0=0, c1=256):
-            hw, hs = codes[e]
-            bank = acc[2 * e + 1 if c1 == 256 else 2 * e][0]
-            nc.tensor.matmul_mx(
-                out=bank[:, 256 : 256 + c1 - c0],
-                lhsT=w2[:, e, :].bitcast(FP4X4),
-                lhsT_scale=w2s[:, e, :],
-                rhs=hw[:, c0:c1].bitcast(FP8X4),
-                rhs_scale=hs[:, c0:c1],
-                start=True,
-                stop=True,
-            )
+            def hq():
+                hw = keep.tile([P, 256], U32, name=f"ra{half + 4}" if half < 4 else f"hw{half}", align_bytes=64)
+                codes.append(hw)
+                nc.vector.quantize_mx(out=hw[:, 0:width].bitcast(FP8X4), scales=hs[:, 0:width], in_=hb[:, 0 : 4 * width])
 
-        def ycp(e, c0=0, c1=256):
-            bank = acc[2 * e + 1 if c1 == 256 else 2 * e][0]
-            nc.scalar.copy(y[:, 256 * e + c0 : 256 * e + c1], bank[:, 256 : 256 + c1 - c0])
+            def m2():
+                nc.tensor.matmul_mx(
+                    out=bank[:, 0:width],
+                    lhsT=w2[:, half // 2, :].bitcast(FP4X4),
+                    lhsT_scale=w2s[:, half // 2, :],
+                    rhs=codes[0][:, 0:width].bitcast(FP8X4),
+                    rhs_scale=hs[:, 0:width],
+                    start=True,
+                    stop=True,
+                )
 
-        A, B = (0,), (1,)
-        prepare(0); g_words(0, "F"); g_words(0, "C")
-        prepare(1); g_bytes(1, "F"); g_words(1, "F"); g_bytes(1, "C")
-        load_scales(w1s, w1_scales, 2, 4)
-        load_scales(w3s, w3_scales, 2, 4)
-        load_w(2)
+            def ycp():
+                nc.scalar.copy(y[:, 128 * half : 128 * half + width], bank[:, 0:width])
+
+            return tcp, hq, m2, ycp
+
+        for k in range(2):
+            prepare(0, k)
+            quantise(0, k)
+        g_words(0, 0, 512)
+        g_words(0, 512, 1024)
+        prepare(1, 0)
+        quantise(1, 1)
+        quantise(1, 0)
+        g_bytes(0, 0, 512)
+        g_bytes(0, 512, 1024)
+        move_bytes()
+        g_words(1, 0, 512)
+        g_words(1, 512, 1024)
+
+        load_w1(2, 0)
+        load_w1(1, 1)
+        load_scales(w3s[0], w3_scales, 0, 2)
+        load_w3(0)
+        load_w3(1)
+        load_w1(2, 1)
+        load_scales(w3s[1], w3_scales, 2, 4)
+        load_w3(2)
         load_scales(w2s, w2_scales, 0, 4)
         nc.sync.dma_start(out=w2[:].bitcast(I32), in_=w2_words[:, 0].rearrange("e p n -> p e n").bitcast(I32))
-        load_w(3)
+        load_w3(3)
         nc.sync.dma_start(pos1_t[:], pos1)
         nc.sync.dma_start(pos2_t[:], pos2)
         nc.sync.dma_start(out=gates[:], in_=gate.rearrange("r p t -> p r t"))
 
-        prepare(2); g_bytes(2, "A"); g_words(2, "A"); g_bytes(2, "B"); g_words(1, "C"); g_words(2, "B")
-        mm(0, 1, A); mm(1, 1, A); mm(0, 1, B); mm(1, 1, B); mm(0, 0); mm(1, 0)
-        for h in (0, 1):
-            mm(h, 2); relu(h)
-        for h in (2, 3):
-            mm(h, 1); mm(h, 0)
-        for h in (2, 3):
-            mm(h, 2); relu(h)
-        mul(0); g_words(2, "C"); mul(1); g_bytes(2, "C"); mul(2); mul(3)
-        mm(4, 1, A); mm(4, 0, A); tr(0); tr(1); tcp(0); mm(4, 1, B); mm(4, 0, B); tcp(1); hq(0)
-        mm(4, 2); relu(4); mm(5, 1, A); mm(5, 0, A); tr(2); tr(3); tcp(2); tcp(3); m2(0); ycp(0); hq(1)
-        mm(5, 1, B); mm(5, 0, B); mm(5, 2); relu(5); mul(4)
-        mm(6, 1); mm(6, 0); m2(1); ycp(1); mul(5); mm(6, 2); relu(6)
-        mm(7, 1, A); mm(7, 0, A); mm(7, 2, A); relu(7); mm(7, 1, B); mm(7, 0, B); mm(7, 2, B); mul(6); mul(7)
-        tr(4); tr(5); tcp(4); tcp(5); tr(6); tcp(6); tr(7); hq(2); hq(3, 0, 128); tcp(7); hq(3, 128, 256)
-        m2(2); m2(3, 0, 128); ycp(2); ycp(3, 0, 128); m2(3, 128, 256); ycp(3, 128, 256)
+        def w3_sum(half):
+            for s in range(PASSES):
+                mm(half, 1, s)
+            mul(half)
+
+        def last_pass(e):
+            for h in (2 * e, 2 * e + 1):
+                mm(h, 0, 2)
+                relu(h)
+
+        for h in range(8):
+            mm(h, 0, 0)
+        for h in range(4):
+            mm(h, 0, 1)
+        for k in range(2):
+            prepare(2, k)
+        for k in range(2):
+            quantise(2, k)
+        for e in range(E):
+            g_bytes(2, 256 * e, 256 * (e + 1))
+            g_words(2, 256 * e, 256 * (e + 1))
+        last_pass(0)
+        for h in range(4, 8):
+            mm(h, 0, 1)
+        last_pass(1)
+        w3_sum(0)
+        w3_sum(1)
+        last_pass(2)
+        w3_sum(2)
+        last_pass(3)
+        w3_sum(3)
+        steps = {}
+        for e in range(3):
+            tr(2 * e)
+            tr(2 * e + 1)
+            steps[e] = second(2 * e, 2)
+            steps[e][0]()
+            if e > 0:
+                for step in steps[e - 1][2:]:
+                    step()
+            if e < 2:
+                w3_sum(2 * e + 4)
+                steps[e][1]()
+                w3_sum(2 * e + 5)
+        steps[2][1]()
+        last = [steps[2][2:]]
+        for h in (6, 7):
+            tr(h)
+            tcp, hq, m2, ycp = second(h, 1)
+            tcp()
+            hq()
+            last.append((m2, ycp))
+        for m2, ycp in last:
+            m2()
+            ycp()
 
         t1 = keep.tile([P, T], F32, name="t1")
         t2 = keep.tile([P, T], F32, name="t2")

@@ -23,12 +23,12 @@ ADD = mybir.AluOpType.add
 P = 128
 PASSES = K // 512
 SLOTS = E * C
-X_PIECES = (
-    ((0, 512, 320), (512, 768, 160)),
-    ((0, 768, 512),),
-    ((0, 512, 192), (512, 768, 128)),
-)
-TURN_BANKS = {0: 2, 2: 4, 4: 6, 6: 3, 7: 5}
+HALVES = ((0, 512), (512, 768))
+X_PIECES = (((0, 512, 352), (512, 768, 128)), ((0, 768, 384),), ((0, 512, 64), (512, 768, 128)))
+A_BANKS = (0, 1, 2, 3, 0, 1, 2, 3)
+B_BANKS = (4, 5, 6, 7, 0, 1, 4, 5)
+TURN_BANKS = {0: 2, 2: 3, 4: 6, 6: 7, 7: 0}
+HOLD = {"gw1_1": "xb2_1", "hw0": "ra5", "hw2": "ra6"}
 
 
 def tile_moe_cap2_glu_relu_kernel(
@@ -38,262 +38,221 @@ def tile_moe_cap2_glu_relu_kernel(
     with ExitStack() as ctx:
         keep = ctx.enter_context(tc.tile_pool(name="keep", bufs=1))
         psum = ctx.enter_context(tc.psum_pool(name="psum", bufs=1))
+        tiles = {}
+
+        def sb(name, shape, dtype):
+            if name not in tiles:
+                tiles[name] = keep.tile(shape, dtype, name=HOLD.get(name, name), align_bytes=64)
+            return tiles[name]
 
         offs_t = keep.tile([P, SLOTS // 16], U16, name="offs_t")
         pos1_t = keep.tile([P, T // 16], U16, name="pos1_t")
         pos2_t = keep.tile([P, T // 16], U16, name="pos2_t")
-        xf = [
-            [keep.tile([P, 4, c1 - c0], F32, name=f"xf{s}_{c0}") for c0, c1, share in X_PIECES[s]] for s in range(PASSES)
-        ]
-        xb = [keep.tile([P, 4 * T], BF16, name=f"xb{s}", align_bytes=64) for s in range(PASSES)]
-        xw = [keep.tile([P, T], U32, name=f"xw{s}", align_bytes=64) for s in range(PASSES)]
-        xs01 = keep.tile([P, T], U8, name="xs01", align_bytes=64)
-        xs2 = keep.tile([P, T], U8, name="xs2", align_bytes=64)
-        gw = [keep.tile([P, SLOTS], U32, name=f"gw{s}", align_bytes=64) for s in range(PASSES)]
-        gs = [keep.tile([P, SLOTS], U8, name=f"gs{s}", align_bytes=64) for s in range(PASSES)]
-        w1 = [[keep.tile([P, 2, 2 * H], U8, name=f"w1_{s}_{i}", align_bytes=64) for i in range(2)] for s in range(PASSES)]
-        w3 = [keep.tile([P, PASSES, 2 * H], U8, name=f"w3_{e}", align_bytes=64) for e in range(E)]
-        w1s = keep.tile([P, E * PASSES, H], U8, name="w1s", align_bytes=64)
-        w3s = [keep.tile([P, 2 * PASSES, H], U8, name=f"w3s_{i}", align_bytes=64) for i in range(2)]
-        w2 = keep.tile([P, E, 2 * N], U8, name="w2", align_bytes=64)
-        w2s = keep.tile([P, E, N], U8, name="w2s", align_bytes=64)
-        gates = keep.tile([P, 2, T], F32, name="gates")
         y = keep.tile([P, SLOTS + PAD], F32, name="y")
         ident = keep.tile([P, P], F32, name="ident")
+        words_dram = (w1_words, w3_words)
+        scales_dram = (w1_scales, w3_scales)
+        where_w, where_s = {}, {}
+
+        def zero(name, shape):
+            nc.vector.memset(sb(name, shape, U8)[:].bitcast(I32), 0)
 
         def load_x(s, k):
             c0, c1, share = X_PIECES[s][k]
             rows = xT[512 * s : 512 * (s + 1), :].rearrange("(p j) t -> p j t", j=4)
-            nc.sync.dma_start(out=xf[s][k][:], in_=rows[:, :, c0:c1])
+            nc.sync.dma_start(out=sb(f"xf{s}_{k}", [P, 4, c1 - c0], F32)[:], in_=rows[:, :, c0:c1])
 
-        def load_w1(s, i):
-            nc.sync.dma_start(
-                out=w1[s][i][:].bitcast(I32), in_=w1_words[2 * i : 2 * i + 2, s].rearrange("e p n -> p e n").bitcast(I32)
-            )
+        def load_pass(m, s, e0, e1):
+            tile = sb(f"w{m}_p{s}_{e0}", [P, e1 - e0, 2 * H], U8)
+            nc.sync.dma_start(out=tile[:].bitcast(I32), in_=words_dram[m][e0:e1, s].rearrange("e p n -> p e n").bitcast(I32))
+            for e in range(e0, e1):
+                where_w[m, e, s] = tile[:, e - e0, :]
 
-        def load_w3(e):
-            nc.sync.dma_start(out=w3[e][:].bitcast(I32), in_=w3_words[e].rearrange("s p n -> p s n").bitcast(I32))
+        def load_expert(m, e, s0=0, s1=PASSES):
+            tile = sb(f"w{m}_e{e}_{s0}", [P, s1 - s0, 2 * H], U8)
+            nc.sync.dma_start(out=tile[:].bitcast(I32), in_=words_dram[m][e, s0:s1].rearrange("s p n -> p s n").bitcast(I32))
+            for s in range(s0, s1):
+                where_w[m, e, s] = tile[:, s - s0, :]
 
-        def load_scales(tile, dram, e0, e1):
-            rows = dram[e0:e1].rearrange("e s (q r) n -> r q (e s) n", r=4)
+        def scale_rows(tile, dram):
+            rows = dram.rearrange("e s (q r) n -> r q (e s) n", r=4)
             for r in range(4):
                 nc.sync.dma_start(out=tile[r:128:32, :, :].bitcast(I32), in_=rows[r].bitcast(I32))
 
-        for tile in (w1s, xs01, xs2, gs[1], w3s[0], w3s[1], w2s):
-            nc.vector.memset(tile[:].bitcast(I32), 0)
-        nc.gpsimd.memset(y[:, SLOTS:], 0.0)
-        make_identity(nc, ident[:])
+        def load_scales(m, e0, e1):
+            tile = tiles[f"s{m}_{e0}"]
+            scale_rows(tile, scales_dram[m][e0:e1])
+            for e in range(e0, e1):
+                for s in range(PASSES):
+                    where_s[m, e, s] = tile[:, PASSES * (e - e0) + s, :]
 
-        for k in range(2):
-            load_x(0, k)
-        nc.sync.dma_start(offs_t[:], offs)
-        load_x(1, 0)
-        load_scales(w1s, w1_scales, 0, 4)
-        load_w1(0, 0)
-        load_w1(0, 1)
-        for k in range(2):
-            load_x(2, k)
-        load_w1(1, 0)
+        def load_w2():
+            nc.sync.dma_start(
+                out=sb("w2", [P, E, 2 * N], U8)[:].bitcast(I32), in_=w2_words[:, 0].rearrange("e p n -> p e n").bitcast(I32)
+            )
+
+        def load_pos():
+            nc.sync.dma_start(pos1_t[:], pos1)
+            nc.sync.dma_start(pos2_t[:], pos2)
+
+        def load_gates():
+            nc.sync.dma_start(out=sb("gates", [P, 2, T], F32)[:], in_=gate.rearrange("r p t -> p r t"))
+
+        def xb(s, part):
+            return sb(f"xb{s}_{part}", [P, 4 * (HALVES[part][1] - HALVES[part][0])], BF16)
 
         def prepare(s, k):
             c0, c1, share = X_PIECES[s][k]
-            for a, b, engine in ((0, share, "vector"), (share, c1 - c0, "scalar")):
-                if a == b:
-                    continue
-                dst = xb[s][:, 4 * (c0 + a) : 4 * (c0 + b)].rearrange("p (c i j) -> p c j i", i=4, j=4)
-                src = xf[s][k][:, :, a:b].rearrange("p j (c i) -> p c j i", i=4)
+            cuts = sorted({0, share, c1 - c0} | ({512 - c0} if c0 < 512 < c1 else set()))
+            for a, b in zip(cuts, cuts[1:]):
+                engine = "vector" if b <= share else "scalar"
+                part = (c0 + a) // 512
+                dst = xb(s, part)[:, 4 * (c0 + a - 512 * part) : 4 * (c0 + b - 512 * part)].rearrange("p (c i j) -> p c j i", i=4, j=4)
+                src = tiles[f"xf{s}_{k}"][:, :, a:b].rearrange("p j (c i) -> p c j i", i=4)
                 if engine == "vector":
                     nc.vector.tensor_copy(dst, src)
                 else:
                     nc.scalar.activation(dst, src, COPY)
 
-        def quantise(s, k):
-            c0, c1 = ((0, 512), (512, 768))[k]
-            nc.vector.quantize_mx(
-                out=xw[s][:, c0:c1].bitcast(FP8X4),
-                scales=(xs01[:, c0:c1], xs01[4:128, c0:c1], xs2[:, c0:c1])[s],
-                in_=xb[s][:, 4 * c0 : 4 * c1],
+        def quantise(s, part):
+            c0, c1 = HALVES[part]
+            plane = (tiles["xs0"][:, c0:c1], tiles["xs0"][4:128, c0:c1], tiles["xs2"][:, c0:c1])[s]
+            nc.vector.quantize_mx(out=sb(f"xw{s}", [P, T], U32)[:, c0:c1].bitcast(FP8X4), scales=plane, in_=xb(s, part)[:])
+
+        def gather(sort, s, start, stop):
+            pair = start // 512
+            if sort == "s":
+                tile, first = sb(f"gs{s}", [P, SLOTS], U8), 0
+            else:
+                tile, first = sb(f"gw{s}_{pair}", [P, 512], U32), 512 * pair
+            nc.vector.tensor_copy(
+                tile[:, start - first : stop - first], tiles[f"x{sort}{s}"][:].indirect(offs_t[:, start // 16 : stop // 16])
             )
-
-        def g_words(s, start, stop):
-            nc.vector.tensor_copy(gw[s][:, start:stop], xw[s][:].indirect(offs_t[:, start // 16 : stop // 16]))
-
-        def g_bytes(s, start, stop):
-            nc.vector.tensor_copy(gs[s][:, start:stop], (xs01, None, xs2)[s][:].indirect(offs_t[:, start // 16 : stop // 16]))
 
         def move_bytes():
             for r in range(4):
-                nc.sync.dma_start(out=gs[1][r:128:32, :].bitcast(I32), in_=gs[0][4 + r : 128 : 32, :].bitcast(I32))
+                nc.sync.dma_start(
+                    out=tiles["gs1"][r:128:32, :].bitcast(I32), in_=tiles["gs0"][4 + r : 128 : 32, :].bitcast(I32)
+                )
 
-        acc, act, hid, turned = {}, {}, {}, {}
+        acc, turned = {}, {}
 
-        def mm(half, m, s):
+        def mm(half, m, s, start=None, stop=None):
             e = half // 2
-            slots = slice(128 * half, 128 * (half + 1))
-            if s == 0:
-                acc[half, m] = psum.tile([P, H], F32, name=f"bank{half}")
-            if m == 0:
-                w, ws = w1[s][e // 2][:, e % 2, :], w1s[:, PASSES * e + s, :]
-            else:
-                w, ws = w3[e][:, s, :], w3s[e // 2][:, PASSES * (e % 2) + s, :]
+            slots = slice(128 * (half % 4), 128 * (half % 4 + 1))
+            first = (half, m) not in acc
+            if first:
+                acc[half, m] = [psum.tile([P, H], F32, name=f"bank{(A_BANKS, B_BANKS)[m][half]}"), 0]
+            acc[half, m][1] = acc[half, m][1] + 1
             nc.tensor.matmul_mx(
-                out=acc[half, m][:],
-                lhsT=gw[s][:, slots].bitcast(FP8X4),
-                lhsT_scale=gs[s][:, slots],
-                rhs=w.bitcast(FP4X4),
-                rhs_scale=ws,
-                start=(s == 0),
-                stop=(s == 2),
+                out=acc[half, m][0][:],
+                lhsT=tiles[f"gw{s}_{half // 4}"][:, slots].bitcast(FP8X4),
+                lhsT_scale=tiles[f"gs{s}"][:, 128 * half : 128 * (half + 1)],
+                rhs=where_w[m, e, s].bitcast(FP4X4),
+                rhs_scale=where_s[m, e, s],
+                start=first,
+                stop=acc[half, m][1] == PASSES,
             )
 
         def relu(half):
-            act[half] = keep.tile([P, H], F32, name=f"ra{half}", align_bytes=64)
             nc.scalar.activation(
-                act[half][:].rearrange("m (u p d) -> m u p d", u=2, d=2),
-                acc[half, 0][:].rearrange("m (p u d) -> m u p d", u=2, d=2),
+                sb(f"ra{half}", [P, H], F32)[:].rearrange("m (u p d) -> m u p d", u=2, d=2),
+                acc[half, 0][0][:].rearrange("m (p u d) -> m u p d", u=2, d=2),
                 RELU,
             )
 
         def mul(half):
-            hid[half] = keep.tile([P, H], BF16, name=f"h{half}", align_bytes=64)
             nc.vector.tensor_tensor(
-                hid[half][:].rearrange("m (u p d) -> m u p d", u=2, d=2),
-                acc[half, 1][:].rearrange("m (p u d) -> m u p d", u=2, d=2),
-                act[half][:].rearrange("m (u p d) -> m u p d", u=2, d=2),
+                sb(f"h{half}", [P, H], BF16)[:].rearrange("m (u p d) -> m u p d", u=2, d=2),
+                acc[half, 1][0][:].rearrange("m (p u d) -> m u p d", u=2, d=2),
+                tiles[f"ra{half}"][:].rearrange("m (u p d) -> m u p d", u=2, d=2),
                 MULT,
             )
 
-        def turn_bank(half):
+        def tr(half):
             lead = half if half in TURN_BANKS else half - 1
             if lead not in turned:
                 turned[lead] = psum.tile([P, H], F32, name=f"bank{TURN_BANKS[lead]}")
-            return turned[lead], 256 * (half - lead)
-
-        def tr(half):
-            bank, first = turn_bank(half)
-            words = hid[half][:].bitcast(F32)
+            first = 256 * (half - lead)
+            words = tiles[f"h{half}"][:].bitcast(F32)
             for u in range(2):
-                nc.tensor.transpose(bank[:, first + 128 * u : first + 128 * (u + 1)], words[:, 128 * u : 128 * (u + 1)], ident[:])
-
-        def second(half, count):
-            bank, first = turn_bank(half)
-            width = 128 * count
-            hb = keep.tile([P, 4 * 256], BF16, name=f"hb{half}", align_bytes=64)
-            hs = keep.tile([P, 256], U8, name=f"hs{half}", align_bytes=64)
-            codes = []
-
-            def tcp():
-                nc.scalar.copy(
-                    hb[:, 0 : 4 * width].bitcast(F32).rearrange("p (g r u) -> p g r u", g=count, u=2),
-                    bank[:, 0 : 2 * width].rearrange("p (g u r) -> p g r u", g=count, u=2),
+                nc.tensor.transpose(
+                    turned[lead][:, first + 128 * u : first + 128 * (u + 1)], words[:, 128 * u : 128 * (u + 1)], ident[:]
                 )
 
-            def hq():
-                hw = keep.tile([P, 256], U32, name=f"ra{half + 4}" if half < 4 else f"hw{half}", align_bytes=64)
-                codes.append(hw)
-                nc.vector.quantize_mx(out=hw[:, 0:width].bitcast(FP8X4), scales=hs[:, 0:width], in_=hb[:, 0 : 4 * width])
+        def groups(lead):
+            return 1 if lead + 1 in TURN_BANKS or lead == 7 else 2
 
-            def m2():
-                nc.tensor.matmul_mx(
-                    out=bank[:, 0:width],
-                    lhsT=w2[:, half // 2, :].bitcast(FP4X4),
-                    lhsT_scale=w2s[:, half // 2, :],
-                    rhs=codes[0][:, 0:width].bitcast(FP8X4),
-                    rhs_scale=hs[:, 0:width],
-                    start=True,
-                    stop=True,
-                )
+        def tcp(lead):
+            count = groups(lead)
+            nc.scalar.copy(
+                sb(f"hb{lead}", [P, 512 * count], BF16)[:].bitcast(F32).rearrange("p (g r u) -> p g r u", g=count, u=2),
+                turned[lead][:, 0 : 256 * count].rearrange("p (g u r) -> p g r u", g=count, u=2),
+            )
 
-            def ycp():
-                nc.scalar.copy(y[:, 128 * half : 128 * half + width], bank[:, 0:width])
+        def hq(lead):
+            width = 128 * groups(lead)
+            nc.vector.quantize_mx(
+                out=sb(f"hw{lead}", [P, width], U32)[:].bitcast(FP8X4), scales=sb(f"hs{lead}", [P, width], U8)[:], in_=tiles[f"hb{lead}"][:]
+            )
 
-            return tcp, hq, m2, ycp
+        def m2(lead):
+            width = 128 * groups(lead)
+            nc.tensor.matmul_mx(
+                out=turned[lead][:, 0:width],
+                lhsT=tiles["w2"][:, lead // 2, :].bitcast(FP4X4),
+                lhsT_scale=tiles["w2s"][:, lead // 2, :],
+                rhs=tiles[f"hw{lead}"][:].bitcast(FP8X4),
+                rhs_scale=tiles[f"hs{lead}"][:],
+                start=True,
+                stop=True,
+            )
 
-        for k in range(2):
-            prepare(0, k)
-            quantise(0, k)
-        g_words(0, 0, 512)
-        g_words(0, 512, 1024)
-        prepare(1, 0)
-        quantise(1, 1)
-        quantise(1, 0)
-        g_bytes(0, 0, 512)
-        g_bytes(0, 512, 1024)
-        move_bytes()
-        g_words(1, 0, 512)
-        g_words(1, 512, 1024)
+        def ycp(lead):
+            width = 128 * groups(lead)
+            nc.scalar.copy(y[:, 128 * lead : 128 * lead + width], turned[lead][:, 0:width])
 
-        load_w1(2, 0)
-        load_w1(1, 1)
-        load_scales(w3s[0], w3_scales, 0, 2)
-        load_w3(0)
-        load_w3(1)
-        load_w1(2, 1)
-        load_scales(w3s[1], w3_scales, 2, 4)
-        load_w3(2)
-        load_scales(w2s, w2_scales, 0, 4)
-        nc.sync.dma_start(out=w2[:].bitcast(I32), in_=w2_words[:, 0].rearrange("e p n -> p e n").bitcast(I32))
-        load_w3(3)
-        nc.sync.dma_start(pos1_t[:], pos1)
-        nc.sync.dma_start(pos2_t[:], pos2)
-        nc.sync.dma_start(out=gates[:], in_=gate.rearrange("r p t -> p r t"))
+        def a_sum(half, passes):
+            for s in passes:
+                mm(half, 0, s)
+            if acc[half, 0][1] == PASSES:
+                relu(half)
 
-        def w3_sum(half):
-            for s in range(PASSES):
+        def b_sum(half, passes=(0, 1, 2)):
+            for s in passes:
                 mm(half, 1, s)
-            mul(half)
 
-        def last_pass(e):
-            for h in (2 * e, 2 * e + 1):
-                mm(h, 0, 2)
-                relu(h)
+        zero("s0_0", [P, 6, H]); zero("s1_0", [P, 6, H]); zero("xs0", [P, T]); zero("xs2", [P, T]); zero("gs1", [P, SLOTS])
+        zero("w2s", [P, E, N]); zero("s0_2", [P, 6, H]); zero("s1_2", [P, 6, H])
+        nc.gpsimd.memset(y[:, SLOTS:], 0.0)
+        make_identity(nc, ident[:])
+        load_x(0, 0); load_x(0, 1)
+        nc.sync.dma_start(offs_t[:], offs)
+        load_x(1, 0)
+        load_scales(0, 0, 2); load_scales(1, 0, 2); load_pass(0, 0, 0, 2); load_pass(1, 0, 0, 2)
+        load_x(2, 0); scale_rows(tiles["w2s"], w2_scales); load_x(2, 1); load_pass(0, 1, 0, 2); load_pass(1, 1, 0, 2)
+        prepare(0, 0); prepare(0, 1); quantise(0, 0); quantise(0, 1)
+        gather("w", 0, 0, 512); gather("w", 0, 512, 1024)
+        prepare(1, 0); quantise(1, 1); quantise(1, 0)
+        gather("s", 0, 0, 512); gather("s", 0, 512, 1024); move_bytes(); gather("w", 1, 0, 512)
+        load_pass(0, 2, 0, 2); load_pass(1, 2, 0, 2); load_scales(0, 2, 4); load_scales(1, 2, 4); load_expert(0, 2); load_expert(0, 3); load_expert(1, 2); load_expert(1, 3); load_w2(); load_pos(); load_gates()
+        for s in range(2):
+            for h in range(4):
+                a_sum(h, (s,))
+            for h in range(4):
+                b_sum(h, (s,))
+        prepare(2, 0); prepare(2, 1); quantise(2, 0); quantise(2, 1)
+        for e in range(2):
+            gather("s", 2, 256 * e, 256 * (e + 1)); gather("w", 2, 256 * e, 256 * (e + 1))
+            a_sum(2 * e, (2,)); a_sum(2 * e + 1, (2,)); b_sum(2 * e, (2,)); b_sum(2 * e + 1, (2,))
+        for e in range(2, 4):
+            gather("w", 1, 256 * e, 256 * (e + 1)); gather("s", 2, 256 * e, 256 * (e + 1)); gather("w", 2, 256 * e, 256 * (e + 1))
+        mul(0); mul(1); mul(2); mul(3)
+        a_sum(4, (0, 1)); a_sum(5, (0, 1)); a_sum(6, (0,)); a_sum(7, (0,)); a_sum(4, (2,)); a_sum(5, (2,)); a_sum(6, (1,)); a_sum(7, (1,)); b_sum(4); a_sum(6, (2,)); a_sum(7, (2,)); b_sum(5)
+        tr(0); tr(1); tcp(0); mul(4); tr(2); tr(3); tcp(2); mul(5); hq(0); b_sum(6); mul(6); hq(2); b_sum(7); m2(0); m2(2); mul(7); ycp(0)
+        tr(4); tr(5); tcp(4); tr(6); tcp(6); ycp(2); hq(4); tr(7); tcp(7); hq(6); hq(7); m2(4); m2(6); m2(7); ycp(4); ycp(6); ycp(7)
 
-        for h in range(8):
-            mm(h, 0, 0)
-        for h in range(4):
-            mm(h, 0, 1)
-        for k in range(2):
-            prepare(2, k)
-        for k in range(2):
-            quantise(2, k)
-        for e in range(E):
-            g_bytes(2, 256 * e, 256 * (e + 1))
-            g_words(2, 256 * e, 256 * (e + 1))
-        last_pass(0)
-        for h in range(4, 8):
-            mm(h, 0, 1)
-        last_pass(1)
-        w3_sum(0)
-        w3_sum(1)
-        last_pass(2)
-        w3_sum(2)
-        last_pass(3)
-        w3_sum(3)
-        steps = {}
-        for e in range(3):
-            tr(2 * e)
-            tr(2 * e + 1)
-            steps[e] = second(2 * e, 2)
-            steps[e][0]()
-            if e > 0:
-                for step in steps[e - 1][2:]:
-                    step()
-            if e < 2:
-                w3_sum(2 * e + 4)
-                steps[e][1]()
-                w3_sum(2 * e + 5)
-        steps[2][1]()
-        last = [steps[2][2:]]
-        for h in (6, 7):
-            tr(h)
-            tcp, hq, m2, ycp = second(h, 1)
-            tcp()
-            hq()
-            last.append((m2, ycp))
-        for m2, ycp in last:
-            m2()
-            ycp()
-
+        gates = tiles["gates"]
         t1 = keep.tile([P, T], F32, name="t1")
         t2 = keep.tile([P, T], F32, name="t2")
         o = keep.tile([P, T], F32, name="o")

@@ -24,11 +24,13 @@ P = 128
 PASSES = K // 512
 SLOTS = E * C
 HALVES = ((0, 512), (512, 768))
-X_PIECES = (((0, 512, 352), (512, 768, 128)), ((0, 768, 384),), ((0, 512, 64), (512, 768, 128)))
-A_BANKS = (0, 1, 2, 3, 0, 1, 2, 3)
-B_BANKS = (4, 5, 6, 7, 0, 1, 4, 5)
-TURN_BANKS = {0: 2, 2: 3, 4: 6, 6: 7, 7: 0}
-HOLD = {"gw1_1": "xb2_1", "hw0": "ra5", "hw2": "ra6"}
+LIVE = 100
+X_PIECES = (((0, 768, 512),), ((0, 768, 448),), ((0, 768, 0),))
+PLANES = (("xs0", 0), ("xs0", 4), ("xs2", 0))
+A_BANKS = (0, 2, 4, 6, 0, 2, 4, 6)
+B_BANKS = (1, 3, 5, 7, 1, 3, 5, 7)
+TURN_BANKS = {0: 0, 2: 2, 4: 4, 6: 6, 7: 1}
+HOLD = {"gw0_6": "xf2_0", "gw1_4": "xb2_0"}
 
 
 def tile_moe_cap2_glu_relu_kernel(
@@ -74,14 +76,14 @@ def tile_moe_cap2_glu_relu_kernel(
             for s in range(s0, s1):
                 where_w[m, e, s] = tile[:, s - s0, :]
 
-        def scale_rows(tile, dram):
+        def scale_rows(queue, tile, dram):
             rows = dram.rearrange("e s (q r) n -> r q (e s) n", r=4)
             for r in range(4):
-                nc.sync.dma_start(out=tile[r:128:32, :, :].bitcast(I32), in_=rows[r].bitcast(I32))
+                queue.dma_start(out=tile[r:128:32, :, :].bitcast(I32), in_=rows[r].bitcast(I32))
 
-        def load_scales(m, e0, e1):
+        def load_scales(queue, m, e0, e1):
             tile = tiles[f"s{m}_{e0}"]
-            scale_rows(tile, scales_dram[m][e0:e1])
+            scale_rows(queue, tile, scales_dram[m][e0:e1])
             for e in range(e0, e1):
                 for s in range(PASSES):
                     where_s[m, e, s] = tile[:, PASSES * (e - e0) + s, :]
@@ -104,77 +106,99 @@ def tile_moe_cap2_glu_relu_kernel(
         def prepare(s, k):
             c0, c1, share = X_PIECES[s][k]
             cuts = sorted({0, share, c1 - c0} | ({512 - c0} if c0 < 512 < c1 else set()))
-            for a, b in zip(cuts, cuts[1:]):
-                engine = "vector" if b <= share else "scalar"
+            for a, b in sorted(zip(cuts, cuts[1:]), reverse=True):
                 part = (c0 + a) // 512
                 dst = xb(s, part)[:, 4 * (c0 + a - 512 * part) : 4 * (c0 + b - 512 * part)].rearrange("p (c i j) -> p c j i", i=4, j=4)
                 src = tiles[f"xf{s}_{k}"][:, :, a:b].rearrange("p j (c i) -> p c j i", i=4)
-                if engine == "vector":
+                if b <= share:
                     nc.vector.tensor_copy(dst, src)
                 else:
                     nc.scalar.activation(dst, src, COPY)
 
         def quantise(s, part):
             c0, c1 = HALVES[part]
-            plane = (tiles["xs0"][:, c0:c1], tiles["xs0"][4:128, c0:c1], tiles["xs2"][:, c0:c1])[s]
-            nc.vector.quantize_mx(out=sb(f"xw{s}", [P, T], U32)[:, c0:c1].bitcast(FP8X4), scales=plane, in_=xb(s, part)[:])
+            name, row = PLANES[s]
+            nc.vector.quantize_mx(out=sb(f"xw{s}", [P, T], U32)[:, c0:c1].bitcast(FP8X4), scales=tiles[name][row:128, c0:c1], in_=xb(s, part)[:])
 
-        def gather(sort, s, start, stop):
-            pair = start // 512
-            if sort == "s":
-                tile, first = sb(f"gs{s}", [P, SLOTS], U8), 0
-            else:
-                tile, first = sb(f"gw{s}_{pair}", [P, 512], U32), 512 * pair
-            nc.vector.tensor_copy(
-                tile[:, start - first : stop - first], tiles[f"x{sort}{s}"][:].indirect(offs_t[:, start // 16 : stop // 16])
-            )
+        slot_w, slot_s = {}, {}
 
-        def move_bytes():
-            for r in range(4):
-                nc.sync.dma_start(
-                    out=tiles["gs1"][r:128:32, :].bitcast(I32), in_=tiles["gs0"][4 + r : 128 : 32, :].bitcast(I32)
-                )
+        def gather_words(s, g0, g1):
+            tile = sb(f"gw{s}_{g0}", [P, 128 * (g1 - g0)], U32)
+            nc.vector.tensor_copy(tile[:], tiles[f"xw{s}"][:].indirect(offs_t[:, 8 * g0 : 8 * g1]))
+            for g in range(g0, g1):
+                slot_w[s, g] = tile[:, 128 * (g - g0) : 128 * (g - g0 + 1)]
+
+        def gather_bytes(name, g0, g1):
+            tile = sb(f"g{name}_{g0}", [P, 128 * (g1 - g0)], U8)
+            nc.vector.tensor_copy(tile[:], tiles[name][:].indirect(offs_t[:, 8 * g0 : 8 * g1]))
+            for s in range(PASSES):
+                if PLANES[s] == (name, 0):
+                    for g in range(g0, g1):
+                        slot_s[s, g] = tile[:, 128 * (g - g0) : 128 * (g - g0 + 1)]
+
+        def move_bytes(queue, s, g0, g1):
+            name, row = PLANES[s]
+            plane = tiles[f"moved{s}_{g0}"]
+            queue.dma_start(out=plane[0:LIVE, :].bitcast(I32), in_=tiles[f"g{name}_{g0}"][row : row + LIVE, :].bitcast(I32))
+            for g in range(g0, g1):
+                slot_s[s, g] = plane[:, 128 * (g - g0) : 128 * (g - g0 + 1)]
+
+        def move_rows(queue, s, g0, g1, rows=range(4)):
+            name, row = PLANES[s]
+            plane = tiles[f"moved{s}_{g0}"]
+            for r in rows:
+                queue.dma_start(out=plane[r:128:32, :].bitcast(I32), in_=tiles[f"g{name}_{g0}"][row + r : 128 : 32, :].bitcast(I32))
+            for g in range(g0, g1):
+                slot_s[s, g] = plane[:, 128 * (g - g0) : 128 * (g - g0 + 1)]
 
         acc, turned = {}, {}
 
-        def mm(half, m, s, start=None, stop=None):
-            e = half // 2
-            slots = slice(128 * (half % 4), 128 * (half % 4 + 1))
-            first = (half, m) not in acc
+        def mm(g, m, s):
+            e = g // 2
+            first = (g, m) not in acc
             if first:
-                acc[half, m] = [psum.tile([P, H], F32, name=f"bank{(A_BANKS, B_BANKS)[m][half]}"), 0]
-            acc[half, m][1] = acc[half, m][1] + 1
+                acc[g, m] = [psum.tile([P, H], F32, name=f"bank{(A_BANKS, B_BANKS)[m][g]}"), 0]
+            acc[g, m][1] = acc[g, m][1] + 1
             nc.tensor.matmul_mx(
-                out=acc[half, m][0][:],
-                lhsT=tiles[f"gw{s}_{half // 4}"][:, slots].bitcast(FP8X4),
-                lhsT_scale=tiles[f"gs{s}"][:, 128 * half : 128 * (half + 1)],
+                out=acc[g, m][0][:],
+                lhsT=slot_w[s, g].bitcast(FP8X4),
+                lhsT_scale=slot_s[s, g],
                 rhs=where_w[m, e, s].bitcast(FP4X4),
                 rhs_scale=where_s[m, e, s],
                 start=first,
-                stop=acc[half, m][1] == PASSES,
+                stop=acc[g, m][1] == PASSES,
             )
+            if m == 0 and acc[g, m][1] == PASSES:
+                relu(g)
 
-        def relu(half):
+        def relu(g):
             nc.scalar.activation(
-                sb(f"ra{half}", [P, H], F32)[:].rearrange("m (u p d) -> m u p d", u=2, d=2),
-                acc[half, 0][0][:].rearrange("m (p u d) -> m u p d", u=2, d=2),
+                sb(f"ra{g}", [P, H], F32)[:].rearrange("m (u p d) -> m u p d", u=2, d=2),
+                acc[g, 0][0][:].rearrange("m (p u d) -> m u p d", u=2, d=2),
                 RELU,
             )
 
-        def mul(half):
+        def mul(g):
             nc.vector.tensor_tensor(
-                sb(f"h{half}", [P, H], BF16)[:].rearrange("m (u p d) -> m u p d", u=2, d=2),
-                acc[half, 1][0][:].rearrange("m (p u d) -> m u p d", u=2, d=2),
-                tiles[f"ra{half}"][:].rearrange("m (u p d) -> m u p d", u=2, d=2),
+                sb(f"h{g}", [P, H], BF16)[:].rearrange("m (u p d) -> m u p d", u=2, d=2),
+                acc[g, 1][0][:].rearrange("m (p u d) -> m u p d", u=2, d=2),
+                tiles[f"ra{g}"][:].rearrange("m (u p d) -> m u p d", u=2, d=2),
                 MULT,
             )
 
-        def tr(half):
-            lead = half if half in TURN_BANKS else half - 1
+        def mul_pool(g):
+            nc.scalar.copy(
+                sb(f"rb{g}", [P, H], F32)[:].rearrange("m (u p d) -> m u p d", u=2, d=2),
+                acc[g, 1][0][:].rearrange("m (p u d) -> m u p d", u=2, d=2),
+            )
+            nc.gpsimd.tensor_tensor(sb(f"h{g}", [P, H], BF16)[:], tiles[f"rb{g}"][:], tiles[f"ra{g}"][:], MULT)
+
+        def tr(g):
+            lead = g if g in TURN_BANKS else g - 1
             if lead not in turned:
                 turned[lead] = psum.tile([P, H], F32, name=f"bank{TURN_BANKS[lead]}")
-            first = 256 * (half - lead)
-            words = tiles[f"h{half}"][:].bitcast(F32)
+            first = 256 * (g - lead)
+            words = tiles[f"h{g}"][:].bitcast(F32)
             for u in range(2):
                 nc.tensor.transpose(
                     turned[lead][:, first + 128 * u : first + 128 * (u + 1)], words[:, 128 * u : 128 * (u + 1)], ident[:]
@@ -212,53 +236,48 @@ def tile_moe_cap2_glu_relu_kernel(
             width = 128 * groups(lead)
             nc.scalar.copy(y[:, 128 * lead : 128 * lead + width], turned[lead][:, 0:width])
 
-        def a_sum(half, passes):
-            for s in passes:
-                mm(half, 0, s)
-            if acc[half, 0][1] == PASSES:
-                relu(half)
+        def sums(gs, ms, passes):
+            for g in gs:
+                for m in ms:
+                    for s in passes:
+                        mm(g, m, s)
 
-        def b_sum(half, passes=(0, 1, 2)):
-            for s in passes:
-                mm(half, 1, s)
+        def tail(cuts):
+            gates = tiles["gates"]
+            for c0, c1 in zip(cuts, cuts[1:]):
+                t1 = keep.tile([P, c1 - c0], F32, name=f"t1_{c0}")
+                t2 = keep.tile([P, c1 - c0], F32, name=f"t2_{c0}")
+                o = keep.tile([P, c1 - c0], F32, name=f"o_{c0}")
+                nc.vector.tensor_tensor(t1[:], y[:].indirect(pos1_t[:, c0 // 16 : c1 // 16]), gates[:, 0, c0:c1], MULT)
+                nc.vector.tensor_tensor(t2[:], y[:].indirect(pos2_t[:, c0 // 16 : c1 // 16]), gates[:, 1, c0:c1], MULT)
+                nc.vector.tensor_tensor(o[:], t1[:], t2[:], ADD)
+                nc.sync.dma_start(out=out[:, c0:c1], in_=o[:])
 
-        zero("s0_0", [P, 6, H]); zero("s1_0", [P, 6, H]); zero("xs0", [P, T]); zero("xs2", [P, T]); zero("gs1", [P, SLOTS])
+        zero("s0_0", [P, 6, H]); zero("s1_0", [P, 6, H]); zero("xs0", [P, T]); zero("xs2", [P, T])
+        zero("moved1_0", [P, 512]); zero("moved1_4", [P, 512])
         zero("w2s", [P, E, N]); zero("s0_2", [P, 6, H]); zero("s1_2", [P, 6, H])
         nc.gpsimd.memset(y[:, SLOTS:], 0.0)
         make_identity(nc, ident[:])
-        load_x(0, 0); load_x(0, 1)
-        nc.sync.dma_start(offs_t[:], offs)
-        load_x(1, 0)
-        load_scales(0, 0, 2); load_scales(1, 0, 2); load_pass(0, 0, 0, 2); load_pass(1, 0, 0, 2)
-        load_x(2, 0); scale_rows(tiles["w2s"], w2_scales); load_x(2, 1); load_pass(0, 1, 0, 2); load_pass(1, 1, 0, 2)
-        prepare(0, 0); prepare(0, 1); quantise(0, 0); quantise(0, 1)
-        gather("w", 0, 0, 512); gather("w", 0, 512, 1024)
+        load_x(0, 0); nc.sync.dma_start(offs_t[:], offs); load_x(1, 0); load_x(2, 0)
+        load_scales(nc.sync, 0, 0, 2); load_pass(0, 0, 0, 2); load_scales(nc.sync, 1, 0, 2); load_pass(1, 0, 0, 2); load_pass(0, 1, 0, 2)
+        prepare(0, 0); quantise(0, 1); quantise(0, 0)
+        gather_words(0, 0, 4); gather_words(0, 4, 6)
         prepare(1, 0); quantise(1, 1); quantise(1, 0)
-        gather("s", 0, 0, 512); gather("s", 0, 512, 1024); move_bytes(); gather("w", 1, 0, 512)
-        load_pass(0, 2, 0, 2); load_pass(1, 2, 0, 2); load_scales(0, 2, 4); load_scales(1, 2, 4); load_expert(0, 2); load_expert(0, 3); load_expert(1, 2); load_expert(1, 3); load_w2(); load_pos(); load_gates()
-        for s in range(2):
-            for h in range(4):
-                a_sum(h, (s,))
-            for h in range(4):
-                b_sum(h, (s,))
-        prepare(2, 0); prepare(2, 1); quantise(2, 0); quantise(2, 1)
-        for e in range(2):
-            gather("s", 2, 256 * e, 256 * (e + 1)); gather("w", 2, 256 * e, 256 * (e + 1))
-            a_sum(2 * e, (2,)); a_sum(2 * e + 1, (2,)); b_sum(2 * e, (2,)); b_sum(2 * e + 1, (2,))
-        for e in range(2, 4):
-            gather("w", 1, 256 * e, 256 * (e + 1)); gather("s", 2, 256 * e, 256 * (e + 1)); gather("w", 2, 256 * e, 256 * (e + 1))
-        mul(0); mul(1); mul(2); mul(3)
-        a_sum(4, (0, 1)); a_sum(5, (0, 1)); a_sum(6, (0,)); a_sum(7, (0,)); a_sum(4, (2,)); a_sum(5, (2,)); a_sum(6, (1,)); a_sum(7, (1,)); b_sum(4); a_sum(6, (2,)); a_sum(7, (2,)); b_sum(5)
-        tr(0); tr(1); tcp(0); mul(4); tr(2); tr(3); tcp(2); mul(5); hq(0); b_sum(6); mul(6); hq(2); b_sum(7); m2(0); m2(2); mul(7); ycp(0)
-        tr(4); tr(5); tcp(4); tr(6); tcp(6); ycp(2); hq(4); tr(7); tcp(7); hq(6); hq(7); m2(4); m2(6); m2(7); ycp(4); ycp(6); ycp(7)
-
-        gates = tiles["gates"]
-        t1 = keep.tile([P, T], F32, name="t1")
-        t2 = keep.tile([P, T], F32, name="t2")
-        o = keep.tile([P, T], F32, name="o")
-        nc.vector.tensor_tensor(t1[:], y[:].indirect(pos1_t[:]), gates[:, 0, :], MULT)
-        nc.vector.tensor_tensor(t2[:], y[:].indirect(pos2_t[:]), gates[:, 1, :], MULT)
-        for c in range(2):
-            cols = slice(384 * c, 384 * (c + 1))
-            nc.vector.tensor_tensor(o[:, cols], t1[:, cols], t2[:, cols], ADD)
-            nc.sync.dma_start(out=out[:, cols], in_=o[:, cols])
+        gather_bytes("xs0", 0, 4); move_rows(nc.sync, 1, 0, 4); gather_words(1, 0, 4); gather_bytes("xs0", 4, 8)
+        load_pass(1, 1, 0, 2); load_pass(0, 2, 0, 2); load_pass(1, 2, 0, 2)
+        prepare(2, 0); quantise(2, 1); quantise(2, 0); gather_words(0, 6, 8)
+        gather_bytes("xs2", 0, 2); gather_words(2, 0, 2); gather_bytes("xs2", 2, 4); gather_words(2, 2, 4)
+        load_scales(nc.sync, 0, 2, 4); load_pass(0, 0, 2, 4); move_rows(nc.sync, 1, 4, 8); load_pass(0, 1, 2, 4); load_pass(0, 2, 2, 4)
+        load_scales(nc.sync, 1, 2, 4); load_expert(1, 2); load_expert(1, 3); load_w2(); scale_rows(nc.sync, tiles["w2s"], w2_scales); load_pos(); load_gates()
+        sums(range(4), (0,), (0,)); sums(range(4), (1,), (0,)); sums(range(4), (0,), (1,)); sums(range(4), (1,), (1,))
+        sums(range(4), (0, 1), (2,))
+        gather_words(1, 4, 8)
+        gather_bytes("xs2", 4, 6); gather_words(2, 4, 6)
+        gather_bytes("xs2", 6, 8); gather_words(2, 6, 8); mul(0); mul(1); mul(2); mul(3)
+        sums(range(4, 8), (0,), (0,)); sums(range(4, 8), (0,), (1,)); sums(range(4, 8), (0,), (2,))
+        sums((4,), (1,), (0, 1, 2)); mul(4); sums((5,), (1,), (0, 1, 2)); mul(5)
+        tr(0); tr(1); tcp(0); tr(2); tr(3); tcp(2); hq(0)
+        sums((6,), (1,), (0, 1, 2)); mul(6); hq(2)
+        sums((7,), (1,), (0, 1, 2)); mul(7)
+        tr(4); tr(5); tcp(4); tr(6); tcp(6); m2(0); m2(2); tr(7); tcp(7); hq(4); hq(6); hq(7); ycp(0); ycp(2); m2(4); m2(6); m2(7); ycp(4); ycp(6); ycp(7)
+        tail((0, 512, 768))

@@ -30,7 +30,7 @@ PLANES = (("xs0", 0), ("xs0", 4), ("xs2", 0))
 A_BANKS = (0, 2, 4, 6, 0, 2, 4, 6)
 B_BANKS = (1, 3, 5, 7, 1, 3, 5, 7)
 TURN_BANKS = {0: 0, 2: 2, 4: 4, 6: 6, 7: 1}
-HOLD = {"gw0_6": "xf2_0", "gw1_4": "xb2_0"}
+HOLD = {"gw0_6": "xf2_0", "gw1_4": "xb2_0", "hw2": "ra7"}
 
 
 def tile_moe_cap2_glu_relu_kernel(
@@ -136,6 +136,14 @@ def tile_moe_cap2_glu_relu_kernel(
                     for g in range(g0, g1):
                         slot_s[s, g] = tile[:, 128 * (g - g0) : 128 * (g - g0 + 1)]
 
+        def gather_bytes_in_two(name, g0, g1):
+            tile = sb(f"g{name}_{g0}", [P, 128 * (g1 - g0)], U8)
+            mid = (g0 + g1) // 2
+            for a, b in ((g0, mid), (mid, g1)):
+                nc.vector.tensor_copy(tile[:, 128 * (a - g0) : 128 * (b - g0)], tiles[name][:].indirect(offs_t[:, 8 * a : 8 * b]))
+            for g in range(g0, g1):
+                slot_s[0, g] = tile[:, 128 * (g - g0) : 128 * (g - g0 + 1)]
+
         def move_bytes(queue, s, g0, g1):
             name, row = PLANES[s]
             plane = tiles[f"moved{s}_{g0}"]
@@ -186,6 +194,18 @@ def tile_moe_cap2_glu_relu_kernel(
                 MULT,
             )
 
+        def mul_turn(g):
+            turned[g] = psum.tile([P, H], F32, name=f"bank{TURN_BANKS[g]}")
+            h = sb(f"h{g}", [P, H], BF16)
+            for u in range(2):
+                nc.vector.tensor_tensor(
+                    h[:, 256 * u : 256 * (u + 1)].rearrange("m (p d) -> m p d", d=2),
+                    acc[g, 1][0][:].rearrange("m (p u d) -> m u p d", u=2, d=2)[:, u],
+                    tiles[f"ra{g}"][:, 256 * u : 256 * (u + 1)].rearrange("m (p d) -> m p d", d=2),
+                    MULT,
+                )
+                nc.tensor.transpose(turned[g][:, 128 * u : 128 * (u + 1)], h[:].bitcast(F32)[:, 128 * u : 128 * (u + 1)], ident[:])
+
         def mul_pool(g):
             nc.scalar.copy(
                 sb(f"rb{g}", [P, H], F32)[:].rearrange("m (u p d) -> m u p d", u=2, d=2),
@@ -207,9 +227,9 @@ def tile_moe_cap2_glu_relu_kernel(
         def groups(lead):
             return 1 if lead + 1 in TURN_BANKS or lead == 7 else 2
 
-        def tcp(lead):
+        def tcp(lead, copy=nc.scalar.copy):
             count = groups(lead)
-            nc.scalar.copy(
+            copy(
                 sb(f"hb{lead}", [P, 512 * count], BF16)[:].bitcast(F32).rearrange("p (g r u) -> p g r u", g=count, u=2),
                 turned[lead][:, 0 : 256 * count].rearrange("p (g u r) -> p g r u", g=count, u=2),
             )
@@ -232,9 +252,9 @@ def tile_moe_cap2_glu_relu_kernel(
                 stop=True,
             )
 
-        def ycp(lead):
+        def ycp(lead, copy=nc.scalar.copy):
             width = 128 * groups(lead)
-            nc.scalar.copy(y[:, 128 * lead : 128 * lead + width], turned[lead][:, 0:width])
+            copy(y[:, 128 * lead : 128 * lead + width], turned[lead][:, 0:width])
 
         def sums(gs, ms, passes):
             for g in gs:
@@ -259,15 +279,15 @@ def tile_moe_cap2_glu_relu_kernel(
         nc.gpsimd.memset(y[:, SLOTS:], 0.0)
         make_identity(nc, ident[:])
         load_x(0, 0); nc.sync.dma_start(offs_t[:], offs); load_x(1, 0); load_x(2, 0)
-        load_scales(nc.sync, 0, 0, 2); load_pass(0, 0, 0, 2); load_scales(nc.sync, 1, 0, 2); load_pass(1, 0, 0, 2); load_pass(0, 1, 0, 2)
+        load_scales(nc.sync, 0, 0, 2); load_pass(0, 0, 0, 1); load_pass(0, 0, 1, 2); load_scales(nc.sync, 1, 0, 2); load_pass(1, 0, 0, 2); load_pass(0, 1, 0, 2)
         prepare(0, 0); quantise(0, 1); quantise(0, 0)
         gather_words(0, 0, 4); gather_words(0, 4, 6)
         prepare(1, 0); quantise(1, 1); quantise(1, 0)
-        gather_bytes("xs0", 0, 4); move_rows(nc.sync, 1, 0, 4); gather_words(1, 0, 4); gather_bytes("xs0", 4, 8)
+        gather_bytes_in_two("xs0", 0, 4); move_rows(nc.sync, 1, 0, 4); gather_words(1, 0, 4); gather_bytes("xs0", 4, 8)
         load_pass(1, 1, 0, 2); load_pass(0, 2, 0, 2); load_pass(1, 2, 0, 2)
         prepare(2, 0); quantise(2, 1); quantise(2, 0); gather_words(0, 6, 8)
         gather_bytes("xs2", 0, 2); gather_words(2, 0, 2); gather_bytes("xs2", 2, 4); gather_words(2, 2, 4)
-        load_scales(nc.sync, 0, 2, 4); load_pass(0, 0, 2, 4); move_rows(nc.sync, 1, 4, 8); load_pass(0, 1, 2, 4); load_pass(0, 2, 2, 4)
+        load_scales(nc.sync, 0, 2, 4); load_pass(0, 0, 2, 4); move_rows(nc.sync, 1, 4, 8, (0, 1)); load_pass(0, 1, 2, 4); move_rows(nc.sync, 1, 4, 8, (2, 3)); load_pass(0, 2, 2, 4)
         load_scales(nc.sync, 1, 2, 4); load_expert(1, 2); load_expert(1, 3); load_w2(); scale_rows(nc.sync, tiles["w2s"], w2_scales); load_pos(); load_gates()
         sums(range(4), (0,), (0,)); sums(range(4), (1,), (0,)); sums(range(4), (0,), (1,)); sums(range(4), (1,), (1,))
         sums(range(4), (0, 1), (2,))
@@ -277,7 +297,7 @@ def tile_moe_cap2_glu_relu_kernel(
         sums(range(4, 8), (0,), (0,)); sums(range(4, 8), (0,), (1,)); sums(range(4, 8), (0,), (2,))
         sums((4,), (1,), (0, 1, 2)); mul(4); sums((5,), (1,), (0, 1, 2)); mul(5)
         tr(0); tr(1); tcp(0); tr(2); tr(3); tcp(2); hq(0)
-        sums((6,), (1,), (0, 1, 2)); mul(6); hq(2)
-        sums((7,), (1,), (0, 1, 2)); mul(7)
-        tr(4); tr(5); tcp(4); tr(6); tcp(6); m2(0); m2(2); tr(7); tcp(7); hq(4); hq(6); hq(7); ycp(0); ycp(2); m2(4); m2(6); m2(7); ycp(4); ycp(6); ycp(7)
+        sums((6,), (1,), (0, 1, 2)); mul(6)
+        sums((7,), (1,), (0, 1, 2)); mul(7); hq(2)
+        tr(4); tr(5); tcp(4); tr(6); tcp(6); m2(0); tr(7); tcp(7); ycp(0, nc.vector.tensor_copy); m2(2); hq(4); hq(6); hq(7); ycp(2); m2(4); m2(6); m2(7); ycp(4, nc.vector.tensor_copy); ycp(6); ycp(7)
         tail((0, 512, 768))

@@ -30,7 +30,8 @@ PLANES = (("xs0", 0), ("xs0", 4), ("xs2", 0))
 A_BANKS = (0, 2, 4, 6, 0, 2, 4, 6)
 B_BANKS = (1, 3, 5, 7, 1, 3, 5, 7)
 TURN_BANKS = {0: 0, 2: 2, 4: 4, 6: 6, 7: 1}
-HOLD = {"gw0_6": "xf2_0", "gw1_4": "xb2_0", "hw2": "ra7"}
+HOLD = {"rb0": "gw2_2", "rb1": "gxs2_2", "rb2": "w1_p2_0"}
+PLACE = {"xb2_0": 0, "gw0_6": 0, "gw1_4": 1024}
 
 
 def tile_moe_cap2_glu_relu_kernel(
@@ -40,9 +41,12 @@ def tile_moe_cap2_glu_relu_kernel(
     with ExitStack() as ctx:
         keep = ctx.enter_context(tc.tile_pool(name="keep", bufs=1))
         psum = ctx.enter_context(tc.psum_pool(name="psum", bufs=1))
+        shared = ctx.enter_context(tc.tile_pool(name="shared", bufs=1))
         tiles = {}
 
         def sb(name, shape, dtype):
+            if name not in tiles and name in PLACE:
+                tiles[name] = shared.tile(shape, dtype, name=name, offset=PLACE[name], align_bytes=64)
             if name not in tiles:
                 tiles[name] = keep.tile(shape, dtype, name=HOLD.get(name, name), align_bytes=64)
             return tiles[name]
@@ -206,6 +210,18 @@ def tile_moe_cap2_glu_relu_kernel(
                 )
                 nc.tensor.transpose(turned[g][:, 128 * u : 128 * (u + 1)], h[:].bitcast(F32)[:, 128 * u : 128 * (u + 1)], ident[:])
 
+        def stage(g):
+            nc.scalar.copy(
+                sb(f"rb{g}", [P, H], F32)[:].rearrange("m (u p d) -> m u p d", u=2, d=2),
+                acc[g, 1][0][:].rearrange("m (p u d) -> m u p d", u=2, d=2),
+            )
+
+        def mul_staged(g):
+            nc.vector.tensor_tensor(sb(f"h{g}", [P, H], BF16)[:], tiles[f"rb{g}"][:], tiles[f"ra{g}"][:], MULT)
+
+        def mul_on_pool(g):
+            nc.gpsimd.tensor_tensor(sb(f"h{g}", [P, H], BF16)[:], tiles[f"rb{g}"][:], tiles[f"ra{g}"][:], MULT)
+
         def mul_pool(g):
             nc.scalar.copy(
                 sb(f"rb{g}", [P, H], F32)[:].rearrange("m (u p d) -> m u p d", u=2, d=2),
@@ -285,19 +301,18 @@ def tile_moe_cap2_glu_relu_kernel(
         prepare(1, 0); quantise(1, 1); quantise(1, 0)
         gather_bytes_in_two("xs0", 0, 4); move_rows(nc.sync, 1, 0, 4); gather_words(1, 0, 4); gather_bytes("xs0", 4, 8)
         load_pass(1, 1, 0, 2); load_pass(0, 2, 0, 2); load_pass(1, 2, 0, 2)
-        prepare(2, 0); quantise(2, 1); quantise(2, 0); gather_words(0, 6, 8)
-        gather_bytes("xs2", 0, 2); gather_words(2, 0, 2); gather_bytes("xs2", 2, 4); gather_words(2, 2, 4)
-        load_scales(nc.sync, 0, 2, 4); load_pass(0, 0, 2, 4); move_rows(nc.sync, 1, 4, 8, (0, 1)); load_pass(0, 1, 2, 4); move_rows(nc.sync, 1, 4, 8, (2, 3)); load_pass(0, 2, 2, 4)
-        load_scales(nc.sync, 1, 2, 4); load_expert(1, 2); load_expert(1, 3); load_w2(); scale_rows(nc.sync, tiles["w2s"], w2_scales); load_pos(); load_gates()
+        prepare(2, 0); quantise(2, 1); quantise(2, 0)
+        gather_bytes("xs2", 0, 2); gather_words(2, 0, 2); gather_bytes("xs2", 2, 4); gather_words(2, 2, 4); gather_words(0, 6, 8); gather_words(1, 4, 8)
+        load_scales(nc.sync, 0, 2, 4); load_pass(0, 0, 2, 4); move_rows(nc.sync, 1, 4, 8, (0, 1)); load_pass(0, 1, 2, 4); move_rows(nc.sync, 1, 4, 8, (2, 3))
+        load_scales(nc.sync, 1, 2, 4); load_pass(1, 0, 2, 4); load_pass(0, 2, 2, 4); load_pass(1, 1, 2, 4); load_pass(1, 2, 2, 4)
+        load_w2(); scale_rows(nc.sync, tiles["w2s"], w2_scales); load_pos(); load_gates()
         sums(range(4), (0,), (0,)); sums(range(4), (1,), (0,)); sums(range(4), (0,), (1,)); sums(range(4), (1,), (1,))
         sums(range(4), (0, 1), (2,))
-        gather_words(1, 4, 8)
-        gather_bytes("xs2", 4, 6); gather_words(2, 4, 6)
-        gather_bytes("xs2", 6, 8); gather_words(2, 6, 8); mul(0); mul(1); mul(2); mul(3)
-        sums(range(4, 8), (0,), (0,)); sums(range(4, 8), (0,), (1,)); sums(range(4, 8), (0,), (2,))
-        sums((4,), (1,), (0, 1, 2)); mul(4); sums((5,), (1,), (0, 1, 2)); mul(5)
-        tr(0); tr(1); tcp(0); tr(2); tr(3); tcp(2); hq(0)
-        sums((6,), (1,), (0, 1, 2)); mul(6)
-        sums((7,), (1,), (0, 1, 2)); mul(7); hq(2)
-        tr(4); tr(5); tcp(4); tr(6); tcp(6); m2(0); tr(7); tcp(7); ycp(0, nc.vector.tensor_copy); m2(2); hq(4); hq(6); hq(7); ycp(2); m2(4); m2(6); m2(7); ycp(4, nc.vector.tensor_copy); ycp(6); ycp(7)
+        for g in range(4):
+            stage(g)
+        gather_bytes("xs2", 4, 6); gather_words(2, 4, 6); gather_bytes("xs2", 6, 8); gather_words(2, 6, 8)
+        for g in range(4):
+            mul_staged(g)
+        sums(range(4, 8), (0,), (0,)); sums(range(4, 8), (0,), (1,)); sums(range(4, 8), (1,), (0,)); sums(range(4, 8), (0,), (2,))
+        sums((4,), (1,), (1, 2)); mul(4); sums((5,), (1,), (1, 2)); mul(5); sums((6,), (1,), (1, 2)); mul(6); tr(0); tr(1); tcp(0); tr(2); tr(3); tcp(2); sums((7,), (1,), (1, 2)); mul(7); tr(4); tr(5); tcp(4); tr(6); tcp(6); tr(7); tcp(7); hq(0); hq(2); m2(0); m2(2); hq(4); hq(6); hq(7); ycp(0); ycp(2); m2(4); m2(6); m2(7); ycp(4, nc.vector.tensor_copy); ycp(6); ycp(7)
         tail((0, 512, 768))

@@ -46,9 +46,9 @@ def tile_moe_cap2_glu_relu_kernel(
 
         def sb(name, shape, dtype):
             if name not in tiles and name in PLACE:
-                tiles[name] = shared.tile(shape, dtype, name=name, offset=PLACE[name], align_bytes=64)
+                tiles[name] = shared.tile(shape, dtype, name=name, offset=PLACE[name], align_bytes=256)
             if name not in tiles:
-                tiles[name] = keep.tile(shape, dtype, name=HOLD.get(name, name), align_bytes=64)
+                tiles[name] = keep.tile(shape, dtype, name=HOLD.get(name, name), align_bytes=256)
             return tiles[name]
 
         offs_t = keep.tile([P, SLOTS // 16], U16, name="offs_t")

@@ -25,13 +25,13 @@ PASSES = K // 512
 SLOTS = E * C
 HALVES = ((0, 512), (512, 768))
 LIVE = 100
-X_PIECES = (((0, 768, 512),), ((0, 768, 448),), ((0, 768, 0),))
+X_PIECES = (((0, 768, 512),), ((0, 768, 512),), ((0, 768, 0),))
 PLANES = (("xs0", 0), ("xs0", 4), ("xs2", 0))
 A_BANKS = (0, 2, 4, 6, 0, 2, 4, 6)
 B_BANKS = (1, 3, 5, 7, 1, 3, 5, 7)
 TURN_BANKS = {0: 0, 2: 2, 4: 4, 6: 6, 7: 1}
 HOLD = {"rb0": "gw2_2", "rb1": "gxs2_2", "rb2": "w1_p2_0"}
-PLACE = {"xb2_0": 0, "gw0_6": 0, "gw1_4": 1024}
+PLACE = {"xb2_0": 0, "gw0_4": 0, "gw0_6": 1024, "gw1_4": 2048, "gw1_6": 3072}
 
 
 def tile_moe_cap2_glu_relu_kernel(
@@ -297,22 +297,20 @@ def tile_moe_cap2_glu_relu_kernel(
         load_x(0, 0); nc.sync.dma_start(offs_t[:], offs); load_x(1, 0); load_x(2, 0)
         load_scales(nc.sync, 0, 0, 2); load_pass(0, 0, 0, 1); load_pass(0, 0, 1, 2); load_scales(nc.sync, 1, 0, 2); load_pass(1, 0, 0, 2); load_pass(0, 1, 0, 2)
         prepare(0, 0); quantise(0, 1); quantise(0, 0)
-        gather_words(0, 0, 4); gather_words(0, 4, 6)
+        gather_words(0, 0, 4)
         prepare(1, 0); quantise(1, 1); quantise(1, 0)
         gather_bytes_in_two("xs0", 0, 4); move_rows(nc.sync, 1, 0, 4); gather_words(1, 0, 4); gather_bytes("xs0", 4, 8)
         load_pass(1, 1, 0, 2); load_pass(0, 2, 0, 2); load_pass(1, 2, 0, 2)
         prepare(2, 0); quantise(2, 1); quantise(2, 0)
-        gather_bytes("xs2", 0, 2); gather_words(2, 0, 2); gather_bytes("xs2", 2, 4); gather_words(2, 2, 4); gather_words(0, 6, 8); gather_words(1, 4, 8)
+        gather_bytes("xs2", 0, 2); gather_words(2, 0, 2); gather_bytes("xs2", 2, 4); gather_words(2, 2, 4); gather_words(0, 4, 6); gather_words(0, 6, 8); gather_words(1, 4, 6); gather_words(1, 6, 8)
         load_scales(nc.sync, 0, 2, 4); load_pass(0, 0, 2, 4); move_rows(nc.sync, 1, 4, 8, (0, 1)); load_pass(0, 1, 2, 4); move_rows(nc.sync, 1, 4, 8, (2, 3))
         load_scales(nc.sync, 1, 2, 4); load_pass(1, 0, 2, 4); load_pass(0, 2, 2, 4); load_pass(1, 1, 2, 4); load_pass(1, 2, 2, 4)
         load_w2(); scale_rows(nc.sync, tiles["w2s"], w2_scales); load_pos(); load_gates()
         sums(range(4), (0,), (0,)); sums(range(4), (1,), (0,)); sums(range(4), (0,), (1,)); sums(range(4), (1,), (1,))
         sums(range(4), (0, 1), (2,))
-        for g in range(4):
-            stage(g)
+        stage(0); mul_on_pool(0); stage(1); mul_on_pool(1); stage(2); stage(3)
         gather_bytes("xs2", 4, 6); gather_words(2, 4, 6); gather_bytes("xs2", 6, 8); gather_words(2, 6, 8)
-        for g in range(4):
-            mul_staged(g)
-        sums(range(4, 8), (0,), (0,)); sums(range(4, 8), (0,), (1,)); sums(range(4, 8), (1,), (0,)); sums(range(4, 8), (0,), (2,))
-        sums((4,), (1,), (1, 2)); mul(4); sums((5,), (1,), (1, 2)); mul(5); sums((6,), (1,), (1, 2)); mul(6); tr(0); tr(1); tcp(0); tr(2); tr(3); tcp(2); sums((7,), (1,), (1, 2)); mul(7); tr(4); tr(5); tcp(4); tr(6); tcp(6); tr(7); tcp(7); hq(0); hq(2); m2(0); m2(2); hq(4); hq(6); hq(7); ycp(0); ycp(2); m2(4); m2(6); m2(7); ycp(4, nc.vector.tensor_copy); ycp(6); ycp(7)
+        mul_staged(2); mul_staged(3)
+        sums(range(4, 8), (0,), (0,)); sums(range(4, 8), (0,), (1,)); sums(range(4, 8), (1,), (0,)); sums((4, 5), (0,), (2,))
+        sums((4,), (1,), (1, 2)); sums((6, 7), (0,), (2,)); mul(4); sums((5,), (1,), (1, 2)); mul(5); sums((6,), (1,), (1, 2)); mul(6); tr(0); tr(1); tcp(0); tr(2); tr(3); tcp(2); sums((7,), (1,), (1, 2)); mul(7); tr(4); tr(5); tcp(4); tr(6); tcp(6); tr(7); tcp(7); hq(0); hq(2); m2(0); m2(2); hq(4); hq(6); hq(7); ycp(0); ycp(2); m2(4); m2(6); m2(7); ycp(4, nc.vector.tensor_copy); ycp(6); ycp(7)
         tail((0, 512, 768))

@@ -303,7 +303,7 @@ def tile_moe_cap2_glu_relu_kernel(
         load_pass(1, 1, 0, 2); load_pass(0, 2, 0, 2); load_pass(1, 2, 0, 2)
         prepare(2, 0); quantise(2, 1); quantise(2, 0)
         gather_bytes("xs2", 0, 2); gather_words(2, 0, 2); gather_bytes("xs2", 2, 4); gather_words(2, 2, 4); gather_words(0, 4, 6); gather_words(0, 6, 8); gather_words(1, 4, 6); gather_words(1, 6, 8)
-        load_scales(nc.sync, 0, 2, 4); load_pass(0, 0, 2, 4); move_rows(nc.sync, 1, 4, 8, (0, 1)); load_pass(0, 1, 2, 4); move_rows(nc.sync, 1, 4, 8, (2, 3))
+        load_scales(nc.sync, 0, 2, 4); load_pass(0, 0, 2, 4); move_rows(nc.sync, 1, 4, 8); load_pass(0, 1, 2, 4)
         load_scales(nc.sync, 1, 2, 4); load_pass(1, 0, 2, 4); load_pass(0, 2, 2, 4); load_pass(1, 1, 2, 4); load_pass(1, 2, 2, 4)
         load_w2(); scale_rows(nc.sync, tiles["w2s"], w2_scales); load_pos(); load_gates()
         sums(range(4), (0,), (0,)); sums(range(4), (1,), (0,)); sums(range(4), (0,), (1,)); sums(range(4), (1,), (1,))

@@ -278,16 +278,30 @@ def tile_moe_cap2_glu_relu_kernel(
                     for s in passes:
                         mm(g, m, s)
 
-        def tail(cuts):
+        def fetch(pos, c0, c1):
+            return y[:].indirect(pos[:, c0 // 16 : c1 // 16])
+
+        def tail():
             gates = tiles["gates"]
-            for c0, c1 in zip(cuts, cuts[1:]):
-                t1 = keep.tile([P, c1 - c0], F32, name=f"t1_{c0}")
-                t2 = keep.tile([P, c1 - c0], F32, name=f"t2_{c0}")
-                o = keep.tile([P, c1 - c0], F32, name=f"o_{c0}")
-                nc.vector.tensor_tensor(t1[:], y[:].indirect(pos1_t[:, c0 // 16 : c1 // 16]), gates[:, 0, c0:c1], MULT)
-                nc.vector.tensor_tensor(t2[:], y[:].indirect(pos2_t[:, c0 // 16 : c1 // 16]), gates[:, 1, c0:c1], MULT)
-                nc.vector.tensor_tensor(o[:], t1[:], t2[:], ADD)
-                nc.sync.dma_start(out=out[:, c0:c1], in_=o[:])
+            first = sb("first", [P, T], F32)
+            second = sb("second", [P, T], F32)
+            raw1 = sb("raw1", [P, 256], F32)
+            raw2 = [sb(f"raw2_{c}", [P, 256], F32) for c in range(3)]
+            res = [sb(f"res{c}", [P, 256], F32) for c in range(3)]
+            nc.vector.tensor_tensor(first[:, 0:512], fetch(pos1_t, 0, 512), gates[:, 0, 0:512], MULT)
+            nc.scalar.activation(raw2[0][:], fetch(pos2_t, 0, 256), COPY)
+            nc.scalar.activation(raw2[1][:], fetch(pos2_t, 256, 512), COPY)
+            nc.scalar.activation(raw1[:], fetch(pos1_t, 512, 768), COPY)
+            nc.scalar.activation(raw2[2][:], fetch(pos2_t, 512, 768), COPY)
+            for c in range(2):
+                nc.vector.tensor_tensor(second[:, 256 * c : 256 * (c + 1)], raw2[c][:], gates[:, 1, 256 * c : 256 * (c + 1)], MULT)
+            for c in range(2):
+                nc.vector.tensor_tensor(res[c][:], first[:, 256 * c : 256 * (c + 1)], second[:, 256 * c : 256 * (c + 1)], ADD)
+                nc.sync.dma_start(out=out[:, 256 * c : 256 * (c + 1)], in_=res[c][:])
+            nc.vector.tensor_tensor(first[:, 512:768], raw1[:], gates[:, 0, 512:768], MULT)
+            nc.vector.tensor_tensor(second[:, 512:768], raw2[2][:], gates[:, 1, 512:768], MULT)
+            nc.vector.tensor_tensor(res[2][:], first[:, 512:768], second[:, 512:768], ADD)
+            nc.sync.dma_start(out=out[:, 512:768], in_=res[2][:])
 
         zero("s0_0", [P, 6, H]); zero("s1_0", [P, 6, H]); zero("xs0", [P, T]); zero("xs2", [P, T])
         zero("moved1_0", [P, 512]); zero("moved1_4", [P, 512])
@@ -313,4 +327,4 @@ def tile_moe_cap2_glu_relu_kernel(
         mul_staged(2); mul_staged(3)
         sums(range(4, 8), (0,), (0,)); sums(range(4, 8), (0,), (1,)); sums(range(4, 8), (1,), (0,)); sums((4, 5), (0,), (2,))
         sums((4,), (1,), (1, 2)); sums((6, 7), (0,), (2,)); mul(4); sums((5,), (1,), (1, 2)); mul(5); sums((6,), (1,), (1, 2)); mul(6); tr(0); tr(1); tcp(0); tr(2); tr(3); tcp(2); sums((7,), (1,), (1, 2)); mul(7); tr(4); tr(5); tcp(4); tr(6); tcp(6); tr(7); tcp(7); hq(0); hq(2); m2(0); m2(2); hq(4); hq(6); hq(7); ycp(0); ycp(2); m2(4); m2(6); m2(7); ycp(4, nc.vector.tensor_copy); ycp(6); ycp(7)
-        tail((0, 512, 768))
+        tail()

@@ -32,6 +32,8 @@ B_BANKS = (1, 3, 5, 7, 1, 3, 5, 7)
 TURN_BANKS = {0: 0, 2: 2, 4: 4, 6: 6, 7: 1}
 HOLD = {"rb0": "gw2_2", "rb1": "gxs2_2", "rb2": "w1_p2_0"}
 PLACE = {"xb2_0": 0, "gw0_4": 0, "gw0_6": 1024, "gw1_4": 2048, "gw1_6": 3072}
+FUSED = 640
+CUTS = (0, 384, 640, 768)
 
 
 def tile_moe_cap2_glu_relu_kernel(
@@ -285,23 +287,28 @@ def tile_moe_cap2_glu_relu_kernel(
             gates = tiles["gates"]
             first = sb("first", [P, T], F32)
             second = sb("second", [P, T], F32)
-            raw1 = sb("raw1", [P, 256], F32)
-            raw2 = [sb(f"raw2_{c}", [P, 256], F32) for c in range(3)]
-            res = [sb(f"res{c}", [P, 256], F32) for c in range(3)]
-            nc.vector.tensor_tensor(first[:, 0:512], fetch(pos1_t, 0, 512), gates[:, 0, 0:512], MULT)
-            nc.scalar.activation(raw2[0][:], fetch(pos2_t, 0, 256), COPY)
-            nc.scalar.activation(raw2[1][:], fetch(pos2_t, 256, 512), COPY)
-            nc.scalar.activation(raw1[:], fetch(pos1_t, 512, 768), COPY)
-            nc.scalar.activation(raw2[2][:], fetch(pos2_t, 512, 768), COPY)
-            for c in range(2):
-                nc.vector.tensor_tensor(second[:, 256 * c : 256 * (c + 1)], raw2[c][:], gates[:, 1, 256 * c : 256 * (c + 1)], MULT)
-            for c in range(2):
-                nc.vector.tensor_tensor(res[c][:], first[:, 256 * c : 256 * (c + 1)], second[:, 256 * c : 256 * (c + 1)], ADD)
-                nc.sync.dma_start(out=out[:, 256 * c : 256 * (c + 1)], in_=res[c][:])
-            nc.vector.tensor_tensor(first[:, 512:768], raw1[:], gates[:, 0, 512:768], MULT)
-            nc.vector.tensor_tensor(second[:, 512:768], raw2[2][:], gates[:, 1, 512:768], MULT)
-            nc.vector.tensor_tensor(res[2][:], first[:, 512:768], second[:, 512:768], ADD)
-            nc.sync.dma_start(out=out[:, 512:768], in_=res[2][:])
+            nc.vector.tensor_tensor(first[:, 0:FUSED], fetch(pos1_t, 0, FUSED), gates[:, 0, 0:FUSED], MULT)
+            for c0, c1 in zip(CUTS, CUTS[1:]):
+                if c0 >= FUSED:
+                    nc.scalar.activation(sb(f"raw1_{c0}", [P, c1 - c0], F32)[:], fetch(pos1_t, c0, c1), COPY)
+                nc.scalar.activation(sb(f"raw2_{c0}", [P, c1 - c0], F32)[:], fetch(pos2_t, c0, c1), COPY)
+
+            def weigh(choice, c0, c1):
+                nc.vector.tensor_tensor((first, second)[choice][:, c0:c1], tiles[f"raw{choice + 1}_{c0}"][:], gates[:, choice, c0:c1], MULT)
+
+            def add_and_store(c0, c1):
+                res = sb(f"res{c0}", [P, c1 - c0], F32)
+                nc.vector.tensor_tensor(res[:], first[:, c0:c1], second[:, c0:c1], ADD)
+                nc.sync.dma_start(out=out[:, c0:c1], in_=res[:])
+
+            a, b, c = zip(CUTS, CUTS[1:])
+            weigh(1, *a)
+            weigh(1, *b)
+            add_and_store(*a)
+            weigh(0, *c)
+            weigh(1, *c)
+            add_and_store(*b)
+            add_and_store(*c)
 
         zero("s0_0", [P, 6, H]); zero("s1_0", [P, 6, H]); zero("xs0", [P, T]); zero("xs2", [P, T])
         zero("moved1_0", [P, 512]); zero("moved1_4", [P, 512])

@@ -32,8 +32,7 @@ B_BANKS = (1, 3, 5, 7, 1, 3, 5, 7)
 TURN_BANKS = {0: 0, 2: 2, 4: 4, 6: 6, 7: 1}
 HOLD = {"rb0": "gw2_2", "rb1": "gxs2_2", "rb2": "w1_p2_0"}
 PLACE = {"xb2_0": 0, "gw0_4": 0, "gw0_6": 1024, "gw1_4": 2048, "gw1_6": 3072}
-FUSED = 640
-CUTS = (0, 384, 640, 768)
+CUTS = (0, 256, 512, 640, 768)
 
 
 def tile_moe_cap2_glu_relu_kernel(
@@ -287,28 +286,24 @@ def tile_moe_cap2_glu_relu_kernel(
             gates = tiles["gates"]
             first = sb("first", [P, T], F32)
             second = sb("second", [P, T], F32)
-            nc.vector.tensor_tensor(first[:, 0:FUSED], fetch(pos1_t, 0, FUSED), gates[:, 0, 0:FUSED], MULT)
-            for c0, c1 in zip(CUTS, CUTS[1:]):
-                if c0 >= FUSED:
-                    nc.scalar.activation(sb(f"raw1_{c0}", [P, c1 - c0], F32)[:], fetch(pos1_t, c0, c1), COPY)
-                nc.scalar.activation(sb(f"raw2_{c0}", [P, c1 - c0], F32)[:], fetch(pos2_t, c0, c1), COPY)
+            nc.vector.tensor_tensor(second[:], y[:].indirect(pos2_t[:]), gates[:, 1, :], MULT)
+            pieces = list(zip(CUTS, CUTS[1:]))
+            for c0, c1 in pieces:
+                nc.scalar.activation(sb(f"raw{c0}", [P, c1 - c0], F32)[:], fetch(pos1_t, c0, c1), COPY)
 
-            def weigh(choice, c0, c1):
-                nc.vector.tensor_tensor((first, second)[choice][:, c0:c1], tiles[f"raw{choice + 1}_{c0}"][:], gates[:, choice, c0:c1], MULT)
+            def weigh(c0, c1):
+                nc.vector.tensor_tensor(first[:, c0:c1], tiles[f"raw{c0}"][:], gates[:, 0, c0:c1], MULT)
 
             def add_and_store(c0, c1):
                 res = sb(f"res{c0}", [P, c1 - c0], F32)
                 nc.vector.tensor_tensor(res[:], first[:, c0:c1], second[:, c0:c1], ADD)
                 nc.sync.dma_start(out=out[:, c0:c1], in_=res[:])
 
-            a, b, c = zip(CUTS, CUTS[1:])
-            weigh(1, *a)
-            weigh(1, *b)
-            add_and_store(*a)
-            weigh(0, *c)
-            weigh(1, *c)
-            add_and_store(*b)
-            add_and_store(*c)
+            weigh(*pieces[0])
+            for piece, ahead in zip(pieces, pieces[1:]):
+                weigh(*ahead)
+                add_and_store(*piece)
+            add_and_store(*pieces[-1])
 
         zero("s0_0", [P, 6, H]); zero("s1_0", [P, 6, H]); zero("xs0", [P, T]); zero("xs2", [P, T])
         zero("moved1_0", [P, 512]); zero("moved1_4", [P, 512])

@@ -30,8 +30,8 @@ PLANES = (("xs0", 0), ("xs0", 4), ("xs2", 0))
 A_BANKS = (0, 2, 4, 6, 0, 2, 4, 6)
 B_BANKS = (1, 3, 5, 7, 1, 3, 5, 7)
 TURN_BANKS = {0: 0, 2: 2, 4: 4, 6: 6, 7: 1}
-HOLD = {"rb0": "gw2_2", "rb1": "gxs2_2", "rb2": "w1_p2_0"}
-PLACE = {"xb2_0": 0, "gw0_4": 0, "gw0_6": 1024, "gw1_4": 2048, "gw1_6": 3072}
+HOLD = {"gw2_4": "gw2_0", "gxs2_4": "gxs2_0", "gw2_6": "gw2_2", "gxs2_6": "gxs2_2", "rb0": "s1_0", "rb1": "w1_p2_0", "rb2": "w0_p2_0"}
+PLACE = {"w0_p1_0": 0, "gw0_4": 0, "gw0_6": 1024, "w1_p1_0": 2048, "gw1_4": 2048, "gw1_6": 3072}
 CUTS = (0, 256, 512, 640, 768)
 
 
@@ -119,6 +119,17 @@ def tile_moe_cap2_glu_relu_kernel(
                     nc.vector.tensor_copy(dst, src)
                 else:
                     nc.scalar.activation(dst, src, COPY)
+
+        def round_part(s, c0, c1, engine):
+            part = c0 // 512
+            dst = xb(s, part)[:, 4 * (c0 - 512 * part) : 4 * (c1 - 512 * part)]
+            src = tiles[f"xf{s}_0"][:, :, c0:c1]
+            if engine == "pool":
+                nc.gpsimd.tensor_copy(dst.rearrange("p (t j) -> p t j", j=4), src.rearrange("p j t -> p t j"))
+            elif engine == "vector":
+                nc.vector.tensor_copy(dst.rearrange("p (c i j) -> p c j i", i=4, j=4), src.rearrange("p j (c i) -> p c j i", i=4))
+            else:
+                nc.scalar.activation(dst.rearrange("p (c i j) -> p c j i", i=4, j=4), src.rearrange("p j (c i) -> p c j i", i=4), COPY)
 
         def quantise(s, part):
             c0, c1 = HALVES[part]
@@ -310,19 +321,21 @@ def tile_moe_cap2_glu_relu_kernel(
         zero("w2s", [P, E, N]); zero("s0_2", [P, 6, H]); zero("s1_2", [P, 6, H])
         nc.gpsimd.memset(y[:, SLOTS:], 0.0)
         make_identity(nc, ident[:])
-        load_x(0, 0); nc.sync.dma_start(offs_t[:], offs); load_x(1, 0); load_x(2, 0)
-        load_scales(nc.sync, 0, 0, 2); load_pass(0, 0, 0, 1); load_pass(0, 0, 1, 2); load_scales(nc.sync, 1, 0, 2); load_pass(1, 0, 0, 2); load_pass(0, 1, 0, 2)
+        load_x(0, 0); nc.sync.dma_start(offs_t[:], offs); load_x(1, 0)
+        load_scales(nc.sync, 0, 0, 2); load_pass(0, 0, 0, 1); load_x(2, 0); load_pass(0, 0, 1, 2)
+        load_scales(nc.sync, 1, 0, 2); load_pass(1, 0, 0, 1); load_pass(1, 0, 1, 2); load_pass(0, 1, 0, 2)
         prepare(0, 0); quantise(0, 1); quantise(0, 0)
         gather_words(0, 0, 4)
         prepare(1, 0); quantise(1, 1); quantise(1, 0)
         gather_bytes_in_two("xs0", 0, 4); move_rows(nc.sync, 1, 0, 4); gather_words(1, 0, 4); gather_bytes("xs0", 4, 8)
         load_pass(1, 1, 0, 2); load_pass(0, 2, 0, 2); load_pass(1, 2, 0, 2)
-        prepare(2, 0); quantise(2, 1); quantise(2, 0)
-        gather_bytes("xs2", 0, 2); gather_words(2, 0, 2); gather_bytes("xs2", 2, 4); gather_words(2, 2, 4); gather_words(0, 4, 6); gather_words(0, 6, 8); gather_words(1, 4, 6); gather_words(1, 6, 8)
+        round_part(2, 512, 768, "pool"); round_part(2, 0, 512, "scalar"); quantise(2, 1); quantise(2, 0)
+        gather_bytes("xs2", 0, 2); gather_words(2, 0, 2); gather_bytes("xs2", 2, 4); gather_words(2, 2, 4)
         load_scales(nc.sync, 0, 2, 4); load_pass(0, 0, 2, 4); move_rows(nc.sync, 1, 4, 8); load_pass(0, 1, 2, 4)
-        load_scales(nc.sync, 1, 2, 4); load_pass(1, 0, 2, 4); load_pass(0, 2, 2, 4); load_pass(1, 1, 2, 4); load_pass(1, 2, 2, 4)
+        load_scales(nc.sync, 1, 2, 4); load_pass(1, 0, 2, 4); load_pass(0, 2, 2, 3); load_expert(1, 2, 1, 3); load_pass(0, 2, 3, 4); load_expert(1, 3, 1, 3)
         load_w2(); scale_rows(nc.sync, tiles["w2s"], w2_scales); load_pos(); load_gates()
         sums(range(4), (0,), (0,)); sums(range(4), (1,), (0,)); sums(range(4), (0,), (1,)); sums(range(4), (1,), (1,))
+        gather_words(0, 4, 6); gather_words(0, 6, 8); gather_words(1, 4, 6); gather_words(1, 6, 8)
         sums(range(4), (0, 1), (2,))
         stage(0); mul_on_pool(0); stage(1); mul_on_pool(1); stage(2); stage(3)
         gather_bytes("xs2", 4, 6); gather_words(2, 4, 6); gather_bytes("xs2", 6, 8); gather_words(2, 6, 8)

@@ -23,16 +23,13 @@ ADD = mybir.AluOpType.add
 P = 128
 PASSES = K // 512
 SLOTS = E * C
-HALVES = ((0, 512), (512, 768))
-LIVE = 100
-X_PIECES = (((0, 768, 512),), ((0, 768, 512),), ((0, 768, 0),))
-PLANES = (("xs0", 0), ("xs0", 4), ("xs2", 0))
-A_BANKS = (0, 2, 4, 6, 0, 2, 4, 6)
-B_BANKS = (1, 3, 5, 7, 1, 3, 5, 7)
-TURN_BANKS = {0: 0, 2: 2, 4: 4, 6: 6, 7: 1}
-HOLD = {"gw2_4": "gw2_0", "gxs2_4": "gxs2_0", "gw2_6": "gw2_2", "gxs2_6": "gxs2_2", "rb0": "s1_0", "rb1": "w1_p2_0", "rb2": "w0_p2_0"}
-PLACE = {"w0_p1_0": 0, "gw0_4": 0, "gw0_6": 1024, "w1_p1_0": 2048, "gw1_4": 2048, "gw1_6": 3072}
+WIDE = 512
+PLANES = (("xs01", 4), ("xs01", 0), ("xs2", 0))
 CUTS = (0, 256, 512, 640, 768)
+SUM_BANKS = ((0, 2, 4, 6, 0, 2, 4, 6), (1, 3, 5, 7, 1, 3, 5, 7))
+TURNS = {0: (0, 2), 2: (2, 2), 4: (4, 2), 6: (6, 1), 7: (1, 1)}
+HOLD = {"gw2_4": "gw2_0", "gs2_4": "gs2_0", "gw2_6": "gw2_2", "gs2_6": "gs2_2", "gw1_4": "gw1_0", "gw1_6": "gw1_2", "rb0": "s1_0", "rb1": "wp1_2_0", "rb2": "wp0_2_0"}
+PLACE = {"wp1_1_0": 0, "gw0_4": 0, "gw0_6": 1024}
 
 
 def tile_moe_cap2_glu_relu_kernel(
@@ -59,219 +56,164 @@ def tile_moe_cap2_glu_relu_kernel(
         ident = keep.tile([P, P], F32, name="ident")
         words_dram = (w1_words, w3_words)
         scales_dram = (w1_scales, w3_scales)
-        where_w, where_s = {}, {}
+        w_words, w_scales, slot_words, slot_scales, acc, turned = {}, {}, {}, {}, {}, {}
 
         def zero(name, shape):
             nc.vector.memset(sb(name, shape, U8)[:].bitcast(I32), 0)
 
-        def load_x(s, k):
-            c0, c1, share = X_PIECES[s][k]
+        def load_x(s):
             rows = xT[512 * s : 512 * (s + 1), :].rearrange("(p j) t -> p j t", j=4)
-            nc.sync.dma_start(out=sb(f"xf{s}_{k}", [P, 4, c1 - c0], F32)[:], in_=rows[:, :, c0:c1])
+            nc.sync.dma_start(out=sb(f"xf{s}", [P, 4, T], F32)[:], in_=rows)
 
-        def load_pass(m, s, e0, e1):
-            tile = sb(f"w{m}_p{s}_{e0}", [P, e1 - e0, 2 * H], U8)
-            nc.sync.dma_start(out=tile[:].bitcast(I32), in_=words_dram[m][e0:e1, s].rearrange("e p n -> p e n").bitcast(I32))
-            for e in range(e0, e1):
-                where_w[m, e, s] = tile[:, e - e0, :]
+        def load_x_rows(s, half):
+            rows = xT[512 * s : 512 * (s + 1), :].rearrange("(p j) t -> p j t", j=4)
+            nc.sync.dma_start(out=sb(f"xf{s}_{half}", [P, 2, T], F32)[:], in_=rows[:, 2 * half : 2 * half + 2, :])
 
-        def load_expert(m, e, s0=0, s1=PASSES):
-            tile = sb(f"w{m}_e{e}_{s0}", [P, s1 - s0, 2 * H], U8)
+        def round_rows(s, half, c0, c1, engine):
+            base = 0 if c0 < WIDE else WIDE
+            dst = rounded(s, base)[:, 4 * (c0 - base) : 4 * (c1 - base)]
+            src = tiles[f"xf{s}_{half}"][:, :, c0:c1]
+            if engine == "pool":
+                nc.gpsimd.tensor_copy(dst.rearrange("p (t j) -> p t j", j=4)[:, :, 2 * half : 2 * half + 2], src.rearrange("p j t -> p t j"))
+                return
+            dst = dst.rearrange("p (c i j) -> p c j i", i=4, j=4)[:, :, 2 * half : 2 * half + 2, :]
+            src = src.rearrange("p j (c i) -> p c j i", i=4)
+            if engine == "vector":
+                nc.vector.tensor_copy(dst, src)
+            else:
+                nc.scalar.activation(dst, src, COPY)
+
+        def load_words(m, e, s0, s1):
+            tile = sb(f"w{m}_{e}_{s0}", [P, s1 - s0, 2 * H], U8)
             nc.sync.dma_start(out=tile[:].bitcast(I32), in_=words_dram[m][e, s0:s1].rearrange("s p n -> p s n").bitcast(I32))
             for s in range(s0, s1):
-                where_w[m, e, s] = tile[:, s - s0, :]
+                w_words[m, e, s] = tile[:, s - s0, :]
 
-        def scale_rows(queue, tile, dram):
+        def load_pass(m, s, e0, e1):
+            tile = sb(f"wp{m}_{s}_{e0}", [P, e1 - e0, 2 * H], U8)
+            nc.sync.dma_start(out=tile[:].bitcast(I32), in_=words_dram[m][e0:e1, s].rearrange("e p n -> p e n").bitcast(I32))
+            for e in range(e0, e1):
+                w_words[m, e, s] = tile[:, e - e0, :]
+
+        def scale_rows(tile, dram):
             rows = dram.rearrange("e s (q r) n -> r q (e s) n", r=4)
             for r in range(4):
-                queue.dma_start(out=tile[r:128:32, :, :].bitcast(I32), in_=rows[r].bitcast(I32))
+                nc.sync.dma_start(out=tile[r:128:32, :, :].bitcast(I32), in_=rows[r].bitcast(I32))
 
-        def load_scales(queue, m, e0, e1):
+        def load_scales(m, e0, e1):
             tile = tiles[f"s{m}_{e0}"]
-            scale_rows(queue, tile, scales_dram[m][e0:e1])
+            scale_rows(tile, scales_dram[m][e0:e1])
             for e in range(e0, e1):
                 for s in range(PASSES):
-                    where_s[m, e, s] = tile[:, PASSES * (e - e0) + s, :]
+                    w_scales[m, e, s] = tile[:, PASSES * (e - e0) + s, :]
 
-        def load_w2():
-            nc.sync.dma_start(
-                out=sb("w2", [P, E, 2 * N], U8)[:].bitcast(I32), in_=w2_words[:, 0].rearrange("e p n -> p e n").bitcast(I32)
-            )
+        def rounded(s, c0):
+            return sb(f"xb{s}_{c0}", [P, 4 * (WIDE if c0 == 0 else T - WIDE)], BF16)
 
-        def load_pos():
-            nc.sync.dma_start(pos1_t[:], pos1)
-            nc.sync.dma_start(pos2_t[:], pos2)
-
-        def load_gates():
-            nc.sync.dma_start(out=sb("gates", [P, 2, T], F32)[:], in_=gate.rearrange("r p t -> p r t"))
-
-        def xb(s, part):
-            return sb(f"xb{s}_{part}", [P, 4 * (HALVES[part][1] - HALVES[part][0])], BF16)
-
-        def prepare(s, k):
-            c0, c1, share = X_PIECES[s][k]
-            cuts = sorted({0, share, c1 - c0} | ({512 - c0} if c0 < 512 < c1 else set()))
-            for a, b in sorted(zip(cuts, cuts[1:]), reverse=True):
-                part = (c0 + a) // 512
-                dst = xb(s, part)[:, 4 * (c0 + a - 512 * part) : 4 * (c0 + b - 512 * part)].rearrange("p (c i j) -> p c j i", i=4, j=4)
-                src = tiles[f"xf{s}_{k}"][:, :, a:b].rearrange("p j (c i) -> p c j i", i=4)
-                if b <= share:
-                    nc.vector.tensor_copy(dst, src)
-                else:
-                    nc.scalar.activation(dst, src, COPY)
-
-        def round_part(s, c0, c1, engine):
-            part = c0 // 512
-            dst = xb(s, part)[:, 4 * (c0 - 512 * part) : 4 * (c1 - 512 * part)]
-            src = tiles[f"xf{s}_0"][:, :, c0:c1]
+        def round_tokens(s, c0, c1, engine):
+            base = 0 if c0 < WIDE else WIDE
+            dst = rounded(s, base)[:, 4 * (c0 - base) : 4 * (c1 - base)]
+            src = tiles[f"xf{s}"][:, :, c0:c1]
             if engine == "pool":
                 nc.gpsimd.tensor_copy(dst.rearrange("p (t j) -> p t j", j=4), src.rearrange("p j t -> p t j"))
-            elif engine == "vector":
-                nc.vector.tensor_copy(dst.rearrange("p (c i j) -> p c j i", i=4, j=4), src.rearrange("p j (c i) -> p c j i", i=4))
+                return
+            dst = dst.rearrange("p (c i j) -> p c j i", i=4, j=4)
+            src = src.rearrange("p j (c i) -> p c j i", i=4)
+            if engine == "vector":
+                nc.vector.tensor_copy(dst, src)
             else:
-                nc.scalar.activation(dst.rearrange("p (c i j) -> p c j i", i=4, j=4), src.rearrange("p j (c i) -> p c j i", i=4), COPY)
+                nc.scalar.activation(dst, src, COPY)
 
-        def quantise(s, part):
-            c0, c1 = HALVES[part]
+        def quantise(s, c0):
+            c1 = WIDE if c0 == 0 else T
             name, row = PLANES[s]
-            nc.vector.quantize_mx(out=sb(f"xw{s}", [P, T], U32)[:, c0:c1].bitcast(FP8X4), scales=tiles[name][row:128, c0:c1], in_=xb(s, part)[:])
-
-        slot_w, slot_s = {}, {}
+            nc.vector.quantize_mx(out=sb(f"xw{s}", [P, T], U32)[:, c0:c1].bitcast(FP8X4), scales=tiles[name][row:128, c0:c1], in_=rounded(s, c0)[:])
 
         def gather_words(s, g0, g1):
             tile = sb(f"gw{s}_{g0}", [P, 128 * (g1 - g0)], U32)
             nc.vector.tensor_copy(tile[:], tiles[f"xw{s}"][:].indirect(offs_t[:, 8 * g0 : 8 * g1]))
             for g in range(g0, g1):
-                slot_w[s, g] = tile[:, 128 * (g - g0) : 128 * (g - g0 + 1)]
+                slot_words[s, g] = tile[:, 128 * (g - g0) : 128 * (g - g0 + 1)]
 
-        def gather_bytes(name, g0, g1):
-            tile = sb(f"g{name}_{g0}", [P, 128 * (g1 - g0)], U8)
-            nc.vector.tensor_copy(tile[:], tiles[name][:].indirect(offs_t[:, 8 * g0 : 8 * g1]))
-            for s in range(PASSES):
-                if PLANES[s] == (name, 0):
-                    for g in range(g0, g1):
-                        slot_s[s, g] = tile[:, 128 * (g - g0) : 128 * (g - g0 + 1)]
-
-        def gather_bytes_in_two(name, g0, g1):
-            tile = sb(f"g{name}_{g0}", [P, 128 * (g1 - g0)], U8)
-            mid = (g0 + g1) // 2
-            for a, b in ((g0, mid), (mid, g1)):
+        def gather_scales(s, g0, g1, cuts=()):
+            name = PLANES[s][0]
+            tile = sb(f"gs{s}_{g0}", [P, 128 * (g1 - g0)], U8)
+            edges = (g0, *cuts, g1)
+            for a, b in zip(edges, edges[1:]):
                 nc.vector.tensor_copy(tile[:, 128 * (a - g0) : 128 * (b - g0)], tiles[name][:].indirect(offs_t[:, 8 * a : 8 * b]))
             for g in range(g0, g1):
-                slot_s[0, g] = tile[:, 128 * (g - g0) : 128 * (g - g0 + 1)]
+                slot_scales[s, g] = tile[:, 128 * (g - g0) : 128 * (g - g0 + 1)]
 
-        def move_bytes(queue, s, g0, g1):
-            name, row = PLANES[s]
-            plane = tiles[f"moved{s}_{g0}"]
-            queue.dma_start(out=plane[0:LIVE, :].bitcast(I32), in_=tiles[f"g{name}_{g0}"][row : row + LIVE, :].bitcast(I32))
+        def lift_rows(s, g0, g1):
+            plane = tiles[f"lifted{g0}"]
+            for r in range(4):
+                nc.sync.dma_start(out=plane[r:128:32, :].bitcast(I32), in_=tiles[f"gs{s}_{g0}"][4 + r : 128 : 32, :].bitcast(I32))
             for g in range(g0, g1):
-                slot_s[s, g] = plane[:, 128 * (g - g0) : 128 * (g - g0 + 1)]
-
-        def move_rows(queue, s, g0, g1, rows=range(4)):
-            name, row = PLANES[s]
-            plane = tiles[f"moved{s}_{g0}"]
-            for r in rows:
-                queue.dma_start(out=plane[r:128:32, :].bitcast(I32), in_=tiles[f"g{name}_{g0}"][row + r : 128 : 32, :].bitcast(I32))
-            for g in range(g0, g1):
-                slot_s[s, g] = plane[:, 128 * (g - g0) : 128 * (g - g0 + 1)]
-
-        acc, turned = {}, {}
+                slot_scales[0, g] = plane[:, 128 * (g - g0) : 128 * (g - g0 + 1)]
 
         def mm(g, m, s):
-            e = g // 2
             first = (g, m) not in acc
             if first:
-                acc[g, m] = [psum.tile([P, H], F32, name=f"bank{(A_BANKS, B_BANKS)[m][g]}"), 0]
+                acc[g, m] = [psum.tile([P, H], F32, name=f"bank{SUM_BANKS[m][g]}"), 0]
             acc[g, m][1] = acc[g, m][1] + 1
             nc.tensor.matmul_mx(
                 out=acc[g, m][0][:],
-                lhsT=slot_w[s, g].bitcast(FP8X4),
-                lhsT_scale=slot_s[s, g],
-                rhs=where_w[m, e, s].bitcast(FP4X4),
-                rhs_scale=where_s[m, e, s],
+                lhsT=slot_words[s, g].bitcast(FP8X4),
+                lhsT_scale=slot_scales[s, g],
+                rhs=w_words[m, g // 2, s].bitcast(FP4X4),
+                rhs_scale=w_scales[m, g // 2, s],
                 start=first,
                 stop=acc[g, m][1] == PASSES,
             )
             if m == 0 and acc[g, m][1] == PASSES:
-                relu(g)
+                nc.scalar.activation(in_halves(sb(f"ra{g}", [P, H], F32)), by_halves(acc[g, 0][0]), RELU)
 
-        def relu(g):
-            nc.scalar.activation(
-                sb(f"ra{g}", [P, H], F32)[:].rearrange("m (u p d) -> m u p d", u=2, d=2),
-                acc[g, 0][0][:].rearrange("m (p u d) -> m u p d", u=2, d=2),
-                RELU,
-            )
+        def in_halves(tile):
+            return tile[:].rearrange("m (u p d) -> m u p d", u=2, d=2)
+
+        def by_halves(bank):
+            return bank[:].rearrange("m (p u d) -> m u p d", u=2, d=2)
+
+        def sums(gs, ms, passes):
+            for g in gs:
+                for m in ms:
+                    for s in passes:
+                        mm(g, m, s)
 
         def mul(g):
-            nc.vector.tensor_tensor(
-                sb(f"h{g}", [P, H], BF16)[:].rearrange("m (u p d) -> m u p d", u=2, d=2),
-                acc[g, 1][0][:].rearrange("m (p u d) -> m u p d", u=2, d=2),
-                tiles[f"ra{g}"][:].rearrange("m (u p d) -> m u p d", u=2, d=2),
-                MULT,
-            )
-
-        def mul_turn(g):
-            turned[g] = psum.tile([P, H], F32, name=f"bank{TURN_BANKS[g]}")
-            h = sb(f"h{g}", [P, H], BF16)
-            for u in range(2):
-                nc.vector.tensor_tensor(
-                    h[:, 256 * u : 256 * (u + 1)].rearrange("m (p d) -> m p d", d=2),
-                    acc[g, 1][0][:].rearrange("m (p u d) -> m u p d", u=2, d=2)[:, u],
-                    tiles[f"ra{g}"][:, 256 * u : 256 * (u + 1)].rearrange("m (p d) -> m p d", d=2),
-                    MULT,
-                )
-                nc.tensor.transpose(turned[g][:, 128 * u : 128 * (u + 1)], h[:].bitcast(F32)[:, 128 * u : 128 * (u + 1)], ident[:])
+            nc.vector.tensor_tensor(in_halves(sb(f"h{g}", [P, H], BF16)), by_halves(acc[g, 1][0]), in_halves(tiles[f"ra{g}"]), MULT)
 
         def stage(g):
-            nc.scalar.copy(
-                sb(f"rb{g}", [P, H], F32)[:].rearrange("m (u p d) -> m u p d", u=2, d=2),
-                acc[g, 1][0][:].rearrange("m (p u d) -> m u p d", u=2, d=2),
-            )
+            nc.scalar.copy(in_halves(sb(f"rb{g}", [P, H], F32)), by_halves(acc[g, 1][0]))
 
-        def mul_staged(g):
-            nc.vector.tensor_tensor(sb(f"h{g}", [P, H], BF16)[:], tiles[f"rb{g}"][:], tiles[f"ra{g}"][:], MULT)
+        def mul_staged(g, engine):
+            engine.tensor_tensor(sb(f"h{g}", [P, H], BF16)[:], tiles[f"rb{g}"][:], tiles[f"ra{g}"][:], MULT)
 
-        def mul_on_pool(g):
-            nc.gpsimd.tensor_tensor(sb(f"h{g}", [P, H], BF16)[:], tiles[f"rb{g}"][:], tiles[f"ra{g}"][:], MULT)
+        def width(lead):
+            return 128 * TURNS[lead][1]
 
-        def mul_pool(g):
-            nc.scalar.copy(
-                sb(f"rb{g}", [P, H], F32)[:].rearrange("m (u p d) -> m u p d", u=2, d=2),
-                acc[g, 1][0][:].rearrange("m (p u d) -> m u p d", u=2, d=2),
-            )
-            nc.gpsimd.tensor_tensor(sb(f"h{g}", [P, H], BF16)[:], tiles[f"rb{g}"][:], tiles[f"ra{g}"][:], MULT)
+        def turn(lead):
+            turned[lead] = psum.tile([P, H], F32, name=f"bank{TURNS[lead][0]}")
+            for i in range(TURNS[lead][1]):
+                words = tiles[f"h{lead + i}"][:].bitcast(F32)
+                for u in range(2):
+                    nc.tensor.transpose(turned[lead][:, 256 * i + 128 * u : 256 * i + 128 * (u + 1)], words[:, 128 * u : 128 * (u + 1)], ident[:])
 
-        def tr(g):
-            lead = g if g in TURN_BANKS else g - 1
-            if lead not in turned:
-                turned[lead] = psum.tile([P, H], F32, name=f"bank{TURN_BANKS[lead]}")
-            first = 256 * (g - lead)
-            words = tiles[f"h{g}"][:].bitcast(F32)
-            for u in range(2):
-                nc.tensor.transpose(
-                    turned[lead][:, first + 128 * u : first + 128 * (u + 1)], words[:, 128 * u : 128 * (u + 1)], ident[:]
-                )
-
-        def groups(lead):
-            return 1 if lead + 1 in TURN_BANKS or lead == 7 else 2
-
-        def tcp(lead, copy=nc.scalar.copy):
-            count = groups(lead)
+        def weave(lead, copy=nc.scalar.copy):
+            count = TURNS[lead][1]
             copy(
                 sb(f"hb{lead}", [P, 512 * count], BF16)[:].bitcast(F32).rearrange("p (g r u) -> p g r u", g=count, u=2),
                 turned[lead][:, 0 : 256 * count].rearrange("p (g u r) -> p g r u", g=count, u=2),
             )
 
-        def hq(lead):
-            width = 128 * groups(lead)
+        def quantise_h(lead):
             nc.vector.quantize_mx(
-                out=sb(f"hw{lead}", [P, width], U32)[:].bitcast(FP8X4), scales=sb(f"hs{lead}", [P, width], U8)[:], in_=tiles[f"hb{lead}"][:]
+                out=sb(f"hw{lead}", [P, width(lead)], U32)[:].bitcast(FP8X4), scales=sb(f"hs{lead}", [P, width(lead)], U8)[:], in_=tiles[f"hb{lead}"][:]
             )
 
-        def m2(lead):
-            width = 128 * groups(lead)
+        def second(lead):
             nc.tensor.matmul_mx(
-                out=turned[lead][:, 0:width],
+                out=turned[lead][:, 0 : width(lead)],
                 lhsT=tiles["w2"][:, lead // 2, :].bitcast(FP4X4),
                 lhsT_scale=tiles["w2s"][:, lead // 2, :],
                 rhs=tiles[f"hw{lead}"][:].bitcast(FP8X4),
@@ -280,34 +222,31 @@ def tile_moe_cap2_glu_relu_kernel(
                 stop=True,
             )
 
-        def ycp(lead, copy=nc.scalar.copy):
-            width = 128 * groups(lead)
-            copy(y[:, 128 * lead : 128 * lead + width], turned[lead][:, 0:width])
+        def keep_y(lead, copy=nc.scalar.copy):
+            copy(y[:, 128 * lead : 128 * lead + width(lead)], turned[lead][:, 0 : width(lead)])
 
-        def sums(gs, ms, passes):
-            for g in gs:
-                for m in ms:
-                    for s in passes:
-                        mm(g, m, s)
+        def load_rest():
+            nc.sync.dma_start(out=sb("w2", [P, E, 2 * N], U8)[:].bitcast(I32), in_=w2_words[:, 0].rearrange("e p n -> p e n").bitcast(I32))
+            scale_rows(tiles["w2s"], w2_scales)
+            nc.sync.dma_start(pos1_t[:], pos1)
+            nc.sync.dma_start(pos2_t[:], pos2)
+            nc.sync.dma_start(out=sb("gates", [P, 2, T], F32)[:], in_=gate.rearrange("r p t -> p r t"))
 
-        def fetch(pos, c0, c1):
-            return y[:].indirect(pos[:, c0 // 16 : c1 // 16])
-
-        def tail():
+        def combine():
             gates = tiles["gates"]
             first = sb("first", [P, T], F32)
-            second = sb("second", [P, T], F32)
-            nc.vector.tensor_tensor(second[:], y[:].indirect(pos2_t[:]), gates[:, 1, :], MULT)
+            other = sb("other", [P, T], F32)
+            nc.vector.tensor_tensor(other[:], y[:].indirect(pos2_t[:]), gates[:, 1, :], MULT)
             pieces = list(zip(CUTS, CUTS[1:]))
             for c0, c1 in pieces:
-                nc.scalar.activation(sb(f"raw{c0}", [P, c1 - c0], F32)[:], fetch(pos1_t, c0, c1), COPY)
+                nc.scalar.activation(sb(f"raw{c0}", [P, c1 - c0], F32)[:], y[:].indirect(pos1_t[:, c0 // 16 : c1 // 16]), COPY)
 
             def weigh(c0, c1):
                 nc.vector.tensor_tensor(first[:, c0:c1], tiles[f"raw{c0}"][:], gates[:, 0, c0:c1], MULT)
 
             def add_and_store(c0, c1):
                 res = sb(f"res{c0}", [P, c1 - c0], F32)
-                nc.vector.tensor_tensor(res[:], first[:, c0:c1], second[:, c0:c1], ADD)
+                nc.vector.tensor_tensor(res[:], first[:, c0:c1], other[:, c0:c1], ADD)
                 nc.sync.dma_start(out=out[:, c0:c1], in_=res[:])
 
             weigh(*pieces[0])
@@ -316,30 +255,44 @@ def tile_moe_cap2_glu_relu_kernel(
                 add_and_store(*piece)
             add_and_store(*pieces[-1])
 
-        zero("s0_0", [P, 6, H]); zero("s1_0", [P, 6, H]); zero("xs0", [P, T]); zero("xs2", [P, T])
-        zero("moved1_0", [P, 512]); zero("moved1_4", [P, 512])
-        zero("w2s", [P, E, N]); zero("s0_2", [P, 6, H]); zero("s1_2", [P, 6, H])
+        def clock(name, ap):
+            nc.gpsimd.tensor_copy(sb(f"clock_{name}", [P, 1], F32)[:], ap)
+
+        zero("s0_0", [P, 6, H]); zero("s1_0", [P, 6, H])
+        zero("xs01", [P, T]); zero("xs2", [P, T]); zero("lifted0", [P, 512]); zero("lifted4", [P, 512]); zero("w2s", [P, E, N])
+        zero("s0_2", [P, 6, H]); zero("s1_2", [P, 6, H])
         nc.gpsimd.memset(y[:, SLOTS:], 0.0)
         make_identity(nc, ident[:])
-        load_x(0, 0); nc.sync.dma_start(offs_t[:], offs); load_x(1, 0)
-        load_scales(nc.sync, 0, 0, 2); load_pass(0, 0, 0, 1); load_x(2, 0); load_pass(0, 0, 1, 2)
-        load_scales(nc.sync, 1, 0, 2); load_pass(1, 0, 0, 1); load_pass(1, 0, 1, 2); load_pass(0, 1, 0, 2)
-        prepare(0, 0); quantise(0, 1); quantise(0, 0)
-        gather_words(0, 0, 4)
-        prepare(1, 0); quantise(1, 1); quantise(1, 0)
-        gather_bytes_in_two("xs0", 0, 4); move_rows(nc.sync, 1, 0, 4); gather_words(1, 0, 4); gather_bytes("xs0", 4, 8)
-        load_pass(1, 1, 0, 2); load_pass(0, 2, 0, 2); load_pass(1, 2, 0, 2)
-        round_part(2, 512, 768, "pool"); round_part(2, 0, 512, "scalar"); quantise(2, 1); quantise(2, 0)
-        gather_bytes("xs2", 0, 2); gather_words(2, 0, 2); gather_bytes("xs2", 2, 4); gather_words(2, 2, 4)
-        load_scales(nc.sync, 0, 2, 4); load_pass(0, 0, 2, 4); move_rows(nc.sync, 1, 4, 8); load_pass(0, 1, 2, 4)
-        load_scales(nc.sync, 1, 2, 4); load_pass(1, 0, 2, 4); load_pass(0, 2, 2, 3); load_expert(1, 2, 1, 3); load_pass(0, 2, 3, 4); load_expert(1, 3, 1, 3)
-        load_w2(); scale_rows(nc.sync, tiles["w2s"], w2_scales); load_pos(); load_gates()
-        sums(range(4), (0,), (0,)); sums(range(4), (1,), (0,)); sums(range(4), (0,), (1,)); sums(range(4), (1,), (1,))
-        gather_words(0, 4, 6); gather_words(0, 6, 8); gather_words(1, 4, 6); gather_words(1, 6, 8)
+
+        load_x(0); nc.sync.dma_start(offs_t[:], offs); load_x_rows(1, 0); load_x_rows(1, 1)
+        load_scales(0, 0, 2); load_pass(0, 0, 0, 1); load_pass(0, 0, 1, 2); load_x_rows(2, 0)
+        round_tokens(0, WIDE, T, "scalar"); round_tokens(0, 0, WIDE, "vector"); quantise(0, WIDE); quantise(0, 0)
+        gather_scales(0, 0, 4); lift_rows(0, 0, 4); gather_words(0, 0, 4)
+        load_x_rows(2, 1); load_pass(0, 1, 0, 2)
+        load_scales(1, 0, 2); load_pass(1, 0, 0, 1); load_pass(1, 0, 1, 2); load_pass(1, 1, 0, 2); load_pass(0, 2, 0, 2); load_pass(1, 2, 0, 2)
+        for half in range(2):
+            round_rows(1, half, WIDE, T, "pool"); round_rows(1, half, 0, WIDE, "scalar")
+        quantise(1, WIDE); quantise(1, 0)
+        for g in (0, 2):
+            gather_scales(1, g, g + 2); gather_words(1, g, g + 2)
+        gather_scales(1, 4, 8)
+        for half in range(2):
+            round_rows(2, half, WIDE, T, "pool"); round_rows(2, half, 0, WIDE, "scalar")
+        quantise(2, WIDE); quantise(2, 0)
+        gather_scales(2, 0, 2); gather_words(2, 0, 2); gather_scales(2, 2, 4); gather_words(2, 2, 4)
+        load_scales(0, 2, 4); load_pass(0, 1, 2, 4); lift_rows(1, 4, 8); load_pass(0, 0, 2, 4)
+        load_scales(1, 2, 4); load_pass(1, 1, 2, 4); load_words(0, 2, 2, 3); load_words(1, 2, 0, 1); load_words(1, 2, 2, 3); load_words(0, 3, 2, 3); load_words(1, 3, 0, 1); load_words(1, 3, 2, 3)
+        load_rest()
+        sums(range(4), (0,), (0,)); sums(range(4), (0,), (1,)); sums(range(4), (1,), (0,)); sums(range(4), (1,), (1,))
+        gather_words(1, 4, 6); gather_words(1, 6, 8); gather_words(0, 4, 6); gather_words(0, 6, 8)
         sums(range(4), (0, 1), (2,))
-        stage(0); mul_on_pool(0); stage(1); mul_on_pool(1); stage(2); stage(3)
-        gather_bytes("xs2", 4, 6); gather_words(2, 4, 6); gather_bytes("xs2", 6, 8); gather_words(2, 6, 8)
-        mul_staged(2); mul_staged(3)
-        sums(range(4, 8), (0,), (0,)); sums(range(4, 8), (0,), (1,)); sums(range(4, 8), (1,), (0,)); sums((4, 5), (0,), (2,))
-        sums((4,), (1,), (1, 2)); sums((6, 7), (0,), (2,)); mul(4); sums((5,), (1,), (1, 2)); mul(5); sums((6,), (1,), (1, 2)); mul(6); tr(0); tr(1); tcp(0); tr(2); tr(3); tcp(2); sums((7,), (1,), (1, 2)); mul(7); tr(4); tr(5); tcp(4); tr(6); tcp(6); tr(7); tcp(7); hq(0); hq(2); m2(0); m2(2); hq(4); hq(6); hq(7); ycp(0); ycp(2); m2(4); m2(6); m2(7); ycp(4, nc.vector.tensor_copy); ycp(6); ycp(7)
-        tail()
+        stage(0); mul_staged(0, nc.gpsimd); stage(1); mul_staged(1, nc.gpsimd); stage(2); stage(3)
+        gather_scales(2, 4, 6); gather_words(2, 4, 6); gather_scales(2, 6, 8); gather_words(2, 6, 8)
+        mul_staged(2, nc.vector); mul_staged(3, nc.vector)
+
+        sums(range(4, 8), (0,), (1,)); sums(range(4, 8), (0,), (0,)); sums(range(4, 8), (1,), (1,)); sums((4, 5), (0,), (2,))
+        sums((4,), (1,), (0, 2)); sums((6, 7), (0,), (2,)); mul(4); sums((5,), (1,), (0, 2)); mul(5); sums((6,), (1,), (0, 2)); mul(6)
+        turn(0); weave(0); turn(2); weave(2); sums((7,), (1,), (0, 2)); mul(7); turn(4); weave(4); turn(6); weave(6); turn(7); weave(7)
+        quantise_h(0); quantise_h(2); second(0); second(2); quantise_h(4); quantise_h(6); quantise_h(7); keep_y(0); keep_y(2); second(4); second(6); second(7)
+        keep_y(4, nc.vector.tensor_copy); keep_y(6); keep_y(7)
+        combine()

@@ -28,7 +28,7 @@ PLANES = (("xs01", 4), ("xs01", 0), ("xs2", 0))
 CUTS = (0, 256, 512, 640, 768)
 SUM_BANKS = ((0, 2, 4, 6, 0, 2, 4, 6), (1, 3, 5, 7, 1, 3, 5, 7))
 TURNS = {0: (0, 2), 2: (2, 2), 4: (4, 2), 6: (6, 1), 7: (1, 1)}
-HOLD = {"gw2_4": "gw2_0", "gs2_4": "gs2_0", "gw2_6": "gw2_2", "gs2_6": "gs2_2", "gw1_4": "gw1_0", "gw1_6": "gw1_2", "rb0": "s1_0", "rb1": "wp1_2_0", "rb2": "wp0_2_0"}
+HOLD = {"xb1_512": "xb0_0", "gw2_4": "gw2_0", "gs2_4": "gs2_0", "gw2_6": "gw2_2", "gs2_6": "gs2_2", "gw1_4": "gw1_0", "gw1_6": "gw1_2", "rb0": "s1_0", "rb1": "wp1_2_0", "rb2": "wp0_2_0"}
 PLACE = {"wp1_1_0": 0, "gw0_4": 0, "gw0_6": 1024}
 
 
@@ -106,6 +106,14 @@ def tile_moe_cap2_glu_relu_kernel(
             for e in range(e0, e1):
                 for s in range(PASSES):
                     w_scales[m, e, s] = tile[:, PASSES * (e - e0) + s, :]
+
+        def load_planes(m, i0, i1):
+            tile = tiles[f"s{m}_{i0}"]
+            rows = scales_dram[m].rearrange("e s (q r) n -> r q (e s) n", r=4)
+            for r in range(4):
+                nc.sync.dma_start(out=tile[r:128:32, :, :].bitcast(I32), in_=rows[r][:, i0:i1, :].bitcast(I32))
+            for i in range(i0, i1):
+                w_scales[m, i // PASSES, i % PASSES] = tile[:, i - i0, :]
 
         def rounded(s, c0):
             return sb(f"xb{s}_{c0}", [P, 4 * (WIDE if c0 == 0 else T - WIDE)], BF16)
@@ -199,6 +207,13 @@ def tile_moe_cap2_glu_relu_kernel(
                 for u in range(2):
                     nc.tensor.transpose(turned[lead][:, 256 * i + 128 * u : 256 * i + 128 * (u + 1)], words[:, 128 * u : 128 * (u + 1)], ident[:])
 
+        def mul_and_turn(g):
+            turned[g] = psum.tile([P, H], F32, name=f"bank{TURNS[g][0]}")
+            h = sb(f"h{g}", [P, H], BF16)
+            for u in range(2):
+                nc.vector.tensor_tensor(in_halves(h)[:, u], by_halves(acc[g, 1][0])[:, u], in_halves(tiles[f"ra{g}"])[:, u], MULT)
+                nc.tensor.transpose(turned[g][:, 128 * u : 128 * (u + 1)], h[:].bitcast(F32)[:, 128 * u : 128 * (u + 1)], ident[:])
+
         def weave(lead, copy=nc.scalar.copy):
             count = TURNS[lead][1]
             copy(
@@ -279,7 +294,8 @@ def tile_moe_cap2_glu_relu_kernel(
         for half in range(2):
             round_rows(2, half, WIDE, T, "pool"); round_rows(2, half, 0, WIDE, "scalar")
         quantise(2, WIDE); quantise(2, 0)
-        gather_scales(2, 0, 2); gather_words(2, 0, 2); gather_scales(2, 2, 4); gather_words(2, 2, 4)
+        for g in range(4):
+            gather_scales(2, g, g + 1); gather_words(2, g, g + 1)
         load_scales(0, 2, 4); load_pass(0, 1, 2, 4); lift_rows(1, 4, 8); load_pass(0, 0, 2, 4)
         load_scales(1, 2, 4); load_pass(1, 1, 2, 4); load_words(0, 2, 2, 3); load_words(1, 2, 0, 1); load_words(1, 2, 2, 3); load_words(0, 3, 2, 3); load_words(1, 3, 0, 1); load_words(1, 3, 2, 3)
         load_rest()
@@ -290,9 +306,10 @@ def tile_moe_cap2_glu_relu_kernel(
         gather_scales(2, 4, 6); gather_words(2, 4, 6); gather_scales(2, 6, 8); gather_words(2, 6, 8)
         mul_staged(2, nc.vector); mul_staged(3, nc.vector)
 
+
         sums(range(4, 8), (0,), (1,)); sums(range(4, 8), (0,), (0,)); sums(range(4, 8), (1,), (1,)); sums((4, 5), (0,), (2,))
         sums((4,), (1,), (0, 2)); sums((6, 7), (0,), (2,)); mul(4); sums((5,), (1,), (0, 2)); mul(5); sums((6,), (1,), (0, 2)); mul(6)
-        turn(0); weave(0); turn(2); weave(2); sums((7,), (1,), (0, 2)); mul(7); turn(4); weave(4); turn(6); weave(6); turn(7); weave(7)
+        turn(0); weave(0); turn(2); weave(2); sums((7,), (1,), (0, 2)); turn(4); weave(4); turn(6); weave(6); mul_and_turn(7); weave(7)
         quantise_h(0); quantise_h(2); second(0); second(2); quantise_h(4); quantise_h(6); quantise_h(7); keep_y(0); keep_y(2); second(4); second(6); second(7)
         keep_y(4, nc.vector.tensor_copy); keep_y(6); keep_y(7)
         combine()

@@ -309,7 +309,7 @@ def tile_moe_cap2_glu_relu_kernel(
 
         sums(range(4, 8), (0,), (1,)); sums(range(4, 8), (0,), (0,)); sums(range(4, 8), (1,), (1,)); sums((4, 5), (0,), (2,))
         sums((4,), (1,), (0, 2)); sums((6, 7), (0,), (2,)); mul(4); sums((5,), (1,), (0, 2)); mul(5); sums((6,), (1,), (0, 2)); mul(6)
-        turn(0); weave(0); turn(2); weave(2); sums((7,), (1,), (0, 2)); turn(4); weave(4); turn(6); weave(6); mul_and_turn(7); weave(7)
-        quantise_h(0); quantise_h(2); second(0); second(2); quantise_h(4); quantise_h(6); quantise_h(7); keep_y(0); keep_y(2); second(4); second(6); second(7)
-        keep_y(4, nc.vector.tensor_copy); keep_y(6); keep_y(7)
+        turn(0); weave(0); turn(2); weave(2); sums((7,), (1,), (0, 2)); turn(4); turn(6); mul_and_turn(7); weave(7); quantise_h(7)
+        weave(4); weave(6, nc.vector.tensor_copy); quantise_h(0); quantise_h(2); quantise_h(4); quantise_h(6); second(7); keep_y(7); second(0); second(2); second(4); second(6)
+        keep_y(0); keep_y(2); keep_y(4); keep_y(6, nc.vector.tensor_copy)
         combine()

@@ -279,20 +279,22 @@ def tile_moe_cap2_glu_relu_kernel(
         nc.gpsimd.memset(y[:, SLOTS:], 0.0)
         make_identity(nc, ident[:])
 
-        load_x(0); nc.sync.dma_start(offs_t[:], offs); load_x_rows(1, 0); load_x_rows(1, 1)
+        load_x_rows(0, 0); load_x_rows(0, 1); nc.sync.dma_start(offs_t[:], offs); load_x_rows(1, 0); load_x_rows(1, 1)
         load_scales(0, 0, 2); load_pass(0, 0, 0, 1); load_pass(0, 0, 1, 2); load_x_rows(2, 0)
-        round_tokens(0, WIDE, T, "scalar"); round_tokens(0, 0, WIDE, "vector"); quantise(0, WIDE); quantise(0, 0)
+        for half in range(2):
+            round_rows(0, half, WIDE, T, "scalar"); round_rows(0, half, 0, WIDE, "vector")
+        quantise(0, WIDE); quantise(0, 0)
         gather_scales(0, 0, 4); lift_rows(0, 0, 4); gather_words(0, 0, 4)
         load_x_rows(2, 1); load_pass(0, 1, 0, 2)
         load_scales(1, 0, 2); load_pass(1, 0, 0, 1); load_pass(1, 0, 1, 2); load_pass(1, 1, 0, 2); load_pass(0, 2, 0, 2); load_pass(1, 2, 0, 2)
-        for half in range(2):
-            round_rows(1, half, WIDE, T, "pool"); round_rows(1, half, 0, WIDE, "scalar")
+        round_rows(1, 0, WIDE, T, "pool"); round_rows(1, 0, 0, WIDE, "scalar")
+        round_rows(1, 1, WIDE, T, "pool"); round_rows(1, 1, 448, WIDE, "pool"); round_rows(1, 1, 0, 448, "scalar")
         quantise(1, WIDE); quantise(1, 0)
         for g in (0, 2):
             gather_scales(1, g, g + 2); gather_words(1, g, g + 2)
         gather_scales(1, 4, 8)
-        for half in range(2):
-            round_rows(2, half, WIDE, T, "pool"); round_rows(2, half, 0, WIDE, "scalar")
+        round_rows(2, 0, WIDE, T, "pool"); round_rows(2, 0, 0, WIDE, "scalar")
+        round_rows(2, 1, WIDE, T, "pool"); round_rows(2, 1, 448, WIDE, "pool"); round_rows(2, 1, 0, 448, "scalar")
         quantise(2, WIDE); quantise(2, 0)
         for g in range(4):
             gather_scales(2, g, g + 1); gather_words(2, g, g + 1)

@@ -23,13 +23,29 @@ ADD = mybir.AluOpType.add
 P = 128
 PASSES = K // 512
 SLOTS = E * C
+GROUP = 128
+W1, W3 = 0, 1
 WIDE = 512
+POOL_TOKENS = 320
 PLANES = (("xs01", 4), ("xs01", 0), ("xs2", 0))
-CUTS = (0, 256, 512, 640, 768)
-SUM_BANKS = ((0, 2, 4, 6, 0, 2, 4, 6), (1, 3, 5, 7, 1, 3, 5, 7))
+LIFT = 4
 TURNS = {0: (0, 2), 2: (2, 2), 4: (4, 2), 6: (6, 1), 7: (1, 1)}
-HOLD = {"xb1_512": "xb0_0", "gw2_4": "gw2_0", "gs2_4": "gs2_0", "gw2_6": "gw2_2", "gs2_6": "gs2_2", "gw1_4": "gw1_0", "gw1_6": "gw1_2", "rb0": "s1_0", "rb1": "wp1_2_0", "rb2": "wp0_2_0"}
-PLACE = {"wp1_1_0": 0, "gw0_4": 0, "gw0_6": 1024}
+CUTS = (0, 256, 512, 640, 768)
+REUSE = {
+    "xb1_512": "xb0_0",
+    "gw0_4": "xf1_1",
+    "gw0_5": "xf2_1",
+    "gw1_4": "gw1_0",
+    "gw1_6": "gw1_2",
+    "gw0_6": "wp1_1_0",
+    "gs2_4": "gs2_0",
+    "gw2_4": "gw2_0",
+    "gs2_6": "gs2_2",
+    "gw2_6": "gw2_2",
+    "rb0": "s1_0",
+    "rb1": "wp1_2_0",
+    "rb2": "wp0_2_0",
+}
 
 
 def tile_moe_cap2_glu_relu_kernel(
@@ -39,14 +55,11 @@ def tile_moe_cap2_glu_relu_kernel(
     with ExitStack() as ctx:
         keep = ctx.enter_context(tc.tile_pool(name="keep", bufs=1))
         psum = ctx.enter_context(tc.psum_pool(name="psum", bufs=1))
-        shared = ctx.enter_context(tc.tile_pool(name="shared", bufs=1))
         tiles = {}
 
         def sb(name, shape, dtype):
-            if name not in tiles and name in PLACE:
-                tiles[name] = shared.tile(shape, dtype, name=name, offset=PLACE[name], align_bytes=256)
             if name not in tiles:
-                tiles[name] = keep.tile(shape, dtype, name=HOLD.get(name, name), align_bytes=256)
+                tiles[name] = keep.tile(shape, dtype, name=REUSE.get(name, name), align_bytes=256)
             return tiles[name]
 
         offs_t = keep.tile([P, SLOTS // 16], U16, name="offs_t")
@@ -56,38 +69,15 @@ def tile_moe_cap2_glu_relu_kernel(
         ident = keep.tile([P, P], F32, name="ident")
         words_dram = (w1_words, w3_words)
         scales_dram = (w1_scales, w3_scales)
-        w_words, w_scales, slot_words, slot_scales, acc, turned = {}, {}, {}, {}, {}, {}
+        w_words, w_scales, slot_words, slot_scales = {}, {}, {}, {}
+        sums, passes_done, turned = {}, {}, {}
 
-        def zero(name, shape):
+        def zero_plane(name, shape):
             nc.vector.memset(sb(name, shape, U8)[:].bitcast(I32), 0)
 
-        def load_x(s):
-            rows = xT[512 * s : 512 * (s + 1), :].rearrange("(p j) t -> p j t", j=4)
-            nc.sync.dma_start(out=sb(f"xf{s}", [P, 4, T], F32)[:], in_=rows)
-
-        def load_x_rows(s, half):
+        def load_x(s, half):
             rows = xT[512 * s : 512 * (s + 1), :].rearrange("(p j) t -> p j t", j=4)
             nc.sync.dma_start(out=sb(f"xf{s}_{half}", [P, 2, T], F32)[:], in_=rows[:, 2 * half : 2 * half + 2, :])
-
-        def round_rows(s, half, c0, c1, engine):
-            base = 0 if c0 < WIDE else WIDE
-            dst = rounded(s, base)[:, 4 * (c0 - base) : 4 * (c1 - base)]
-            src = tiles[f"xf{s}_{half}"][:, :, c0:c1]
-            if engine == "pool":
-                nc.gpsimd.tensor_copy(dst.rearrange("p (t j) -> p t j", j=4)[:, :, 2 * half : 2 * half + 2], src.rearrange("p j t -> p t j"))
-                return
-            dst = dst.rearrange("p (c i j) -> p c j i", i=4, j=4)[:, :, 2 * half : 2 * half + 2, :]
-            src = src.rearrange("p j (c i) -> p c j i", i=4)
-            if engine == "vector":
-                nc.vector.tensor_copy(dst, src)
-            else:
-                nc.scalar.activation(dst, src, COPY)
-
-        def load_words(m, e, s0, s1):
-            tile = sb(f"w{m}_{e}_{s0}", [P, s1 - s0, 2 * H], U8)
-            nc.sync.dma_start(out=tile[:].bitcast(I32), in_=words_dram[m][e, s0:s1].rearrange("s p n -> p s n").bitcast(I32))
-            for s in range(s0, s1):
-                w_words[m, e, s] = tile[:, s - s0, :]
 
         def load_pass(m, s, e0, e1):
             tile = sb(f"wp{m}_{s}_{e0}", [P, e1 - e0, 2 * H], U8)
@@ -95,86 +85,79 @@ def tile_moe_cap2_glu_relu_kernel(
             for e in range(e0, e1):
                 w_words[m, e, s] = tile[:, e - e0, :]
 
-        def scale_rows(tile, dram):
+        def load_expert(m, e, s0, s1):
+            tile = sb(f"we{m}_{e}_{s0}", [P, s1 - s0, 2 * H], U8)
+            nc.sync.dma_start(out=tile[:].bitcast(I32), in_=words_dram[m][e, s0:s1].rearrange("s p n -> p s n").bitcast(I32))
+            for s in range(s0, s1):
+                w_words[m, e, s] = tile[:, s - s0, :]
+
+        def load_scale_rows(tile, dram):
             rows = dram.rearrange("e s (q r) n -> r q (e s) n", r=4)
             for r in range(4):
                 nc.sync.dma_start(out=tile[r:128:32, :, :].bitcast(I32), in_=rows[r].bitcast(I32))
 
-        def load_scales(m, e0, e1):
+        def load_scales(m, e0):
             tile = tiles[f"s{m}_{e0}"]
-            scale_rows(tile, scales_dram[m][e0:e1])
-            for e in range(e0, e1):
+            load_scale_rows(tile, scales_dram[m][e0 : e0 + 2])
+            for e in (e0, e0 + 1):
                 for s in range(PASSES):
                     w_scales[m, e, s] = tile[:, PASSES * (e - e0) + s, :]
-
-        def load_planes(m, i0, i1):
-            tile = tiles[f"s{m}_{i0}"]
-            rows = scales_dram[m].rearrange("e s (q r) n -> r q (e s) n", r=4)
-            for r in range(4):
-                nc.sync.dma_start(out=tile[r:128:32, :, :].bitcast(I32), in_=rows[r][:, i0:i1, :].bitcast(I32))
-            for i in range(i0, i1):
-                w_scales[m, i // PASSES, i % PASSES] = tile[:, i - i0, :]
 
         def rounded(s, c0):
             return sb(f"xb{s}_{c0}", [P, 4 * (WIDE if c0 == 0 else T - WIDE)], BF16)
 
-        def round_tokens(s, c0, c1, engine):
+        def round_x(s, half, c0, c1, engine):
             base = 0 if c0 < WIDE else WIDE
             dst = rounded(s, base)[:, 4 * (c0 - base) : 4 * (c1 - base)]
-            src = tiles[f"xf{s}"][:, :, c0:c1]
-            if engine == "pool":
-                nc.gpsimd.tensor_copy(dst.rearrange("p (t j) -> p t j", j=4), src.rearrange("p j t -> p t j"))
+            src = tiles[f"xf{s}_{half}"][:, :, c0:c1]
+            if engine is nc.gpsimd:
+                nc.gpsimd.tensor_copy(dst.rearrange("p (t j) -> p t j", j=4)[:, :, 2 * half : 2 * half + 2], src.rearrange("p j t -> p t j"))
                 return
-            dst = dst.rearrange("p (c i j) -> p c j i", i=4, j=4)
+            dst = dst.rearrange("p (c i j) -> p c j i", i=4, j=4)[:, :, 2 * half : 2 * half + 2, :]
             src = src.rearrange("p j (c i) -> p c j i", i=4)
-            if engine == "vector":
+            if engine is nc.vector:
                 nc.vector.tensor_copy(dst, src)
             else:
                 nc.scalar.activation(dst, src, COPY)
 
-        def quantise(s, c0):
+        def quantise_x(s, c0):
             c1 = WIDE if c0 == 0 else T
             name, row = PLANES[s]
-            nc.vector.quantize_mx(out=sb(f"xw{s}", [P, T], U32)[:, c0:c1].bitcast(FP8X4), scales=tiles[name][row:128, c0:c1], in_=rounded(s, c0)[:])
+            codes = sb(f"xw{s}", [P, T], U32)
+            nc.vector.quantize_mx(out=codes[:, c0:c1].bitcast(FP8X4), scales=tiles[name][row:128, c0:c1], in_=rounded(s, c0)[:])
+
+        def round_and_quantise(s):
+            round_x(s, 0, WIDE, T, nc.gpsimd)
+            round_x(s, 0, 0, WIDE, nc.scalar)
+            round_x(s, 1, 0, POOL_TOKENS, nc.gpsimd)
+            round_x(s, 1, POOL_TOKENS, WIDE, nc.scalar)
+            round_x(s, 1, WIDE, T, nc.scalar)
+            quantise_x(s, 0)
+            quantise_x(s, WIDE)
+
+        def by_group(where, s, g0, g1, tile):
+            for g in range(g0, g1):
+                where[s, g] = tile[:, GROUP * (g - g0) : GROUP * (g - g0 + 1)]
 
         def gather_words(s, g0, g1):
-            tile = sb(f"gw{s}_{g0}", [P, 128 * (g1 - g0)], U32)
+            tile = sb(f"gw{s}_{g0}", [P, GROUP * (g1 - g0)], U32)
             nc.vector.tensor_copy(tile[:], tiles[f"xw{s}"][:].indirect(offs_t[:, 8 * g0 : 8 * g1]))
-            for g in range(g0, g1):
-                slot_words[s, g] = tile[:, 128 * (g - g0) : 128 * (g - g0 + 1)]
+            by_group(slot_words, s, g0, g1, tile)
 
-        def gather_scales(s, g0, g1, cuts=()):
-            name = PLANES[s][0]
-            tile = sb(f"gs{s}_{g0}", [P, 128 * (g1 - g0)], U8)
-            edges = (g0, *cuts, g1)
-            for a, b in zip(edges, edges[1:]):
-                nc.vector.tensor_copy(tile[:, 128 * (a - g0) : 128 * (b - g0)], tiles[name][:].indirect(offs_t[:, 8 * a : 8 * b]))
-            for g in range(g0, g1):
-                slot_scales[s, g] = tile[:, 128 * (g - g0) : 128 * (g - g0 + 1)]
+        def gather_scales(s, g0, g1):
+            tile = sb(f"gs{s}_{g0}", [P, GROUP * (g1 - g0)], U8)
+            nc.vector.tensor_copy(tile[:], tiles[PLANES[s][0]][:].indirect(offs_t[:, 8 * g0 : 8 * g1]))
+            by_group(slot_scales, s, g0, g1, tile)
 
-        def lift_rows(s, g0, g1):
+        def gather_pass(s, g0, g1):
+            gather_scales(s, g0, g1)
+            gather_words(s, g0, g1)
+
+        def lift_pass0_scales(gathered, g0):
             plane = tiles[f"lifted{g0}"]
             for r in range(4):
-                nc.sync.dma_start(out=plane[r:128:32, :].bitcast(I32), in_=tiles[f"gs{s}_{g0}"][4 + r : 128 : 32, :].bitcast(I32))
-            for g in range(g0, g1):
-                slot_scales[0, g] = plane[:, 128 * (g - g0) : 128 * (g - g0 + 1)]
-
-        def mm(g, m, s):
-            first = (g, m) not in acc
-            if first:
-                acc[g, m] = [psum.tile([P, H], F32, name=f"bank{SUM_BANKS[m][g]}"), 0]
-            acc[g, m][1] = acc[g, m][1] + 1
-            nc.tensor.matmul_mx(
-                out=acc[g, m][0][:],
-                lhsT=slot_words[s, g].bitcast(FP8X4),
-                lhsT_scale=slot_scales[s, g],
-                rhs=w_words[m, g // 2, s].bitcast(FP4X4),
-                rhs_scale=w_scales[m, g // 2, s],
-                start=first,
-                stop=acc[g, m][1] == PASSES,
-            )
-            if m == 0 and acc[g, m][1] == PASSES:
-                nc.scalar.activation(in_halves(sb(f"ra{g}", [P, H], F32)), by_halves(acc[g, 0][0]), RELU)
+                nc.sync.dma_start(out=plane[r:128:32, :].bitcast(I32), in_=tiles[gathered][LIFT + r : 128 : 32, :].bitcast(I32))
+            by_group(slot_scales, 0, g0, g0 + 4, plane)
 
         def in_halves(tile):
             return tile[:].rearrange("m (u p d) -> m u p d", u=2, d=2)
@@ -182,23 +165,40 @@ def tile_moe_cap2_glu_relu_kernel(
         def by_halves(bank):
             return bank[:].rearrange("m (p u d) -> m u p d", u=2, d=2)
 
-        def sums(gs, ms, passes):
-            for g in gs:
-                for m in ms:
+        def add_pass(g, m, s):
+            done = passes_done.get((g, m), 0)
+            if done == 0:
+                sums[g, m] = psum.tile([P, H], F32, name=f"bank{2 * (g % 4) + m}")
+            passes_done[g, m] = done + 1
+            nc.tensor.matmul_mx(
+                out=sums[g, m][:],
+                lhsT=slot_words[s, g].bitcast(FP8X4),
+                lhsT_scale=slot_scales[s, g],
+                rhs=w_words[m, g // 2, s].bitcast(FP4X4),
+                rhs_scale=w_scales[m, g // 2, s],
+                start=done == 0,
+                stop=done == PASSES - 1,
+            )
+            if m == W1 and done == PASSES - 1:
+                nc.scalar.activation(in_halves(sb(f"ra{g}", [P, H], F32)), by_halves(sums[g, W1]), RELU)
+
+        def add_passes(groups, matrices, passes):
+            for g in groups:
+                for m in matrices:
                     for s in passes:
-                        mm(g, m, s)
+                        add_pass(g, m, s)
 
-        def mul(g):
-            nc.vector.tensor_tensor(in_halves(sb(f"h{g}", [P, H], BF16)), by_halves(acc[g, 1][0]), in_halves(tiles[f"ra{g}"]), MULT)
+        def free_w3_bank(g):
+            nc.scalar.copy(in_halves(sb(f"rb{g}", [P, H], F32)), by_halves(sums[g, W3]))
 
-        def stage(g):
-            nc.scalar.copy(in_halves(sb(f"rb{g}", [P, H], F32)), by_halves(acc[g, 1][0]))
-
-        def mul_staged(g, engine):
+        def product_in_sbuf(g, engine):
             engine.tensor_tensor(sb(f"h{g}", [P, H], BF16)[:], tiles[f"rb{g}"][:], tiles[f"ra{g}"][:], MULT)
 
+        def product(g):
+            nc.vector.tensor_tensor(in_halves(sb(f"h{g}", [P, H], BF16)), by_halves(sums[g, W3]), in_halves(tiles[f"ra{g}"]), MULT)
+
         def width(lead):
-            return 128 * TURNS[lead][1]
+            return GROUP * TURNS[lead][1]
 
         def turn(lead):
             turned[lead] = psum.tile([P, H], F32, name=f"bank{TURNS[lead][0]}")
@@ -207,14 +207,14 @@ def tile_moe_cap2_glu_relu_kernel(
                 for u in range(2):
                     nc.tensor.transpose(turned[lead][:, 256 * i + 128 * u : 256 * i + 128 * (u + 1)], words[:, 128 * u : 128 * (u + 1)], ident[:])
 
-        def mul_and_turn(g):
+        def product_and_turn(g):
             turned[g] = psum.tile([P, H], F32, name=f"bank{TURNS[g][0]}")
             h = sb(f"h{g}", [P, H], BF16)
             for u in range(2):
-                nc.vector.tensor_tensor(in_halves(h)[:, u], by_halves(acc[g, 1][0])[:, u], in_halves(tiles[f"ra{g}"])[:, u], MULT)
+                nc.vector.tensor_tensor(in_halves(h)[:, u], by_halves(sums[g, W3])[:, u], in_halves(tiles[f"ra{g}"])[:, u], MULT)
                 nc.tensor.transpose(turned[g][:, 128 * u : 128 * (u + 1)], h[:].bitcast(F32)[:, 128 * u : 128 * (u + 1)], ident[:])
 
-        def weave(lead, copy=nc.scalar.copy):
+        def weave(lead, copy):
             count = TURNS[lead][1]
             copy(
                 sb(f"hb{lead}", [P, 512 * count], BF16)[:].bitcast(F32).rearrange("p (g r u) -> p g r u", g=count, u=2),
@@ -222,11 +222,10 @@ def tile_moe_cap2_glu_relu_kernel(
             )
 
         def quantise_h(lead):
-            nc.vector.quantize_mx(
-                out=sb(f"hw{lead}", [P, width(lead)], U32)[:].bitcast(FP8X4), scales=sb(f"hs{lead}", [P, width(lead)], U8)[:], in_=tiles[f"hb{lead}"][:]
-            )
+            codes = sb(f"hw{lead}", [P, width(lead)], U32)
+            nc.vector.quantize_mx(out=codes[:].bitcast(FP8X4), scales=sb(f"hs{lead}", [P, width(lead)], U8)[:], in_=tiles[f"hb{lead}"][:])
 
-        def second(lead):
+        def times_w2(lead):
             nc.tensor.matmul_mx(
                 out=turned[lead][:, 0 : width(lead)],
                 lhsT=tiles["w2"][:, lead // 2, :].bitcast(FP4X4),
@@ -237,21 +236,14 @@ def tile_moe_cap2_glu_relu_kernel(
                 stop=True,
             )
 
-        def keep_y(lead, copy=nc.scalar.copy):
-            copy(y[:, 128 * lead : 128 * lead + width(lead)], turned[lead][:, 0 : width(lead)])
-
-        def load_rest():
-            nc.sync.dma_start(out=sb("w2", [P, E, 2 * N], U8)[:].bitcast(I32), in_=w2_words[:, 0].rearrange("e p n -> p e n").bitcast(I32))
-            scale_rows(tiles["w2s"], w2_scales)
-            nc.sync.dma_start(pos1_t[:], pos1)
-            nc.sync.dma_start(pos2_t[:], pos2)
-            nc.sync.dma_start(out=sb("gates", [P, 2, T], F32)[:], in_=gate.rearrange("r p t -> p r t"))
+        def keep_y(lead, copy):
+            copy(y[:, GROUP * lead : GROUP * lead + width(lead)], turned[lead][:, 0 : width(lead)])
 
         def combine():
             gates = tiles["gates"]
             first = sb("first", [P, T], F32)
-            other = sb("other", [P, T], F32)
-            nc.vector.tensor_tensor(other[:], y[:].indirect(pos2_t[:]), gates[:, 1, :], MULT)
+            second = sb("second", [P, T], F32)
+            nc.vector.tensor_tensor(second[:], y[:].indirect(pos2_t[:]), gates[:, 1, :], MULT)
             pieces = list(zip(CUTS, CUTS[1:]))
             for c0, c1 in pieces:
                 nc.scalar.activation(sb(f"raw{c0}", [P, c1 - c0], F32)[:], y[:].indirect(pos1_t[:, c0 // 16 : c1 // 16]), COPY)
@@ -261,7 +253,7 @@ def tile_moe_cap2_glu_relu_kernel(
 
             def add_and_store(c0, c1):
                 res = sb(f"res{c0}", [P, c1 - c0], F32)
-                nc.vector.tensor_tensor(res[:], first[:, c0:c1], other[:, c0:c1], ADD)
+                nc.vector.tensor_tensor(res[:], first[:, c0:c1], second[:, c0:c1], ADD)
                 nc.sync.dma_start(out=out[:, c0:c1], in_=res[:])
 
             weigh(*pieces[0])
@@ -270,48 +262,121 @@ def tile_moe_cap2_glu_relu_kernel(
                 add_and_store(*piece)
             add_and_store(*pieces[-1])
 
-        def clock(name, ap):
-            nc.gpsimd.tensor_copy(sb(f"clock_{name}", [P, 1], F32)[:], ap)
+        early, late = range(0, 4), range(4, 8)
+        on_scalar, on_vector = nc.scalar.copy, nc.vector.tensor_copy
 
-        zero("s0_0", [P, 6, H]); zero("s1_0", [P, 6, H])
-        zero("xs01", [P, T]); zero("xs2", [P, T]); zero("lifted0", [P, 512]); zero("lifted4", [P, 512]); zero("w2s", [P, E, N])
-        zero("s0_2", [P, 6, H]); zero("s1_2", [P, 6, H])
+        for m in (W1, W3):
+            zero_plane(f"s{m}_0", [P, 2 * PASSES, H])
+        zero_plane("xs01", [P, T])
+        zero_plane("xs2", [P, T])
+        zero_plane("lifted0", [P, 4 * GROUP])
+        zero_plane("lifted4", [P, 4 * GROUP])
+        zero_plane("w2s", [P, E, N])
+        for m in (W1, W3):
+            zero_plane(f"s{m}_2", [P, 2 * PASSES, H])
         nc.gpsimd.memset(y[:, SLOTS:], 0.0)
         make_identity(nc, ident[:])
 
-        load_x_rows(0, 0); load_x_rows(0, 1); nc.sync.dma_start(offs_t[:], offs); load_x_rows(1, 0); load_x_rows(1, 1)
-        load_scales(0, 0, 2); load_pass(0, 0, 0, 1); load_pass(0, 0, 1, 2); load_x_rows(2, 0)
+        load_x(0, 0)
+        load_x(0, 1)
+        nc.sync.dma_start(offs_t[:], offs)
+        load_x(1, 0)
+        load_x(1, 1)
+        load_scales(W1, 0)
+        load_pass(W1, 0, 0, 1)
+        load_pass(W1, 0, 1, 2)
+        load_x(2, 0)
+
         for half in range(2):
-            round_rows(0, half, WIDE, T, "scalar"); round_rows(0, half, 0, WIDE, "vector")
-        quantise(0, WIDE); quantise(0, 0)
-        gather_scales(0, 0, 4); lift_rows(0, 0, 4); gather_words(0, 0, 4)
-        load_x_rows(2, 1); load_pass(0, 1, 0, 2)
-        load_scales(1, 0, 2); load_pass(1, 0, 0, 1); load_pass(1, 0, 1, 2); load_pass(1, 1, 0, 2); load_pass(0, 2, 0, 2); load_pass(1, 2, 0, 2)
-        round_rows(1, 0, WIDE, T, "pool"); round_rows(1, 0, 0, WIDE, "scalar")
-        round_rows(1, 1, WIDE, T, "pool"); round_rows(1, 1, 448, WIDE, "pool"); round_rows(1, 1, 0, 448, "scalar")
-        quantise(1, WIDE); quantise(1, 0)
-        for g in (0, 2):
-            gather_scales(1, g, g + 2); gather_words(1, g, g + 2)
+            round_x(0, half, WIDE, T, nc.scalar)
+            round_x(0, half, 0, WIDE, nc.vector)
+        quantise_x(0, WIDE)
+        quantise_x(0, 0)
+        gather_scales(0, 0, 4)
+        lift_pass0_scales("gs0_0", 0)
+        gather_words(0, 0, 4)
+
+        load_x(2, 1)
+        load_pass(W1, 1, 0, 2)
+        load_scales(W3, 0)
+        load_pass(W3, 0, 0, 1)
+        load_pass(W3, 0, 1, 2)
+        load_pass(W3, 1, 0, 2)
+        load_pass(W1, 2, 0, 2)
+        load_pass(W3, 2, 0, 2)
+
+        round_and_quantise(1)
+        gather_words(0, 4, 5)
+        gather_pass(1, 0, 2)
+        gather_pass(1, 2, 4)
         gather_scales(1, 4, 8)
-        round_rows(2, 0, WIDE, T, "pool"); round_rows(2, 0, 0, WIDE, "scalar")
-        round_rows(2, 1, WIDE, T, "pool"); round_rows(2, 1, 448, WIDE, "pool"); round_rows(2, 1, 0, 448, "scalar")
-        quantise(2, WIDE); quantise(2, 0)
-        for g in range(4):
-            gather_scales(2, g, g + 1); gather_words(2, g, g + 1)
-        load_scales(0, 2, 4); load_pass(0, 1, 2, 4); lift_rows(1, 4, 8); load_pass(0, 0, 2, 4)
-        load_scales(1, 2, 4); load_pass(1, 1, 2, 4); load_words(0, 2, 2, 3); load_words(1, 2, 0, 1); load_words(1, 2, 2, 3); load_words(0, 3, 2, 3); load_words(1, 3, 0, 1); load_words(1, 3, 2, 3)
-        load_rest()
-        sums(range(4), (0,), (0,)); sums(range(4), (0,), (1,)); sums(range(4), (1,), (0,)); sums(range(4), (1,), (1,))
-        gather_words(1, 4, 6); gather_words(1, 6, 8); gather_words(0, 4, 6); gather_words(0, 6, 8)
-        sums(range(4), (0, 1), (2,))
-        stage(0); mul_staged(0, nc.gpsimd); stage(1); mul_staged(1, nc.gpsimd); stage(2); stage(3)
-        gather_scales(2, 4, 6); gather_words(2, 4, 6); gather_scales(2, 6, 8); gather_words(2, 6, 8)
-        mul_staged(2, nc.vector); mul_staged(3, nc.vector)
+        round_and_quantise(2)
+        gather_words(0, 5, 6)
+        for g in early:
+            gather_pass(2, g, g + 1)
 
+        load_scales(W1, 2)
+        load_pass(W1, 0, 2, 4)
+        lift_pass0_scales("gs1_4", 4)
+        load_pass(W1, 1, 2, 4)
+        load_scales(W3, 2)
+        load_pass(W3, 0, 2, 4)
+        load_pass(W1, 2, 2, 4)
+        load_expert(W3, 2, 1, 3)
+        load_expert(W3, 3, 1, 3)
+        nc.sync.dma_start(out=sb("w2", [P, E, 2 * N], U8)[:].bitcast(I32), in_=w2_words[:, 0].rearrange("e p n -> p e n").bitcast(I32))
+        load_scale_rows(tiles["w2s"], w2_scales)
+        nc.sync.dma_start(pos1_t[:], pos1)
+        nc.sync.dma_start(pos2_t[:], pos2)
+        nc.sync.dma_start(out=sb("gates", [P, 2, T], F32)[:], in_=gate.rearrange("r p t -> p r t"))
 
-        sums(range(4, 8), (0,), (1,)); sums(range(4, 8), (0,), (0,)); sums(range(4, 8), (1,), (1,)); sums((4, 5), (0,), (2,))
-        sums((4,), (1,), (0, 2)); sums((6, 7), (0,), (2,)); mul(4); sums((5,), (1,), (0, 2)); mul(5); sums((6,), (1,), (0, 2)); mul(6)
-        turn(0); weave(0); turn(2); weave(2); sums((7,), (1,), (0, 2)); turn(4); turn(6); mul_and_turn(7); weave(7); quantise_h(7)
-        weave(4); weave(6, nc.vector.tensor_copy); quantise_h(0); quantise_h(2); quantise_h(4); quantise_h(6); second(7); keep_y(7); second(0); second(2); second(4); second(6)
-        keep_y(0); keep_y(2); keep_y(4); keep_y(6, nc.vector.tensor_copy)
+        for m in (W1, W3):
+            for s in (0, 1):
+                add_passes(early, (m,), (s,))
+        gather_words(1, 4, 6)
+        gather_words(1, 6, 8)
+        gather_words(0, 6, 8)
+        add_passes(early, (W1, W3), (2,))
+        for g in (0, 1):
+            free_w3_bank(g)
+            product_in_sbuf(g, nc.gpsimd)
+        for g in (2, 3):
+            free_w3_bank(g)
+        gather_pass(2, 4, 6)
+        gather_pass(2, 6, 8)
+        for g in (2, 3):
+            product_in_sbuf(g, nc.vector)
+
+        add_passes((4, 5), (W1,), (0,))
+        add_passes(late, (W1,), (1,))
+        add_passes((6, 7), (W1,), (0,))
+        add_passes(late, (W3,), (0,))
+        add_passes((4, 5), (W1,), (2,))
+        add_passes((4,), (W3,), (1, 2))
+        add_passes((6, 7), (W1,), (2,))
+        product(4)
+        for g in (5, 6):
+            add_passes((g,), (W3,), (1, 2))
+            product(g)
+
+        for lead in (0, 2):
+            turn(lead)
+            weave(lead, on_scalar)
+        add_passes((7,), (W3,), (1, 2))
+        turn(4)
+        turn(6)
+        product_and_turn(7)
+        weave(7, on_scalar)
+        quantise_h(7)
+        weave(4, on_scalar)
+        weave(6, on_vector)
+        for lead in (0, 2, 4, 6):
+            quantise_h(lead)
+        times_w2(7)
+        keep_y(7, on_scalar)
+        for lead in (0, 2, 4, 6):
+            times_w2(lead)
+        for lead in (0, 2, 4):
+            keep_y(lead, on_scalar)
+        keep_y(6, on_vector)
         combine()

@@ -34,10 +34,10 @@ CUTS = (0, 256, 512, 640, 768)
 REUSE = {
     "xb1_512": "xb0_0",
     "gw0_4": "xf1_1",
-    "gw0_5": "xf2_1",
-    "gw1_4": "gw1_0",
+    "gw1_4": "xf2_1",
+    "gw1_5": "gw1_0",
     "gw1_6": "gw1_2",
-    "gw0_6": "wp1_1_0",
+    "gw0_5": "wp1_1_0",
     "gs2_4": "gs2_0",
     "gw2_4": "gw2_0",
     "gs2_6": "gs2_2",
@@ -311,14 +311,14 @@ def tile_moe_cap2_glu_relu_kernel(
         gather_pass(1, 2, 4)
         gather_scales(1, 4, 8)
         round_and_quantise(2)
-        gather_words(0, 5, 6)
+        gather_words(1, 4, 5)
         for g in early:
             gather_pass(2, g, g + 1)
 
         load_scales(W1, 2)
-        load_pass(W1, 0, 2, 4)
-        lift_pass0_scales("gs1_4", 4)
         load_pass(W1, 1, 2, 4)
+        lift_pass0_scales("gs1_4", 4)
+        load_pass(W1, 0, 2, 4)
         load_scales(W3, 2)
         load_pass(W3, 0, 2, 4)
         load_pass(W1, 2, 2, 4)
@@ -333,9 +333,9 @@ def tile_moe_cap2_glu_relu_kernel(
         for m in (W1, W3):
             for s in (0, 1):
                 add_passes(early, (m,), (s,))
-        gather_words(1, 4, 6)
+        gather_words(1, 5, 6)
         gather_words(1, 6, 8)
-        gather_words(0, 6, 8)
+        gather_words(0, 5, 8)
         add_passes(early, (W1, W3), (2,))
         for g in (0, 1):
             free_w3_bank(g)
@@ -347,9 +347,8 @@ def tile_moe_cap2_glu_relu_kernel(
         for g in (2, 3):
             product_in_sbuf(g, nc.vector)
 
-        add_passes((4, 5), (W1,), (0,))
         add_passes(late, (W1,), (1,))
-        add_passes((6, 7), (W1,), (0,))
+        add_passes(late, (W1,), (0,))
         add_passes(late, (W3,), (0,))
         add_passes((4, 5), (W1,), (2,))
         add_passes((4,), (W3,), (1, 2))

@@ -320,10 +320,11 @@ def tile_moe_cap2_glu_relu_kernel(
         lift_pass0_scales("gs1_4", 4)
         load_pass(W1, 0, 2, 4)
         load_scales(W3, 2)
-        load_pass(W3, 0, 2, 4)
-        load_pass(W1, 2, 2, 4)
-        load_expert(W3, 2, 1, 3)
-        load_expert(W3, 3, 1, 3)
+        load_pass(W3, 1, 2, 4)
+        for e in (2, 3):
+            load_expert(W1, e, 2, 3)
+            load_expert(W3, e, 0, 1)
+            load_expert(W3, e, 2, 3)
         nc.sync.dma_start(out=sb("w2", [P, E, 2 * N], U8)[:].bitcast(I32), in_=w2_words[:, 0].rearrange("e p n -> p e n").bitcast(I32))
         load_scale_rows(tiles["w2s"], w2_scales)
         nc.sync.dma_start(pos1_t[:], pos1)
@@ -349,19 +350,19 @@ def tile_moe_cap2_glu_relu_kernel(
 
         add_passes(late, (W1,), (1,))
         add_passes(late, (W1,), (0,))
-        add_passes(late, (W3,), (0,))
+        add_passes(late, (W3,), (1,))
         add_passes((4, 5), (W1,), (2,))
-        add_passes((4,), (W3,), (1, 2))
+        add_passes((4,), (W3,), (0, 2))
         add_passes((6, 7), (W1,), (2,))
         product(4)
         for g in (5, 6):
-            add_passes((g,), (W3,), (1, 2))
+            add_passes((g,), (W3,), (0, 2))
             product(g)
 
         for lead in (0, 2):
             turn(lead)
             weave(lead, on_scalar)
-        add_passes((7,), (W3,), (1, 2))
+        add_passes((7,), (W3,), (0, 2))
         turn(4)
         turn(6)
         product_and_turn(7)

@@ -37,7 +37,7 @@ REUSE = {
     "gw1_4": "xf2_1",
     "gw1_5": "gw1_0",
     "gw1_6": "gw1_2",
-    "gw0_5": "wp1_1_0",
+    "gw0_6": "wp1_1_0",
     "gs2_4": "gs2_0",
     "gw2_4": "gw2_0",
     "gs2_6": "gs2_2",
@@ -295,6 +295,7 @@ def tile_moe_cap2_glu_relu_kernel(
         gather_scales(0, 0, 4)
         lift_pass0_scales("gs0_0", 0)
         gather_words(0, 0, 4)
+        gather_words(0, 5, 6)
 
         load_x(2, 1)
         load_pass(W1, 1, 0, 2)
@@ -336,7 +337,7 @@ def tile_moe_cap2_glu_relu_kernel(
                 add_passes(early, (m,), (s,))
         gather_words(1, 5, 6)
         gather_words(1, 6, 8)
-        gather_words(0, 5, 8)
+        gather_words(0, 6, 8)
         add_passes(early, (W1, W3), (2,))
         for g in (0, 1):
             free_w3_bank(g)

from contextlib import ExitStack

import concourse.mybir as mybir
from concourse.masks import make_identity

K, T, E, C, H, N = 1536, 768, 4, 256, 512, 128
PAD = 32
FLOPS = 3355443200

F32 = mybir.dt.float32
BF16 = mybir.dt.bfloat16
U32 = mybir.dt.uint32
I32 = mybir.dt.int32
U16 = mybir.dt.uint16
U8 = mybir.dt.uint8
FP8X4 = mybir.dt.float8_e4m3fn_x4
FP4X4 = mybir.dt.float4_e2m1fn_x4
COPY = mybir.ActivationFunctionType.Copy
RELU = mybir.ActivationFunctionType.Relu
MULT = mybir.AluOpType.mult
ADD = mybir.AluOpType.add

P = 128
PASSES = K // 512
SLOTS = E * C
GROUP = 128
W1, W3 = 0, 1
WIDE = 512
POOL_TOKENS = 320
PLANES = (("xs01", 4), ("xs01", 0), ("xs2", 0))
LIFT = 4
TURNS = {0: (0, 2), 2: (2, 2), 4: (4, 2), 6: (6, 1), 7: (1, 1)}
CUTS = (0, 256, 512, 640, 768)
REUSE = {
    "xb1_512": "xb0_0",
    "gw0_4": "xf1_1",
    "gw1_4": "xf2_1",
    "gw1_5": "gw1_0",
    "gw1_6": "gw1_2",
    "gw0_6": "wp1_1_0",
    "gs2_4": "gs2_0",
    "gw2_4": "gw2_0",
    "gs2_6": "gs2_2",
    "gw2_6": "gw2_2",
    "rb0": "s1_0",
    "rb1": "wp1_2_0",
    "rb2": "wp0_2_0",
}


def tile_moe_cap2_glu_relu_kernel(
    tc, xT, w1_words, w1_scales, w3_words, w3_scales, w2_words, w2_scales, gate, offs, pos1, pos2, out
):
    nc = tc.nc
    with ExitStack() as ctx:
        keep = ctx.enter_context(tc.tile_pool(name="keep", bufs=1))
        psum = ctx.enter_context(tc.psum_pool(name="psum", bufs=1))
        tiles = {}

        def sb(name, shape, dtype):
            if name not in tiles:
                tiles[name] = keep.tile(shape, dtype, name=REUSE.get(name, name), align_bytes=256)
            return tiles[name]

        offs_t = keep.tile([P, SLOTS // 16], U16, name="offs_t")
        pos1_t = keep.tile([P, T // 16], U16, name="pos1_t")
        pos2_t = keep.tile([P, T // 16], U16, name="pos2_t")
        y = keep.tile([P, SLOTS + PAD], F32, name="y")
        ident = keep.tile([P, P], F32, name="ident")
        words_dram = (w1_words, w3_words)
        scales_dram = (w1_scales, w3_scales)
        w_words, w_scales, slot_words, slot_scales = {}, {}, {}, {}
        sums, passes_done, turned = {}, {}, {}

        def zero_plane(name, shape):
            nc.vector.memset(sb(name, shape, U8)[:].bitcast(I32), 0)

        def load_x(s, half):
            rows = xT[512 * s : 512 * (s + 1), :].rearrange("(p j) t -> p j t", j=4)
            nc.sync.dma_start(out=sb(f"xf{s}_{half}", [P, 2, T], F32)[:], in_=rows[:, 2 * half : 2 * half + 2, :])

        def load_pass(m, s, e0, e1):
            tile = sb(f"wp{m}_{s}_{e0}", [P, e1 - e0, 2 * H], U8)
            nc.sync.dma_start(out=tile[:].bitcast(I32), in_=words_dram[m][e0:e1, s].rearrange("e p n -> p e n").bitcast(I32))
            for e in range(e0, e1):
                w_words[m, e, s] = tile[:, e - e0, :]

        def load_expert(m, e, s0, s1):
            tile = sb(f"we{m}_{e}_{s0}", [P, s1 - s0, 2 * H], U8)
            nc.sync.dma_start(out=tile[:].bitcast(I32), in_=words_dram[m][e, s0:s1].rearrange("s p n -> p s n").bitcast(I32))
            for s in range(s0, s1):
                w_words[m, e, s] = tile[:, s - s0, :]

        def load_scale_rows(tile, dram):
            rows = dram.rearrange("e s (q r) n -> r q (e s) n", r=4)
            for r in range(4):
                nc.sync.dma_start(out=tile[r:128:32, :, :].bitcast(I32), in_=rows[r].bitcast(I32))

        def load_scales(m, e0):
            tile = tiles[f"s{m}_{e0}"]
            load_scale_rows(tile, scales_dram[m][e0 : e0 + 2])
            for e in (e0, e0 + 1):
                for s in range(PASSES):
                    w_scales[m, e, s] = tile[:, PASSES * (e - e0) + s, :]

        def rounded(s, c0):
            return sb(f"xb{s}_{c0}", [P, 4 * (WIDE if c0 == 0 else T - WIDE)], BF16)

        def round_x(s, half, c0, c1, engine):
            base = 0 if c0 < WIDE else WIDE
            dst = rounded(s, base)[:, 4 * (c0 - base) : 4 * (c1 - base)]
            src = tiles[f"xf{s}_{half}"][:, :, c0:c1]
            if engine is nc.gpsimd:
                nc.gpsimd.tensor_copy(dst.rearrange("p (t j) -> p t j", j=4)[:, :, 2 * half : 2 * half + 2], src.rearrange("p j t -> p t j"))
                return
            dst = dst.rearrange("p (c i j) -> p c j i", i=4, j=4)[:, :, 2 * half : 2 * half + 2, :]
            src = src.rearrange("p j (c i) -> p c j i", i=4)
            if engine is nc.vector:
                nc.vector.tensor_copy(dst, src)
            else:
                nc.scalar.activation(dst, src, COPY)

        def quantise_x(s, c0):
            c1 = WIDE if c0 == 0 else T
            name, row = PLANES[s]
            codes = sb(f"xw{s}", [P, T], U32)
            nc.vector.quantize_mx(out=codes[:, c0:c1].bitcast(FP8X4), scales=tiles[name][row:128, c0:c1], in_=rounded(s, c0)[:])

        def round_and_quantise(s):
            round_x(s, 0, WIDE, T, nc.gpsimd)
            round_x(s, 0, 0, WIDE, nc.scalar)
            round_x(s, 1, 0, POOL_TOKENS, nc.gpsimd)
            round_x(s, 1, POOL_TOKENS, WIDE, nc.scalar)
            round_x(s, 1, WIDE, T, nc.scalar)
            quantise_x(s, 0)
            quantise_x(s, WIDE)

        def by_group(where, s, g0, g1, tile):
            for g in range(g0, g1):
                where[s, g] = tile[:, GROUP * (g - g0) : GROUP * (g - g0 + 1)]

        def gather_words(s, g0, g1):
            tile = sb(f"gw{s}_{g0}", [P, GROUP * (g1 - g0)], U32)
            nc.vector.tensor_copy(tile[:], tiles[f"xw{s}"][:].indirect(offs_t[:, 8 * g0 : 8 * g1]))
            by_group(slot_words, s, g0, g1, tile)

        def gather_scales(s, g0, g1):
            tile = sb(f"gs{s}_{g0}", [P, GROUP * (g1 - g0)], U8)
            nc.vector.tensor_copy(tile[:], tiles[PLANES[s][0]][:].indirect(offs_t[:, 8 * g0 : 8 * g1]))
            by_group(slot_scales, s, g0, g1, tile)

        def gather_pass(s, g0, g1):
            gather_scales(s, g0, g1)
            gather_words(s, g0, g1)

        def lift_pass0_scales(gathered, g0):
            plane = tiles[f"lifted{g0}"]
            for r in range(4):
                nc.sync.dma_start(out=plane[r:128:32, :].bitcast(I32), in_=tiles[gathered][LIFT + r : 128 : 32, :].bitcast(I32))
            by_group(slot_scales, 0, g0, g0 + 4, plane)

        def in_halves(tile):
            return tile[:].rearrange("m (u p d) -> m u p d", u=2, d=2)

        def by_halves(bank):
            return bank[:].rearrange("m (p u d) -> m u p d", u=2, d=2)

        def add_pass(g, m, s):
            done = passes_done.get((g, m), 0)
            if done == 0:
                sums[g, m] = psum.tile([P, H], F32, name=f"bank{2 * (g % 4) + m}")
            passes_done[g, m] = done + 1
            nc.tensor.matmul_mx(
                out=sums[g, m][:],
                lhsT=slot_words[s, g].bitcast(FP8X4),
                lhsT_scale=slot_scales[s, g],
                rhs=w_words[m, g // 2, s].bitcast(FP4X4),
                rhs_scale=w_scales[m, g // 2, s],
                start=done == 0,
                stop=done == PASSES - 1,
            )
            if m == W1 and done == PASSES - 1:
                nc.scalar.activation(in_halves(sb(f"ra{g}", [P, H], F32)), by_halves(sums[g, W1]), RELU)

        def add_passes(groups, matrices, passes):
            for g in groups:
                for m in matrices:
                    for s in passes:
                        add_pass(g, m, s)

        def free_w3_bank(g):
            nc.scalar.copy(in_halves(sb(f"rb{g}", [P, H], F32)), by_halves(sums[g, W3]))

        def product_in_sbuf(g, engine):
            engine.tensor_tensor(sb(f"h{g}", [P, H], BF16)[:], tiles[f"rb{g}"][:], tiles[f"ra{g}"][:], MULT)

        def product(g):
            nc.vector.tensor_tensor(in_halves(sb(f"h{g}", [P, H], BF16)), by_halves(sums[g, W3]), in_halves(tiles[f"ra{g}"]), MULT)

        def width(lead):
            return GROUP * TURNS[lead][1]

        def turn(lead):
            turned[lead] = psum.tile([P, H], F32, name=f"bank{TURNS[lead][0]}")
            for i in range(TURNS[lead][1]):
                words = tiles[f"h{lead + i}"][:].bitcast(F32)
                for u in range(2):
                    nc.tensor.transpose(turned[lead][:, 256 * i + 128 * u : 256 * i + 128 * (u + 1)], words[:, 128 * u : 128 * (u + 1)], ident[:])

        def product_and_turn(g):
            turned[g] = psum.tile([P, H], F32, name=f"bank{TURNS[g][0]}")
            h = sb(f"h{g}", [P, H], BF16)
            for u in range(2):
                nc.vector.tensor_tensor(in_halves(h)[:, u], by_halves(sums[g, W3])[:, u], in_halves(tiles[f"ra{g}"])[:, u], MULT)
                nc.tensor.transpose(turned[g][:, 128 * u : 128 * (u + 1)], h[:].bitcast(F32)[:, 128 * u : 128 * (u + 1)], ident[:])

        def weave(lead, copy):
            count = TURNS[lead][1]
            copy(
                sb(f"hb{lead}", [P, 512 * count], BF16)[:].bitcast(F32).rearrange("p (g r u) -> p g r u", g=count, u=2),
                turned[lead][:, 0 : 256 * count].rearrange("p (g u r) -> p g r u", g=count, u=2),
            )

        def quantise_h(lead):
            codes = sb(f"hw{lead}", [P, width(lead)], U32)
            nc.vector.quantize_mx(out=codes[:].bitcast(FP8X4), scales=sb(f"hs{lead}", [P, width(lead)], U8)[:], in_=tiles[f"hb{lead}"][:])

        def times_w2(lead):
            nc.tensor.matmul_mx(
                out=turned[lead][:, 0 : width(lead)],
                lhsT=tiles["w2"][:, lead // 2, :].bitcast(FP4X4),
                lhsT_scale=tiles["w2s"][:, lead // 2, :],
                rhs=tiles[f"hw{lead}"][:].bitcast(FP8X4),
                rhs_scale=tiles[f"hs{lead}"][:],
                start=True,
                stop=True,
            )

        def keep_y(lead, copy):
            copy(y[:, GROUP * lead : GROUP * lead + width(lead)], turned[lead][:, 0 : width(lead)])

        def combine():
            gates = tiles["gates"]
            first = sb("first", [P, T], F32)
            second = sb("second", [P, T], F32)
            nc.vector.tensor_tensor(second[:], y[:].indirect(pos2_t[:]), gates[:, 1, :], MULT)
            pieces = list(zip(CUTS, CUTS[1:]))
            for c0, c1 in pieces:
                nc.scalar.activation(sb(f"raw{c0}", [P, c1 - c0], F32)[:], y[:].indirect(pos1_t[:, c0 // 16 : c1 // 16]), COPY)

            def weigh(c0, c1):
                nc.vector.tensor_tensor(first[:, c0:c1], tiles[f"raw{c0}"][:], gates[:, 0, c0:c1], MULT)

            def add_and_store(c0, c1):
                res = sb(f"res{c0}", [P, c1 - c0], F32)
                nc.vector.tensor_tensor(res[:], first[:, c0:c1], second[:, c0:c1], ADD)
                nc.sync.dma_start(out=out[:, c0:c1], in_=res[:])

            weigh(*pieces[0])
            for piece, ahead in zip(pieces, pieces[1:]):
                weigh(*ahead)
                add_and_store(*piece)
            add_and_store(*pieces[-1])

        early, late = range(0, 4), range(4, 8)
        on_scalar, on_vector = nc.scalar.copy, nc.vector.tensor_copy

        for m in (W1, W3):
            zero_plane(f"s{m}_0", [P, 2 * PASSES, H])
        zero_plane("xs01", [P, T])
        zero_plane("xs2", [P, T])
        zero_plane("lifted0", [P, 4 * GROUP])
        zero_plane("lifted4", [P, 4 * GROUP])
        zero_plane("w2s", [P, E, N])
        for m in (W1, W3):
            zero_plane(f"s{m}_2", [P, 2 * PASSES, H])
        nc.gpsimd.memset(y[:, SLOTS:], 0.0)
        make_identity(nc, ident[:])

        load_x(0, 0)
        load_x(0, 1)
        nc.sync.dma_start(offs_t[:], offs)
        load_x(1, 0)
        load_x(1, 1)
        load_scales(W1, 0)
        load_pass(W1, 0, 0, 1)
        load_pass(W1, 0, 1, 2)
        load_x(2, 0)

        for half in range(2):
            round_x(0, half, WIDE, T, nc.scalar)
            round_x(0, half, 0, WIDE, nc.vector)
        quantise_x(0, WIDE)
        quantise_x(0, 0)
        gather_scales(0, 0, 4)
        lift_pass0_scales("gs0_0", 0)
        gather_words(0, 0, 4)
        gather_words(0, 5, 6)

        load_x(2, 1)
        load_pass(W1, 1, 0, 2)
        load_scales(W3, 0)
        load_pass(W3, 0, 0, 1)
        load_pass(W3, 0, 1, 2)
        load_pass(W3, 1, 0, 2)
        load_pass(W1, 2, 0, 2)
        load_pass(W3, 2, 0, 2)

        round_and_quantise(1)
        gather_words(0, 4, 5)
        gather_pass(1, 0, 2)
        gather_pass(1, 2, 4)
        gather_scales(1, 4, 8)
        round_and_quantise(2)
        gather_words(1, 4, 5)
        for g in early:
            gather_pass(2, g, g + 1)

        load_scales(W1, 2)
        load_pass(W1, 1, 2, 4)
        lift_pass0_scales("gs1_4", 4)
        load_pass(W1, 0, 2, 4)
        load_scales(W3, 2)
        load_pass(W3, 1, 2, 4)
        for e in (2, 3):
            load_expert(W1, e, 2, 3)
            load_expert(W3, e, 0, 1)
            load_expert(W3, e, 2, 3)
        nc.sync.dma_start(out=sb("w2", [P, E, 2 * N], U8)[:].bitcast(I32), in_=w2_words[:, 0].rearrange("e p n -> p e n").bitcast(I32))
        load_scale_rows(tiles["w2s"], w2_scales)
        nc.sync.dma_start(pos1_t[:], pos1)
        nc.sync.dma_start(pos2_t[:], pos2)
        nc.sync.dma_start(out=sb("gates", [P, 2, T], F32)[:], in_=gate.rearrange("r p t -> p r t"))

        for m in (W1, W3):
            for s in (0, 1):
                add_passes(early, (m,), (s,))
        gather_words(1, 5, 6)
        gather_words(1, 6, 8)
        gather_words(0, 6, 8)
        add_passes(early, (W1, W3), (2,))
        for g in (0, 1):
            free_w3_bank(g)
            product_in_sbuf(g, nc.gpsimd)
        for g in (2, 3):
            free_w3_bank(g)
        gather_pass(2, 4, 6)
        gather_pass(2, 6, 8)
        for g in (2, 3):
            product_in_sbuf(g, nc.vector)

        add_passes(late, (W1,), (1,))
        add_passes(late, (W1,), (0,))
        add_passes(late, (W3,), (1,))
        add_passes((4, 5), (W1,), (2,))
        add_passes((4,), (W3,), (0, 2))
        add_passes((6, 7), (W1,), (2,))
        product(4)
        for g in (5, 6):
            add_passes((g,), (W3,), (0, 2))
            product(g)

        for lead in (0, 2):
            turn(lead)
            weave(lead, on_scalar)
        add_passes((7,), (W3,), (0, 2))
        turn(4)
        turn(6)
        product_and_turn(7)
        weave(7, on_scalar)
        quantise_h(7)
        weave(4, on_scalar)
        weave(6, on_vector)
        for lead in (0, 2, 4, 6):
            quantise_h(lead)
        times_w2(7)
        keep_y(7, on_scalar)
        for lead in (0, 2, 4, 6):
            times_w2(lead)
        for lead in (0, 2, 4):
            keep_y(lead, on_scalar)
        keep_y(6, on_vector)
        combine()
